import numpy as np, ml_dtypes
CORES = [2,6,10,14,18,22,26,30]
N = 8
BF = ml_dtypes.bfloat16
def gentries(a):
    return np.ascontiguousarray(a.reshape(8, 16, -1).transpose(0, 2, 1)).reshape(8, -1)
def gtable(e):
    e = np.asarray(e); return np.ascontiguousarray(e.reshape(8, -1, 16).transpose(0, 2, 1)).reshape(128, -1).astype(np.int32)
V, H, Q, ST = 4096, 1024, 3, 2
MOST, SAME = 2 ** (Q + 1) - 1, 3
def sizes(w):
    return 1 + np.minimum((w * (V - 1 - H)) // np.add.reduce(w, axis=-1, keepdims=True), MOST - 1)
def usual(rng):
    return sizes((1000 * rng.standard_exponential((N, 8, H))).astype(np.int64) + 1)
def forest(rng, n, stale, last):
    pool = rng.permutation(V - 1) + 1; r = np.zeros((Q + 1, H), np.int64)
    if last: pool = np.concatenate([pool[pool == V - 1], pool[pool != V - 1]])
    c = rng.integers(0, V, (Q, V)) if stale else np.zeros((Q, V), np.int64)
    high = pool[:0]; at = 0
    for o in range(Q, -1, -1):
        hs = np.nonzero((n >> o) & 1)[0]
        a = pool[at:at + hs.size]; at += hs.size; r[o, hs] = a
        k = pool[at:at + high.size]; at += high.size
        if o < Q: c[o, high] = k
        high = np.concatenate([high, a, k])
    return r, c
def forests(rng, n, stale=False, last=False):
    p = [[forest(rng, n[q, g], stale, last) for g in range(8)] for q in range(N)]
    return np.array([[x[0] for x in a] for a in p]), np.array([[x[1] for x in a] for a in p])
def records(rng):
    v = rng.integers(0, 256, (N, 8, 16, V))
    lev = np.clip(rng.integers(0, 256, (N, 8, 1, V)) + rng.integers(-40, 41, (N, 8, 16, V)), 0, 255)
    return np.where(rng.random((N, 8, 1, V)) < 0.5, v, lev)
def pack(v, r, c):
    return {"rec": np.ascontiguousarray(v.reshape(N, 128, V)).astype(np.float32).astype(BF), "rt": np.stack([gtable(a.reshape(8, -1)) for a in r]),
            "ch": np.ascontiguousarray(c.reshape(N, 8, Q * V)).astype(np.int32)}
def setup_inputs(rng):
    r, c = forests(rng, usual(rng)); return pack(records(rng), r, c)
def setup_inputs_alike(rng):
    n = usual(rng); n[:, 0] = 1; n[:, 2] = SAME
    for q in range(N):
        n[q, 4] = rng.permutation(2 ** (np.arange(H) % (Q + 1)))
        room = MOST - n[q, 6]; before = np.add.accumulate(room) - room
        n[q, 6] = n[q, 6] + np.clip(V - 1 - np.add.reduce(n[q, 6]) - before, 0, room)
        for g in (5, 7):
            more = 2 ** (1 + (q + g // 2) % Q) - 1; many = min(H, (V - 1 - H) // more)
            n[q, g] = rng.permutation(1 + more * (np.arange(H) < many).astype(np.int64))
    r, c = forests(rng, n, last=True); v = records(rng)
    for q in range(N):
        for g in (1, 3): v[q, g] = v[q, g][:, rng.integers(0, 8, V)]
    return pack(v, r, c)
def setup_inputs_ties(rng):
    r, c = forests(rng, usual(rng))
    base = np.array([1, 128, 254, 128, 1, 254, 128, 128])[rng.permutation(8)].reshape(1, 8, 1, 1)
    k = rng.choice(np.array([0, 7, 8, 9, 16]), (N, 8, 1, V)); low = rng.integers(0, 2, (N, 8, 1, V))
    up = np.argsort(rng.random((N, 8, 16, V), dtype=np.float32), axis=2) < k
    return pack(base + np.where(up, 1, -low), r, c)
def setup_inputs_tall(rng):
    n = np.ones((N, 8, H), np.int64)
    run = [np.full((V - 1 - H) // (MOST - 1), MOST), 2 ** Q + 1 - (np.arange(2 * ((V - 1 - H) // MOST)) & 1)]
    st = np.stack([rng.integers(1, H - run[g & 1].size + 1, N) for g in range(8)], axis=1)
    for q in range(N):
        for g in range(8): n[q, g, st[q, g]:st[q, g] + run[g & 1].size] = run[g & 1]
    r, c = forests(rng, n); v = rng.integers(100, 256, (N, 8, 16, V))
    for q in range(N):
        for g in range(8):
            k = np.arange(run[g & 1].size); h = st[q, g] + k
            o = np.where((k + (0 if g & 1 else int(rng.integers(0, 2)))) & 1 == 1, Q, 0)
            v[q, g][:, r[q, g, o, h]] = rng.integers(0, 100, (16, k.size))
            v[q, g][:, r[q, g, 0, 0]] = (np.arange(16) == rng.integers(0, 16)).astype(np.int64)
    return pack(v, r, c)
def setup_inputs_stale(rng):
    n = usual(rng); n[:, :, 0] = 1
    r, c = forests(rng, n, True); v = records(rng); v[..., 0] = 0
    for q in range(N):
        for g in range(8):
            t = (0, 1, H - 1, H, 4080, H // 2)[(q + g) % 6]
            v[q, g][:, r[q, g, 0, 0]] = rng.permutation(np.clip(t - 255 * np.arange(16), 0, 255))
    return pack(v, r, c)
def setup_inputs_spread(rng):
    r, c = forests(rng, sizes(np.exp2(12 * rng.random((N, 8, H))).astype(np.int64)))
    v = (np.exp2(8 * rng.random((N, 8, 1, V))) * rng.random((N, 8, 16, V))).astype(np.int64); u = rng.random((N, 8, 1, V))
    return pack(np.where(u < 0.0625, 0, np.where(u > 0.9375, 255, np.minimum(v, 255))), r, c)
def check_inputs(d):
    bad = []
    x = np.asarray(d["rec"]).astype(np.float32)
    if not np.all((x >= 0) & (x <= 255) & (x == np.floor(x))): bad.append("whole numbers from 0 to 255 in rec")
    for k in ("rt", "ch"):
        if np.min(d[k]) < 0 or np.max(d[k]) > V - 1: bad.append("range of " + k)
    if "range of rt" in bad or "range of ch" in bad: return bad
    empty, lack, twice = False, False, False
    for q in range(N):
        rr = gentries(d["rt"][q]).reshape(8, Q + 1, H); cc = np.asarray(d["ch"][q]).reshape(8, Q, V)
        for g in range(8):
            if not np.all(np.max(rr[g], axis=0) > 0): empty = True
            high = np.zeros(0, np.int64)
            for o in range(Q, -1, -1):
                a = rr[g, o][rr[g, o] > 0].astype(np.int64); k = cc[g, o][high].astype(np.int64) if o < Q else high
                if np.any(k == 0): lack = True
                high = np.concatenate([high, a, k])
            if np.unique(high).size != high.size: twice = True
    if empty: bad.append("every heap has a root")
    if lack: bad.append("every child that counts is a node")
    if twice: bad.append("no node stands twice")
    return bad
def pick(v, ix):
    return np.take_along_axis(v, ix[:, :, None, :], 3)
def beats(x, y):
    return np.add.reduce((x < y).astype(np.int64), axis=2) >= 9
def reference(rec, rt, ch):
    v = rec.astype(np.float32).astype(np.int64).reshape(N, 8, 16, V); kid = ch.astype(np.int64).reshape(N, 8, Q, V)
    root = np.stack([gentries(a) for a in rt]).astype(np.int64).reshape(N, 8, Q + 1, H)
    for step in range(ST):
        m = root[:, :, 0].copy(); order = np.zeros_like(m)
        for o in range(1, Q + 1):
            a = root[:, :, o]; w = (a > 0) & ((m == 0) | beats(pick(v, a), pick(v, m)))
            m = np.where(w, a, m); order = np.where(w, o, order)
        for o in range(Q + 1): root[:, :, o] = np.where(order == o, 0, root[:, :, o])
        z = pick(v, m); got = np.roll(z, 1, axis=0)
        s = np.add.reduce(got[:, :, :, 0], axis=2) & (H - 1)
        np.put_along_axis(v, m[:, :, None, :], (z + got) >> 1, 3)
        j = (np.arange(H) + s[:, :, None]) & (H - 1)
        mj = np.take_along_axis(m, j, 2); oj = np.take_along_axis(order, j, 2)
        c = m
        for o in range(Q):
            a = root[:, :, o].copy(); b = np.where(o < oj, np.take_along_axis(kid[:, :, o], mj, 2), 0)
            n = (a > 0).astype(np.int64) + (b > 0) + (c > 0); link = n >= 2
            x = np.where((n == 2) & (a > 0), a, b); y = np.where(c > 0, c, b)
            win = beats(pick(v, y), pick(v, x)); wn = np.where(win, y, x); ls = np.where(win, x, y)
            rl = pick(v, ls); new = rl + np.clip(pick(v, wn) - rl, -1, 1)
            i = np.nonzero(link)
            v[i[0], i[1], :, ls[i]] = new.transpose(0, 1, 3, 2)[i]
            kid[i[0], i[1], o, wn[i]] = ls[i]
            root[:, :, o] = np.where(n == 1, a + b + c, np.where(n == 3, a, 0))
            c = np.where(link, wn, 0)
        root[:, :, Q] = np.where(root[:, :, Q] > 0, root[:, :, Q], c)
    return {"yrec": v.reshape(N, 128, V).astype(np.float32).astype(BF), "yrt": np.stack([gtable(a.reshape(8, -1)) for a in root]).astype(np.float32)}

@@ -1,0 +1,423 @@
+from concourse.mybir import AluOpType as A, ActivationFunctionType as F
+
+V, H = 4096, 1024
+ZONE, DUMMY, WIN = V, V + H, V + 2 * H
+MAGIC = 12582912.0
+OPT = {"smode": ((0, 2), (0, 2)), "cmode": ((), ()), "put": 512, "late": False, "early": False, "ch": (2, 1), "copy": 0}
+ORDER = ("AFAuApA9AGAOANAJAaEMAAAPARAKAXATAHAbAsAoAIAqAZAYAkAVAgAfAtAeBJABArAUAlAWASAnA1AiAQA/A+BCAjBHBAACBIBKAEADAyBLBPBBAvBDBMBEBNBOBFBXAwBGAzBfBZBQBYBeBRBaBbBcBdBSBnBTBpA0BUAcBoBqBrBVAmBsBWA8BtBxA2BgA6ByAxBiA4A7A5BhBjBkA3BlALBmRuB0B5R1B3B2B6B7B8B9AdCAB4CFCGCBCDBzB+AMSCAhB/BvCVBwCHCICKCJCECWCXCSCTCLCMCNCUCOCPCYCZCaCcCQCRCbCuCtCdCqCgCeChCfCiCsCjClCxCyCvCkCoCwCzC0CmC1CpC2C3C4CnDMDpC5C6DJC7DKC8DLENC/DADNDBDOEOCrDPDQDCDoC9DREQDDDTDSC+DaDUDnDHDXDkDEDWDFDGDVDsEPDtDIDqDrDuDvDbDlDwDcDmDxDyDdELD5EREDD6ETD2DYDZESD7DzEUD8EEEVD0EWEcEXD1EZEYEaEJDeDfEbDiEdD3EiEhD4DgDhEHEeEIEfEGEgEKD9D+EkEjEmDjD/EAElEnEoEpExEqEyErEuEBEzE6E0ECE2E1EsEtE7E8E9FCE+E4E5FOFPFDE/E3FREvFBFZFQFEFSFFFGFTFMFIFKVNVJFaEFFUEwFLFcFVFWFAFXFbFdFHFYFfFgFjFhFiFkFzFeF1FnFlFoF0FmFxFpF4F5FyF2F3F6F7F8F9F+F/GAFqFsFvFrGGGIGBGCGRFtGSFwGQGDFuGTGUGqGEGVGFGHGpGJGWGXGYGZGKGbGeWaGLGMGNGOGcGrGtGsGuGiGoGvGPGwGfGxGgGzGhGjG0G3GdGmG4G1GkG5GlG2GnG6G7G8G/G9G+HAGyHBHCHDHFHHHKHEHGHIHJ")
+ABC = "ABCDEFGHIJKLMNOPQRSTUVWXYZabcdefghijklmnopqrstuvwxyz0123456789+/"
+
+SCRATCH = {
+    "G0": ("sbuf", [128, WIN], "bfloat16"), "G1": ("sbuf", [128, WIN], "bfloat16"), "G2": ("sbuf", [128, WIN], "bfloat16"),
+    "O": ("sbuf", [128, WIN], "bfloat16"),
+    "CW": ("sbuf", [128, V], "bfloat16"), "RT": ("sbuf", [128, 256], "int32"), "CHN": ("sbuf", [128, 768], "int32"),
+    "HL": ("sbuf", [128, 1536], "bfloat16"), "B": ("sbuf", [128, 52 * H], "bfloat16"),
+    "ZS": ("sbuf", [128, 4 * 144], "bfloat16"), "BO": ("sbuf", [128, 128], "bfloat16"), "ID": ("sbuf", [128, 512], "bfloat16"),
+    "U": ("sbuf", [128, 3072], "uint16"), "I": ("sbuf", [128, 32], "int32"), "S": ("sbuf", [128, 14336], "float32"),
+    "D0": ("psum", [128, 512], "float32"), "D1": ("psum", [128, 512], "float32"),
+    "D2": ("psum", [128, 512], "float32"), "D3": ("psum", [128, 512], "float32"),
+    "CA": ("psum", [128, 512], "float32"), "CB": ("psum", [128, 512], "float32"),
+    "CC": ("psum", [128, 512], "float32"), "VP": ("psum", [128, 512], "float32"),
+}
+PSUM = ("D0", "D1", "D2", "D3", "CA", "CB", "CC", "VP")
+SEMAPHORES = ["cV", "cS", "cP", "cG"] + ["d%d" % i for i in range(24)] + ["arr%d" % i for i in range(8)] + ["snt%d" % i for i in range(8)]
+
+
+def engines(topo, a, b):
+    e = topo.engines(a, b)
+    return e[::max(1, len(e) // 8)]
+
+
+def build(g, core, T, topo):
+    rank, n = T.rank_of(core), len(T.cores)
+    nxt, prv = T.cores[(rank + 1) % n], T.cores[(rank - 1) % n]
+    Q = {"V": g.vector, "S": g.scalar, "P": g.tensor, "G": g, "Y": g.sync}
+    ops, recs, top = [], {}, {"S": 0, "U": 0, "B": 0, "VP": 0, "D": 0, "d": 0}
+
+    def ap(x):
+        if x[0] == "ind":
+            return ap(x[1]).indirect(ap(x[2]))
+        if len(x) == 4:
+            return T[x[0]][:, x[1]:x[2]:x[3]]
+        return T[x[0]][:, x[1]:x[2]]
+
+    def add(kind, qs, outs, ins, fn, sem=None, cnt=1, after=()):
+        rd, wr = [], []
+        for x in ins:
+            if isinstance(x, tuple):
+                rd += [x[1], x[2]] if x[0] == "ind" else [x]
+        for o in outs:
+            if o[0] == "ind":
+                wr.append(o[1]); rd.append(o[2])
+            else:
+                wr.append(o)
+        deps, me = set(after), len(ops)
+        for x, w in [(x, 0) for x in rd] + [(x, 1) for x in wr]:
+            for lo, hi, w2, who in recs.get(x[0], []):
+                if (x[0] in PSUM and (ops[who]["qs"] != qs or len(qs) > 1)) or ((w or w2) and lo < x[2] and x[1] < hi):
+                    deps.add(who)
+        for x, w in [(x, 0) for x in rd] + [(x, 1) for x in wr]:
+            recs.setdefault(x[0], []).append((x[1], x[2], w, me))
+        ops.append({"kind": kind, "qs": qs, "deps": deps, "fn": fn, "sem": sem, "cnt": cnt})
+        return me
+
+    def new(buf, w):
+        lo = top[buf]
+        if buf == "VP" and lo + w > 512:
+            lo = 0
+        top[buf] = lo + (w + 15) // 16 * 16
+        return (buf, lo, lo + w)
+
+    def sub(x, lo, w):
+        return (x[0], x[1] + lo, x[1] + lo + w)
+
+    def wid(x):
+        return x[2] - x[1]
+
+    def val(x):
+        return ap(x) if isinstance(x, tuple) else x
+
+    def out(o, like):
+        return new(o, wid(like)) if isinstance(o, str) else o
+
+    def tt(o, a, b, op):
+        o = out(o, b)
+        add("c", "V", [o], [a, b], lambda q: g.vector.tensor_tensor(ap(o), ap(a), ap(b), op))
+        return o
+
+    def ts(o, a, s1, op0, s2=None, op1=None):
+        o = out(o, a)
+        if op1 is None:
+            add("c", "V", [o], [a, s1], lambda q: g.vector.tensor_scalar(ap(o), ap(a), val(s1), None, op0))
+        else:
+            add("c", "V", [o], [a, s1, s2], lambda q: g.vector.tensor_scalar(ap(o), ap(a), val(s1), val(s2), op0, op1))
+        return o
+
+    def cp(o, a):
+        o = out(o, a)
+        add("c", "V", [o], [a], lambda q: g.vector.tensor_copy(ap(o), ap(a)))
+        return o
+
+    def fill(o, c):
+        return add("c", "V", [o], [], lambda q: g.vector.memset(ap(o), c))
+
+    def act(o, a, f, bias, scale=1.0):
+        add("c", "S", [o], [a], lambda q: g.scalar.activation(ap(o), ap(a), f, bias=bias, scale=scale))
+
+    def move(o, a):
+        add("c", "SV", [o], [a], lambda q: g.vector.tensor_copy(ap(o), ap(a)) if q == "V" else g.scalar.activation(ap(o), ap(a), F.Copy))
+        return o
+
+    def sign(o, a):
+        add("c", "SV", [o], [a], lambda q: g.vector.tensor_scalar(ap(o), ap(a), -1.0, 1.0, A.max, A.min) if q == "V"
+            else g.scalar.activation(ap(o), ap(a), F.Sign))
+
+    def mm(o, whole, terms):
+        def fn(q):
+            for i, (l, r) in enumerate(terms):
+                last = g.tensor.matmul(ap(o), ap(l), ap(r), i == 0, i == len(terms) - 1)
+            return last
+        add("c", "P", [o], whole, fn)
+
+    def iota(o, pat, base, cm):
+        add("c", "G", [o], [], lambda q: g.iota(ap(o), pat, base, cm, allow_small_or_imprecise_dtypes=True))
+        return o
+
+    def dma(q, o, i, rd, wr, after=()):
+        top["d"] += 1
+        return add("d", q, wr, rd, lambda q: Q[q].dma_start(o, i), "d%d" % (top["d"] - 1), 16, after)
+
+    def ind(win, end, off):
+        return ("ind", (win, 0, end), off)
+
+    def lists(o, src, sel):
+        z = sel * 144
+        mm(o, [("ZS", z, z + 144), src], [(("ZS", z + 15 - i, z + 143 - i), (src[0], src[1] + i, src[2], 16)) for i in range(16)])
+
+    def half(x, h):
+        w = wid(x) // 2
+        return sub(x, w * h, w)
+
+    def col(x, o, k=1):
+        return sub(x, 64 * o, 64 * k)
+
+    I1, IN, I2, IM = ("ID", 0, 128), ("ID", 128, 256), ("ID", 256, 384), ("ID", 384, 512)
+
+    def mix(terms):
+        d = ("D%d" % (top["D"] % 4), 0, 512)
+        top["D"] += 1
+        mm(d, [x for p in terms for x in p], terms)
+        return d
+
+    def gather(win, end, off):
+        o = new("B", H)
+        for h in range(2):
+            move(half(o, h), ind(win, end, half(off, h)))
+        return o
+
+    dma("S", T.RT[:], T.rt[:], [], [("RT", 0, 256)])
+    d1 = dma("Y", T.G0[:, 0:V], T.rec[:], [], [("G0", 0, V)])
+    for o in range(3):
+        d1 = dma("Y", T.CHN[:, o * 256:(o + 1) * 256], T.ch[:, o * V:(o + 1) * V], [], [("CHN", o * 256, (o + 1) * 256)])
+    d0 = fill(("CW", 0, V), 0.0)
+    add("c", "G", [("I", 0, 1)], [], lambda q: g.iota(ap(("I", 0, 1)), [[0, 1]], 0, 1))
+    tz = iota(new("S", 144), [[1, 144]], -15, 0)
+    ig = iota(new("S", 128), [[16, 8], [0, 16]], 0, 0)
+    dc0 = iota(new("S", 256), [[16, 2], [-1, 128]], 0, 1)
+    dz0 = iota(new("S", 192), [[0, 3], [16, 64]], DUMMY, 1)
+    ob0 = iota(new("S", 16), [[128, 4], [16, 4]], 0, 1)
+    iota(sub(ob0, 0, 15), [[128, 3], [16, 5]], 0, 1)
+    ts(("I", 1, 2), ("I", 0, 1), 112, A.bitwise_and)
+    ts(("I", 2, 3), ("I", 0, 1), 1, A.arith_shift_right, 7, A.bitwise_and)
+    c2 = cp("S", ("I", 1, 3))
+    g16, ph = sub(c2, 0, 1), sub(c2, 1, 1)
+    ts(("ZS", 0, 144), tz, g16, A.is_equal)
+    r = cp("S", ("RT", 0, 256)); ur = cp("U", ("RT", 0, 256))
+    roots, uroots = [col(r, o) for o in range(4)], [col(ur, o) for o in range(4)]
+    rid = r
+    for o in range(3):
+        ts(("ZS", 144 * (o + 1), 144 * (o + 2)), tz, g16, A.is_equal, ts("S", ph, float(o), A.is_equal), A.mult)
+    ts(("BO", 0, 128), ig, g16, A.is_equal)
+    for x, c in ((I1, 1.0), (IN, -1.0), (I2, 2.0), (IM, -2.0)):
+        ts(x, sub(dc0, 0, 128), 0.0, A.is_equal, c, A.mult)
+    far = ts("S", ig, g16, A.not_equal, 999.0, A.mult)
+    dz = ts("S", dz0, g16, A.subtract)
+    z = ts("S", col(dz0, 0), g16, A.subtract, float(-H), A.add)
+    ob = ts("S", ob0, g16, A.subtract)
+    dc = new("S", 256)
+    for k in range(2):
+        tt(half(dc, k), half(dc0, k), far, A.add)
+    bw = new("S", 400)
+    fill(bw, 0.0)
+    fill(("G0", DUMMY, WIN), 256.0)
+    for w in ("G1", "G2") if OPT["late"] else ("G1",):
+        iota((w, DUMMY, WIN), [[0, H]], 256, 0)
+    gxs, nls = [new("S", 320), new("S", 320)], [new("S", 256), new("S", 256)]
+    yss = [new("S", 256), new("S", 256)]
+    for t in range(2):
+        cp(col(yss[t], 0), z)
+        fill(col(gxs[t], 0), 1.0); fill(col(gxs[t], 4), 0.0); fill(col(nls[t], 0), 0.0)
+    for k in range(2):
+        d = ("D%d" % k, 0, 384)
+        cp(d, ("CHN", 384 * k, 384 * k + 384))
+        move(("HL", 384 * k, 384 * k + 384), d)
+        tt(("HL", 768 + 384 * k, 768 + 384 * k + 384), d, ("HL", 384 * k, 384 * k + 384), A.subtract)
+    fill(("G0", 0, 1), 256.0)
+    rows = []
+    for o in range(3):
+        for k in range(2):
+            c = k * 768 + o * 256
+            rows.append(dma("Y", T.CW[2 * o + k:128:16, :], T.HL[:, c:c + 256], [("HL", c, c + 256)], [], [d0]))
+    recs["CW"] += [(0, V, 1, x) for x in rows]
+    dma("Y", T.O[:, 0:V], T.rec[:], [], [("O", 0, V)], [d1])
+
+    def renew(w):
+        c = OPT["copy"]
+        if c < V:
+            dma("Y", T[w][:, c:V], T.O[:, c:V], [("O", c, V)], [(w, c, V)])
+        for k in range(0, c, 1024):
+            move((w, k, k + 1024), ("O", k, k + 1024))
+
+    dlt = wnm = lid = None
+    for t in range(2):
+        end = V if t == 0 else DUMMY
+        gx, nl = gxs[t], nls[t]
+        zx, wx = new("B", 16 + H), new("B", 16 + H)
+        zt, wt = sub(zx, 16, H), sub(wx, 16, H)
+        fill(sub(zx, 0, 16), 0.0)
+
+        def shift(src):
+            mm(("CA", 64, 66), [("BO", 0, 128), src], [(("BO", 0, 128), src)])
+            i0 = 8 + 8 * t
+            cp(("I", i0, i0 + 1), ("CA", 64, 65))
+            ts(("I", i0 + 2, i0 + 3), ("I", i0, i0 + 1), 4, A.arith_shift_right, 63, A.bitwise_and)
+            ts(("I", i0 + 3, i0 + 4), ("I", i0, i0 + 1), 15, A.bitwise_and)
+            return cp("S", ("I", i0 + 2, i0 + 4))
+        wl, m, um, nh = new("S", 128), roots[0], uroots[0], OPT["ch"][t]
+        for o in (1, 2, 3):
+            ro = gather("G0", end, uroots[o])
+            m2, um2, cm = new("S", 64), new("U", 64), new("B", H)
+            for h in range(2):
+                sm = (o, h) in OPT["cmode"][t]
+                if sm:
+                    mo = move(new("B", 512), ind("G0", end, half(um, h)))
+                    act(half(cm, h), mix([(I1, mo), (IN, half(ro, h))]), F.Sign, -0.5)
+                else:
+                    tt(half(cm, h), ind("G0", end, half(um, h)), half(ro, h), A.is_gt)
+                if nh == 1 and h == 0:
+                    continue
+                part = (lambda x: half(x, h)) if nh == 2 else (lambda x: x)
+                cnt = ("CB" if h and nh == 2 else "CA", 0, 64 // nh)
+                lists(cnt, part(cm), 0)
+                d = tt("S" if nh == 2 else "VP", part(roots[o]), part(m), A.subtract)
+                w = ts(part(col(gx, 3) if o == 3 else col(wl, o - 1)), cnt, 2.0 if sm else 9.0, A.is_ge)
+                tt(part(m2), part(m), tt("S" if nh == 2 else "VP", w, d, A.mult), A.add)
+                cp(part(um2), part(m2))
+            m, um = m2, um2
+        mid, umid, cg = (m, um, new("B", H)) if t == 0 else (new("S", 64), new("U", 64), new("B", H))
+        for h in range(2):
+            move(half(zt, h), ind("G0", end, half(um, h)))
+            if h == 0 and OPT["early"]:
+                cp(sub(zx, 0, 2), shift(sub(cp(new("B", 16), ind("G0", end, sub(um, 0, 1))), 0, 2)))
+            pa, pb = (sub(wx, 0, 528), sub(zx, 0, 528)) if h == 0 and OPT["early"] else (half(wt, h), half(zt, h))
+            e, k = engines(topo, core, nxt), 2 * t + h
+            r_id, pid = topo.addr(nxt)[:2]
+
+            def send(q, a=pa, b=pb, k=k, e=e, r_id=r_id, pid=pid):
+                g.remote_dma(ap(a), ap(b), T.sem["arr%d" % k], T.sem["snt%d" % k], pid, r_id, sum(1 << x for x in e))
+            s = add("r", "G", [], [pb], send, "snt%d" % k, len(e))
+            add("a", "", [pa], [], None, "arr%d" % k, len(engines(topo, prv, core)), [s])
+        if t == 1:
+            cp(umid, tt(mid, m, tt("VP", dlt, tt("VP", m, z, A.is_equal), A.mult), A.add))
+        for h in range(2):
+            move(half(cg, h), ind("CW", V, half(umid, h)))
+        for o in range(3):
+            lists(("CC", 64 * o, 64 * o + 64), cg, 1 + o)
+        tt(col(gx, 2), col(wl, 1), col(gx, 3), A.max)
+        tt(col(gx, 1), col(wl, 0), col(gx, 2), A.max)
+        a = tt("S", rid, tt("VP", col(gx, 0, 4), col(gx, 1, 4), A.is_equal), A.mult)
+        nd = tt("S", dz, ts("VP", col(a, 0, 3), 0.0, A.is_equal), A.mult)
+        a1 = tt("S", col(a, 0, 3), nd, A.add)
+        kid = ("CC", 0, 192)
+        if t == 1:
+            eq = new("VP", 192)
+            for o in range(3):
+                tt(col(eq, o), col(wnm, o), m, A.is_equal)
+            kid = tt("VP", tt("S", tt("S", lid, kid, A.subtract), eq, A.mult), kid, A.add)
+        dlt = tt("S", mid, z, A.subtract)
+        for o in range(3):
+            move(sub(bw, 128 * o + 64, 64), tt(sub(bw, 128 * o, 64), col(gx, o + 1), col(kid, o), A.mult))
+        Gw = ["G0"] * 3 if t == 0 else ["G1", "G1", "G2" if OPT["late"] else "G1"]
+        zn = (Gw[0], ZONE, DUMMY)
+        sc = sub(wx, 0, 2) if OPT["early"] else shift(sub(wt, 0, 2))
+        uob = ts("U", ob, sub(sc, 0, 1), A.add)
+        pp = ts("S", dc, sub(sc, 1, 1), A.is_equal)
+        g1 = cp(new("S", 240), ("ind", bw, sub(uob, 0, 15)))
+        bs = [("CB", 0, 64), ("CC", 64, 192)]
+        for o in range(3):
+            mm(("CC" if o else "CB", 64 * o, 64 * o + 64), [pp, g1], [(half(pp, 0), sub(g1, 80 * o, 64)), (half(pp, 1), sub(g1, 80 * o + 1, 64))])
+        for h in range(2):
+            d = mix([(I1, half(zt, h)), (I1, half(wt, h))])
+            act(d, d, F.Identity, MAGIC, 0.4995)
+            act(half(zn, h), d, F.Identity, -MAGIC)
+        if Gw[2] != Gw[0]:
+            dma("Y", T.G2[:, ZONE:DUMMY], T.G1[:, ZONE:DUMMY], [zn], [("G2", ZONE, DUMMY)])
+        x1, th, ux = new("S", 192), col(nl, 1, 3), new("U", 192)
+        for o, k, b in ((0, 1, bs[0]), (1, 2, bs[1])):
+            nb = ts("VP", b, 0.0, A.is_equal)
+            tt(col(x1, o, k), tt("S", col(a1, o, k), nb, A.mult), b, A.add)
+            if o == 0:
+                cp(col(ux, 0), col(x1, 0))
+            tt(col(th, o, k), col(nd, o, k), nb, A.mult)
+        tt(col(th, 1), col(th, 1), col(th, 0), A.max)
+        tt(col(th, 2), col(th, 2), col(th, 1), A.max)
+        cp(col(ux, 1, 2), tt(col(x1, 1, 2), col(x1, 1, 2), col(th, 1, 2), A.max))
+        xt = [col(x1, o) for o in range(3)]
+        st = new("S", 256)
+        ts(col(st, 3), tt("VP", col(th, 2), col(a, 3), A.add), 0.0, A.is_equal)
+        tt(col(st, 0, 3), th, col(nl, 0, 3), A.is_gt)
+        tt(col(a, 0, 3), col(a, 0, 3), tt("VP", x1, col(a, 0, 3), A.not_equal), A.mult)
+        pw = OPT["put"]
+        for c in range(0, H, pw):
+            cp(ind("O", V, sub(umid, c // 16, pw // 16)), sub(zn, c, pw))
+        ys, yd, lid, rl4 = yss[t], zn, new("S", 192), new("S", 256)
+        y, roots, uroots = col(ys, 0), [], []
+
+        def root(o, k):
+            ro = tt(col(rl4, o, k), col(a, o, k), tt("VP", col(st, o, k), col(ys, o, k), A.mult), A.add)
+            uo = cp("U", ro)
+            roots.extend([col(ro, j) for j in range(k)]); uroots.extend([col(uo, j) for j in range(k)])
+        for o in range(3):
+            win, cm = Gw[o], new("B", H)
+            if t == 0 and o:
+                root(2, 1) if o == 2 else root(0, 2)
+            dl = tt("VP", y, xt[o], A.subtract)
+            sm = o in OPT["smode"][t]
+            if sm:
+                xd = gather(win, WIN, col(ux, o))
+            for h in range(2):
+                if sm:
+                    act(half(cm, h), mix([(I1, half(xd, h)), (IN, half(yd, h))]), F.Sign, -0.5)
+                else:
+                    tt(half(cm, h), ind(win, WIN, half(col(ux, o), h)), half(yd, h), A.is_gt)
+            lists(("CA", 0, 64), cm, 0)
+            p = tt("VP", ts("S", ("CA", 0, 64), 2.0 if sm else 9.0, A.is_ge), dl, A.mult)
+            y2 = tt(col(ys, o + 1), xt[o], p, A.add)
+            ls = tt("S", y, p, A.subtract)
+            if t == 0 and o == 2:
+                root(3, 1)
+            yo, last = yd, sm and o == 2
+            if not last:
+                yd = gather(win, WIN, cp("U", y2))
+            rl = new("B", H) if sm and not last else gather(win, WIN, cp("U", ls))
+            ut = cp("U", tt(col(lid, o), ls, tt("VP", dlt, tt("VP", ls, z, A.is_equal), A.mult), A.add))
+            sg = new("B", H)
+            for h in range(2):
+                if last:
+                    sign(half(sg, h), mix([(I1, half(xd, h)), (I1, half(yo, h)), (IM, half(rl, h))]))
+                elif sm:
+                    x, y0, y1 = half(xd, h), half(yo, h), half(yd, h)
+                    sign(half(sg, h), mix([(I2, y1), (IN, x), (IN, y0)]))
+                    move(half(rl, h), mix([(I1, x), (I1, y0), (IN, y1)]))
+                else:
+                    sign(half(sg, h), mix([(I1, half(yd, h)), (IN, half(rl, h))]))
+            if t == 0 and o == 2 and OPT["late"]:
+                renew("G1")
+            for c in range(0, H, pw):
+                tt(ind("O", WIN, sub(ut, c // 16, pw // 16)), sub(rl, c, pw), sub(sg, c, pw), A.add)
+            y = y2
+        dm = tt("S", dlt, tt("VP", y, z, A.is_equal), A.mult)
+        if t == 0:
+            renew("G2" if OPT["late"] else "G1")
+            pr = new("VP", 256)
+            for o in range(4):
+                tt(col(pr, o), col(st, o), dm, A.mult)
+            rid = tt("S", rl4, pr, A.add)
+            wnm = tt("S", col(ys, 1, 3), th, A.add)
+        else:
+            yid, pr = tt("S", dm, y, A.add), new("VP", 256)
+            for o in range(4):
+                tt(col(pr, o), col(st, o), yid, A.mult)
+            res = tt("S", a, pr, A.add)
+            dma("Y", T.yrt[:], ap(res), [res], [])
+            dma("Y", T.yrec[:], T.O[:, 0:V], [("O", 0, V)], [])
+    return ops, Q
+
+
+def rank_program(g, core, T, topo):
+    if T.rank_of(core) is None:
+        return
+    ops, Q = build(g, core, T, topo)
+    count, seen, tok, final = {"V": 0, "S": 0, "P": 0, "G": 0}, {k: {} for k in Q}, {}, {}
+    order = [64 * ABC.index(ORDER[k]) + ABC.index(ORDER[k + 1]) for k in range(0, len(ORDER), 2)] or list(range(len(ops)))
+    place, known = {c % 1024: k for k, c in enumerate(order)}, {}
+
+    def wait(q, s, v):
+        if seen[q].get(s, 0) < v:
+            seen[q][s] = v
+            Q[q].wait_ge(T.sem[s], v)
+
+    for code in order:
+        i = code % 1024
+        op = ops[i]
+        known[i] = {}
+        if op["kind"] != "a":
+            q = "V" if code >= 1024 else op["qs"][0]
+            for d in sorted(op["deps"], key=lambda d: -place[d]):
+                wait(q, tok[d][0], tok[d][1])
+                for s in known[d]:
+                    seen[q][s] = max(seen[q].get(s, 0), known[d][s])
+            known[i] = dict(seen[q])
+            ins = op["fn"](q)
+        if op["kind"] == "c":
+            count[q] += 1
+            tok[i] = ("c" + q, count[q])
+            ins.then_inc(T.sem["c" + q], 1)
+        else:
+            tok[i] = (op["sem"], op["cnt"])
+            if op["kind"] == "d":
+                ins.then_inc(T.sem[op["sem"]], 16)
+        final[tok[i][0]] = tok[i][1]
+    seen["G"] = {}
+    for s in sorted(final):
+        wait("G", s, final[s])

@@ -1,26 +1,33 @@
 from concourse.mybir import AluOpType as A, ActivationFunctionType as F
 
 V, H = 4096, 1024
-ZONE, DUMMY, WIN = V, V + H, V + 2 * H
+WIN = V + H
+FAR = 1024.0
 MAGIC = 12582912.0
-OPT = {"smode": ((0, 2), (0, 2)), "cmode": ((), ()), "put": 512, "late": False, "early": False, "ch": (2, 1), "copy": 0}
-ORDER = ("AFAuApA9AGAOANAJAaEMAAAPARAKAXATAHAbAsAoAIAqAZAYAkAVAgAfAtAeBJABArAUAlAWASAnA1AiAQA/A+BCAjBHBAACBIBKAEADAyBLBPBBAvBDBMBEBNBOBFBXAwBGAzBfBZBQBYBeBRBaBbBcBdBSBnBTBpA0BUAcBoBqBrBVAmBsBWA8BtBxA2BgA6ByAxBiA4A7A5BhBjBkA3BlALBmRuB0B5R1B3B2B6B7B8B9AdCAB4CFCGCBCDBzB+AMSCAhB/BvCVBwCHCICKCJCECWCXCSCTCLCMCNCUCOCPCYCZCaCcCQCRCbCuCtCdCqCgCeChCfCiCsCjClCxCyCvCkCoCwCzC0CmC1CpC2C3C4CnDMDpC5C6DJC7DKC8DLENC/DADNDBDOEOCrDPDQDCDoC9DREQDDDTDSC+DaDUDnDHDXDkDEDWDFDGDVDsEPDtDIDqDrDuDvDbDlDwDcDmDxDyDdELD5EREDD6ETD2DYDZESD7DzEUD8EEEVD0EWEcEXD1EZEYEaEJDeDfEbDiEdD3EiEhD4DgDhEHEeEIEfEGEgEKD9D+EkEjEmDjD/EAElEnEoEpExEqEyErEuEBEzE6E0ECE2E1EsEtE7E8E9FCE+E4E5FOFPFDE/E3FREvFBFZFQFEFSFFFGFTFMFIFKVNVJFaEFFUEwFLFcFVFWFAFXFbFdFHFYFfFgFjFhFiFkFzFeF1FnFlFoF0FmFxFpF4F5FyF2F3F6F7F8F9F+F/GAFqFsFvFrGGGIGBGCGRFtGSFwGQGDFuGTGUGqGEGVGFGHGpGJGWGXGYGZGKGbGeWaGLGMGNGOGcGrGtGsGuGiGoGvGPGwGfGxGgGzGhGjG0G3GdGmG4G1GkG5GlG2GnG6G7G8G/G9G+HAGyHBHCHDHFHHHKHEHGHIHJ")
-ABC = "ABCDEFGHIJKLMNOPQRSTUVWXYZabcdefghijklmnopqrstuvwxyz0123456789+/"
+BIG = 8192.0
+OPT = {"nh": (2, 1), "form": ("AAA", "BAB"), "meld": ("SSS", "SSS"), "send": ((512, 512), (512, 512)), "put": 512, "putz": 512, "early": 1,
+       "lin": ((0, 0), (0, 0)), "after": 1, "zcmp": 1, "held": 3, "parts": (512, 512),
+       "lat": 0.12, "turns": 1, "tries": 25000, "heat": 0.25, "seed": 1,
+       "onv": ("root.0", "first.2", "first.10", "z.0"), "late": {}}
+
+RATES = ({"f": 1.0, "g": 1.12, "g2": 1.45, "s": 3.3, "s2": 3.7, "pe": 0.5, "fixp": 0.02, "lat": 0.12, "land": 0.2, "slow": 0.08, "net": 2.4, "first": 1.9, "mb": 3.4},
+         {"f": 1.07, "g": 1.65, "g2": 1.9, "s": 3.6, "s2": 3.6, "pe": 0.45, "fixp": 0.0, "lat": 0.04, "land": 0.5, "slow": 0.0, "net": 1.6, "first": 2.5, "mb": 5.0},
+         {"f": 1.05, "g": 1.2, "g2": 2.2, "s": 2.6, "s2": 3.1, "pe": 0.7, "fixp": 0.0, "lat": 0.06, "land": 0.4, "slow": 0.12, "net": 3.0, "first": 1.4, "mb": 3.8})
 
 SCRATCH = {
-    "G0": ("sbuf", [128, WIN], "bfloat16"), "G1": ("sbuf", [128, WIN], "bfloat16"), "G2": ("sbuf", [128, WIN], "bfloat16"),
-    "O": ("sbuf", [128, WIN], "bfloat16"),
-    "CW": ("sbuf", [128, V], "bfloat16"), "RT": ("sbuf", [128, 256], "int32"), "CHN": ("sbuf", [128, 768], "int32"),
-    "HL": ("sbuf", [128, 1536], "bfloat16"), "B": ("sbuf", [128, 52 * H], "bfloat16"),
-    "ZS": ("sbuf", [128, 4 * 144], "bfloat16"), "BO": ("sbuf", [128, 128], "bfloat16"), "ID": ("sbuf", [128, 512], "bfloat16"),
-    "U": ("sbuf", [128, 3072], "uint16"), "I": ("sbuf", [128, 32], "int32"), "S": ("sbuf", [128, 14336], "float32"),
-    "D0": ("psum", [128, 512], "float32"), "D1": ("psum", [128, 512], "float32"),
-    "D2": ("psum", [128, 512], "float32"), "D3": ("psum", [128, 512], "float32"),
-    "CA": ("psum", [128, 512], "float32"), "CB": ("psum", [128, 512], "float32"),
-    "CC": ("psum", [128, 512], "float32"), "VP": ("psum", [128, 512], "float32"),
+    "A": ("sbuf", [128, WIN], "bfloat16"), "B": ("sbuf", [128, WIN], "bfloat16"), "C": ("sbuf", [128, WIN], "bfloat16"),
+    "CW": ("sbuf", [128, V], "int32"),
+    "RT": ("sbuf", [128, 256], "int32"), "W": ("sbuf", [128, 56 * H], "bfloat16"), "KG": ("sbuf", [128, 2 * H], "float16"),
+    "ZS": ("sbuf", [128, 144], "bfloat16"), "ZK": ("sbuf", [128, 3 * 144], "float16"), "BO": ("sbuf", [128, 128], "bfloat16"),
+    "ID": ("sbuf", [128, 1664], "bfloat16"), "ONE": ("sbuf", [128, 512], "bfloat16"),
+    "U": ("sbuf", [128, 3072], "uint16"), "I": ("sbuf", [128, 64], "int32"), "S": ("sbuf", [128, 15360], "float32"),
+    "P0": ("psum", [128, 512], "float32"), "P1": ("psum", [128, 512], "float32"), "P2": ("psum", [128, 512], "float32"),
+    "P3": ("psum", [128, 512], "float32"), "P4": ("psum", [128, 512], "float32"), "KD": ("psum", [128, 512], "float32"),
+    "XB": ("psum", [128, 512], "float32"), "YS": ("psum", [128, 512], "float32"),
 }
-PSUM = ("D0", "D1", "D2", "D3", "CA", "CB", "CC", "VP")
-SEMAPHORES = ["cV", "cS", "cP", "cG"] + ["d%d" % i for i in range(24)] + ["arr%d" % i for i in range(8)] + ["snt%d" % i for i in range(8)]
+POOL = ("P0", "P1", "P2", "P3", "P4")
+SEMAPHORES = ["cV", "cS", "cP", "cG"] + ["d%d" % i for i in range(16)] + ["arr%d" % i for i in range(8)] + ["snt%d" % i for i in range(8)]
+PLAN = {}
 
 
 def engines(topo, a, b):
@@ -28,20 +35,28 @@ def engines(topo, a, b):
     return e[::max(1, len(e) // 8)]
 
 
-def build(g, core, T, topo):
+def build(g, core, T, topo, bank, R):
     rank, n = T.rank_of(core), len(T.cores)
     nxt, prv = T.cores[(rank + 1) % n], T.cores[(rank - 1) % n]
     Q = {"V": g.vector, "S": g.scalar, "P": g.tensor, "G": g, "Y": g.sync}
-    ops, recs, top = [], {}, {"S": 0, "U": 0, "B": 0, "VP": 0, "D": 0, "d": 0}
+    ops, recs, top = [], {}, {"S": 0, "U": 0, "W": 0, "#": 0, "d": 0, "r": 0, "tag": "load"}
+    cyc = 0.83e-3 * R["f"]
 
     def ap(x):
         if x[0] == "ind":
             return ap(x[1]).indirect(ap(x[2]))
-        if len(x) == 4:
-            return T[x[0]][:, x[1]:x[2]:x[3]]
-        return T[x[0]][:, x[1]:x[2]]
+        b = T[bank.get(x[0], x[0])]
+        return b[:, x[1]:x[2]:x[3]] if len(x) == 4 else b[:, x[1]:x[2]]
 
-    def add(kind, qs, outs, ins, fn, sem=None, cnt=1, after=()):
+    def psum(x):
+        return x[0][0] == "#" or x[0] in ("KD", "XB", "YS")
+
+    def wid(x):
+        if x[0] == "ind":
+            return 16 * wid(x[2])
+        return (x[2] - x[1] + x[3] - 1) // x[3] if len(x) == 4 else x[2] - x[1]
+
+    def add(kind, qs, outs, ins, fn, cost, sem=None, cnt=1, after=()):
         rd, wr = [], []
         for x in ins:
             if isinstance(x, tuple):
@@ -54,25 +69,33 @@ def build(g, core, T, topo):
         deps, me = set(after), len(ops)
         for x, w in [(x, 0) for x in rd] + [(x, 1) for x in wr]:
             for lo, hi, w2, who in recs.get(x[0], []):
-                if (x[0] in PSUM and (ops[who]["qs"] != qs or len(qs) > 1)) or ((w or w2) and lo < x[2] and x[1] < hi):
+                if (psum(x) and (ops[who]["qs"] != qs or len(qs) > 1)) or ((w or w2) and lo < x[2] and x[1] < hi):
                     deps.add(who)
         for x, w in [(x, 0) for x in rd] + [(x, 1) for x in wr]:
             recs.setdefault(x[0], []).append((x[1], x[2], w, me))
-        ops.append({"kind": kind, "qs": qs, "deps": deps, "fn": fn, "sem": sem, "cnt": cnt})
+        ops.append({"kind": kind, "qs": qs, "deps": deps, "fn": fn, "sem": sem, "cnt": cnt, "cost": cost, "tag": top["tag"],
+                    "lent": [x[0] for x in rd + wr if x[0][0] == "#"]})
         return me
+
+    def span(o, a, per, two=False):
+        if o[0] == "ind":
+            return 0.05 + wid(o) * R["s2" if two else "s"] * cyc
+        if a[0] == "ind":
+            return 0.055 + wid(o) * R["g2" if two else "g"] * cyc
+        return 0.005 + max(64, wid(o) * per) * cyc
 
     def new(buf, w):
         lo = top[buf]
-        if buf == "VP" and lo + w > 512:
-            lo = 0
+        if buf == "#":
+            top[buf] += 1
+            return ("#%d" % lo, 0, w)
         top[buf] = lo + (w + 15) // 16 * 16
         return (buf, lo, lo + w)
 
     def sub(x, lo, w):
+        if len(x) == 4:
+            return (x[0], x[1] + lo * x[3], x[1] + (lo + w - 1) * x[3] + 1, x[3])
         return (x[0], x[1] + lo, x[1] + lo + w)
-
-    def wid(x):
-        return x[2] - x[1]
 
     def val(x):
         return ap(x) if isinstance(x, tuple) else x
@@ -82,328 +105,634 @@ def build(g, core, T, topo):
 
     def tt(o, a, b, op):
         o = out(o, b)
-        add("c", "V", [o], [a, b], lambda q: g.vector.tensor_tensor(ap(o), ap(a), ap(b), op))
+        add("c", "V", [o], [a, b], lambda q: g.vector.tensor_tensor(ap(o), ap(a), ap(b), op), span(o, a, 1 if psum(a) or psum(b) else 2, True))
         return o
 
     def ts(o, a, s1, op0, s2=None, op1=None):
         o = out(o, a)
         if op1 is None:
-            add("c", "V", [o], [a, s1], lambda q: g.vector.tensor_scalar(ap(o), ap(a), val(s1), None, op0))
+            add("c", "V", [o], [a, s1], lambda q: g.vector.tensor_scalar(ap(o), ap(a), val(s1), None, op0), span(o, a, 1))
         else:
-            add("c", "V", [o], [a, s1, s2], lambda q: g.vector.tensor_scalar(ap(o), ap(a), val(s1), val(s2), op0, op1))
+            add("c", "V", [o], [a, s1, s2], lambda q: g.vector.tensor_scalar(ap(o), ap(a), val(s1), val(s2), op0, op1), span(o, a, 1))
         return o
 
     def cp(o, a):
         o = out(o, a)
-        add("c", "V", [o], [a], lambda q: g.vector.tensor_copy(ap(o), ap(a)))
+        add("c", "V", [o], [a], lambda q: g.vector.tensor_copy(ap(o), ap(a)), span(o, a, 1))
         return o
 
-    def fill(o, c):
-        return add("c", "V", [o], [], lambda q: g.vector.memset(ap(o), c))
-
-    def act(o, a, f, bias, scale=1.0):
-        add("c", "S", [o], [a], lambda q: g.scalar.activation(ap(o), ap(a), f, bias=bias, scale=scale))
-
-    def move(o, a):
-        add("c", "SV", [o], [a], lambda q: g.vector.tensor_copy(ap(o), ap(a)) if q == "V" else g.scalar.activation(ap(o), ap(a), F.Copy))
+    def pick(o, d0, d1, op=A.add):
+        add("c", "V", [o], [d0, d1], lambda q: g.vector.tensor_tensor_scan(ap(o), ap(d0), ap(d1), 0.0, A.mult, op), span(o, d0, 1))
         return o
 
-    def sign(o, a):
-        add("c", "SV", [o], [a], lambda q: g.vector.tensor_scalar(ap(o), ap(a), -1.0, 1.0, A.max, A.min) if q == "V"
-            else g.scalar.activation(ap(o), ap(a), F.Sign))
+    def fill(o, c, per=1):
+        return add("c", "V", [o], [], lambda q: g.vector.memset(ap(o), c), span(o, o, per))
 
-    def mm(o, whole, terms):
+    def act(o, a, scale=1.0, bias=0.0, f=F.Identity):
+        o = out(o, a)
+        add("c", "S", [o], [a], lambda q: g.scalar.activation(ap(o), ap(a), f, bias=bias, scale=scale), span(o, a, 1))
+        return o
+
+    def either(name, o, a, fv, fs):
+        name = "%s.%d" % (name, len([x for x in ops if x.get("name", "").startswith(name + ".")]))
+        i = add("c", "SV", [o], [a], lambda q: fv() if q == "V" else fs(), span(o, a, 1))
+        ops[i]["name"] = name
+        return o
+
+    def move(name, o, a):
+        return either(name, o, a, lambda: g.vector.tensor_copy(ap(o), ap(a)), lambda: g.scalar.activation(ap(o), ap(a), F.Copy))
+
+    def sign(name, o, a):
+        return either(name, o, a, lambda: g.vector.tensor_scalar(ap(o), ap(a), -1.0, 1.0, A.max, A.min),
+                      lambda: g.scalar.activation(ap(o), ap(a), F.Sign))
+
+    def above(name, o, d):
+        either(name, o, d, lambda: g.vector.tensor_scalar(ap(o), ap(d), 0.0, 0.5, A.is_gt, A.subtract),
+               lambda: g.scalar.activation(ap(o), ap(d), F.Sign, bias=-0.5))
+
+    def flag(o, a):
+        act(o, a, 1.0, 0.5 - V, F.Sign)
+
+    def mm(o, whole, terms, per=1, opens=True, closes=True):
         def fn(q):
             for i, (l, r) in enumerate(terms):
-                last = g.tensor.matmul(ap(o), ap(l), ap(r), i == 0, i == len(terms) - 1)
+                last = g.tensor.matmul(ap(o), ap(l), ap(r), opens and i == 0, closes and i == len(terms) - 1)
             return last
-        add("c", "P", [o], whole, fn)
+        add("c", "P", [o], whole, fn, len(terms) * (per * max(64, wid(o)) * R["pe"] * 1e-3 + R["fixp"]))
 
-    def iota(o, pat, base, cm):
-        add("c", "G", [o], [], lambda q: g.iota(ap(o), pat, base, cm, allow_small_or_imprecise_dtypes=True))
+    def iota(o, pat, base, cm, after=()):
+        kw = {} if o[0] in ("I", "CW") else {"allow_small_or_imprecise_dtypes": True}
+        add("c", "G", [o], [], lambda q: g.iota(ap(o), pat, base, cm, **kw), 0.13 + 2 * wid(o) * cyc, after=after)
         return o
 
-    def dma(q, o, i, rd, wr, after=()):
+    def dma(q, o, i, rd, wr, cost, after=()):
         top["d"] += 1
-        return add("d", q, wr, rd, lambda q: Q[q].dma_start(o, i), "d%d" % (top["d"] - 1), 16, after)
+        return add("d", q, wr, rd, lambda q: Q[q].dma_start(o, i), cost, "d%d" % (top["d"] - 1), 16, after)
 
-    def ind(win, end, off):
-        return ("ind", (win, 0, end), off)
+    def renew(o, i, end, after=()):
+        dma("Y", T[o][:, 0:end], T[i][:, 0:end], [(i, 0, end)], [(o, 0, end)], R["mb"], after)
+
+    def ind(win, off):
+        return ("ind", win if isinstance(win, tuple) else (win, 0, SCRATCH[win][1][1]), off)
 
     def lists(o, src, sel):
-        z = sel * 144
-        mm(o, [("ZS", z, z + 144), src], [(("ZS", z + 15 - i, z + 143 - i), (src[0], src[1] + i, src[2], 16)) for i in range(16)])
+        mm(o, [sel, src], [(sub(sel, 15 - i, 128), (src[0], src[1] + i, src[2], 16)) for i in range(16)])
+        return o
 
-    def half(x, h):
-        w = wid(x) // 2
-        return sub(x, w * h, w)
+    def count(cm):
+        return lists(new("#", wid(cm) // 16), cm, ("ZS", 0, 144))
+
+    def part(x, h, k=2):
+        return sub(x, wid(x) // k * h, wid(x) // k)
 
     def col(x, o, k=1):
         return sub(x, 64 * o, 64 * k)
 
-    I1, IN, I2, IM = ("ID", 0, 128), ("ID", 128, 256), ("ID", 256, 384), ("ID", 384, 512)
+    def pair(x, o, k=1):
+        return sub(x, 128 * o, 128 * k)
 
-    def mix(terms):
-        d = ("D%d" % (top["D"] % 4), 0, 512)
-        top["D"] += 1
-        mm(d, [x for p in terms for x in p], terms)
+    def even(x):
+        return (x[0], x[1], x[2] - 1, 2)
+
+    def odd(x):
+        return (x[0], x[1] + 1, x[2], 2)
+
+    I1, IN, IM, IH, IQ, IR, I2, IB, IC, K1, N1, N2, N3 = [("ID", 128 * k, 128 * k + 128) for k in range(13)]
+
+    def mix(terms, early=0):
+        d = new("#", wid(terms[0][1]))
+        early = early if OPT["early"] else 0
+        if early:
+            mm(d, [x for p in terms[:early] for x in p], terms[:early], 1, True, False)
+        mm(d, [x for p in terms[early:] for x in p], terms[early:], 1, not early, True)
         return d
 
-    def gather(win, end, off):
-        o = new("B", H)
+    def halves(terms, h):
+        return [(l, part(v, h)) for l, v in terms]
+
+    def gather(name, win, off, o=None):
+        o = o or new("W", H)
         for h in range(2):
-            move(half(o, h), ind(win, end, half(off, h)))
+            move(name, part(o, h), ind(win, part(off, h)))
         return o
 
-    dma("S", T.RT[:], T.rt[:], [], [("RT", 0, 256)])
-    d1 = dma("Y", T.G0[:, 0:V], T.rec[:], [], [("G0", 0, V)])
-    for o in range(3):
-        d1 = dma("Y", T.CHN[:, o * 256:(o + 1) * 256], T.ch[:, o * V:(o + 1) * V], [], [("CHN", o * 256, (o + 1) * 256)])
-    d0 = fill(("CW", 0, V), 0.0)
-    add("c", "G", [("I", 0, 1)], [], lambda q: g.iota(ap(("I", 0, 1)), [[0, 1]], 0, 1))
+    def knockout(name, rec, later, ids, chain, k, nh):
+        wh, w, win = H // nh, 64 // nh, A.is_ge if later else A.is_lt
+        cms = sub(duel, 6 * k * wh, 6 * wh)
+        for h in range(k * 2 // nh, (k + 1) * 2 // nh):
+            r = [sub(rec, o * H + h * 512, 512) for o in range(4)]
+            at = [sub(cms, j * wh + h * 512 % wh, 512) for j in range(6)]
+            if OPT["held"]:
+                d = mix([(I1, r[0])])
+            for j, (a, b) in enumerate(((0, 1), (0, 2), (0, 3), (1, 2), (1, 3), (2, 3))):
+                if j < OPT["held"]:
+                    tt(at[j], d, r[b], A.is_gt if later else A.is_lt)
+                else:
+                    above(name, at[j], mix([(I1, r[a]), (IN, r[b])] if later else [(IN, r[a]), (I1, r[b])]))
+        f = [part(odd(pair(fq, o)), k, nh) for o in range(3)]
+        ca, cb = count(sub(cms, 0, 3 * wh)), count(sub(cms, 3 * wh, 3 * wh))
+        ts(f[0], sub(ca, 0, w), 9.0 if OPT["held"] else 0.5, win)
+        fa, fb = ts("S", sub(ca, w, 2 * w), 9.0 if OPT["held"] else 0.5, win), ts(("KD", 384, 384 + 2 * w), sub(cb, 0, 2 * w), 0.5, win)
+        fc = ts("S", sub(cb, 2 * w, w), 0.5, win)
+        d = tt(fb, fb, fa, A.subtract)
+        tt(f[1], tt(sub(d, 0, w), sub(d, 0, w), f[0], A.mult), sub(fa, 0, w), A.add)
+        u = tt(sub(d, w, w), tt(sub(d, w, w), sub(d, w, w), f[0], A.mult), sub(fa, w, w), A.add)
+        tt(f[2], tt("S", tt(sub(d, 0, w), fc, u, A.subtract), f[1], A.mult), u, A.add)
+        for o in range(3):
+            tt(part(even(chain[o]), k, nh), part(ids[o], k, nh), part(odd(chain[o]), k, nh), A.subtract)
+            pick(part(chain[o + 1], k, nh), part(pair(fq, o), k, nh), part(chain[o], k, nh))
+        return f
+
+    dma("S", T.RT[:], T.rt[:], [], [("RT", 0, 256)], 2.0)
+    first = dma("Y", T.A[:, 0:V], T.rec[:], [], [("A", 0, V)], R["mb"] + 0.3)
+    dma("Y", T.B[:, 0:V], T.rec[:], [], [("B", 0, V)], R["mb"], [first])
+    iota(("I", 0, 1), [[0, 1]], 0, 1)
+    dz0 = iota(new("S", 256), [[0, 4], [16, 64]], V, 1)
     tz = iota(new("S", 144), [[1, 144]], -15, 0)
-    ig = iota(new("S", 128), [[16, 8], [0, 16]], 0, 0)
     dc0 = iota(new("S", 256), [[16, 2], [-1, 128]], 0, 1)
-    dz0 = iota(new("S", 192), [[0, 3], [16, 64]], DUMMY, 1)
-    ob0 = iota(new("S", 16), [[128, 4], [16, 4]], 0, 1)
-    iota(sub(ob0, 0, 15), [[128, 3], [16, 5]], 0, 1)
-    ts(("I", 1, 2), ("I", 0, 1), 112, A.bitwise_and)
-    ts(("I", 2, 3), ("I", 0, 1), 1, A.arith_shift_right, 7, A.bitwise_and)
-    c2 = cp("S", ("I", 1, 3))
-    g16, ph = sub(c2, 0, 1), sub(c2, 1, 1)
-    ts(("ZS", 0, 144), tz, g16, A.is_equal)
-    r = cp("S", ("RT", 0, 256)); ur = cp("U", ("RT", 0, 256))
-    roots, uroots = [col(r, o) for o in range(4)], [col(ur, o) for o in range(4)]
-    rid = r
+    ig = iota(new("S", 128), [[16, 8], [0, 16]], 0, 0)
+    n0 = iota(new("S", 5), [[256, 5]], 0, 16)
+    iota(("CW", 0, V), [[0, V]], V, 0, range(len(ops) - 6, len(ops)))
     for o in range(3):
-        ts(("ZS", 144 * (o + 1), 144 * (o + 2)), tz, g16, A.is_equal, ts("S", ph, float(o), A.is_equal), A.mult)
+        dma("Y", T.CW[o:128:16, :], T.ch[:, o * V:(o + 1) * V], [], [("CW", 0, V)] if o == 0 else [], 2.5, [len(ops) - 1 - o])
+    recs["CW"] += [(0, V, 1, len(ops) - 1), (0, V, 1, len(ops) - 2)]
+    ts(("I", 1, 2), ("I", 0, 1), 112, A.bitwise_and)
+    ts(("I", 2, 3), ("I", 0, 1), 15, A.bitwise_and)
+    c2 = cp("S", ("I", 1, 3))
+    g16, i16 = sub(c2, 0, 1), sub(c2, 1, 1)
+    dp = ts("S", dz0, g16, A.subtract)
+    rr, ur = new("S", 512), new("U", 256)
+    r = cp(("KD", 0, 256), ("RT", 0, 256))
+    cp(ur, tt(odd(rr), r, tt("S", ts(("KD", 256, 512), r, 0.0, A.is_equal), dp, A.mult), A.max))
+    fill(("A", V, WIN), FAR, 0.5)
+    act(("B", V, WIN), ("A", V, WIN))
+    ts(("ZS", 0, 144), tz, g16, A.is_equal)
+    dc_, dm_, nb_, dp2, bw = [act(new("S", 384), ("A", V, V + 384), 0.0) for k in range(5)]
+    ll = new("W", 320)
+    act(col(ll, 0), ("A", V, V + 64), 0.0, -1.0)
+    act(odd(dp2), col(dp, 0, 3))
+    duel, fq = new("W", 6 * H), act(new("W", 384), ("A", V, V + 384), 0.0)
+    c16 = new("W", 192)
+    for o in range(3):
+        ts(col(c16, o), col(dp, 0), i16, A.subtract, float((o + 1) * H - V), A.add)
+    jp, dj = new("S", 384), act(new("S", 384), ("A", V, V + 384), 0.0)
+    for o in range(3):
+        act(odd(pair(jp, o)), col(dp, 0), 1.0, float((o + 1) * H - V))
+    act(odd(pair(dj, 0)), ("A", V, V + 64), -1.0)
+    j2 = act("S", col(dp, 0), 2.0, float(H - 2 * V))
+    rows = ts("S", sub(tz, 15, 3), i16, A.is_equal, ts("S", i16, 3.0, A.is_equal), A.add)
+    for o in range(3):
+        ts(("ZK", 144 * o, 144 * o + 144), tz, g16, A.is_equal, sub(rows, o, 1), A.mult)
     ts(("BO", 0, 128), ig, g16, A.is_equal)
-    for x, c in ((I1, 1.0), (IN, -1.0), (I2, 2.0), (IM, -2.0)):
-        ts(x, sub(dc0, 0, 128), 0.0, A.is_equal, c, A.mult)
+    ts(I1, sub(dc0, 0, 128), 0.0, A.is_equal)
+    for x, c in ((IN, -1.0), (IM, -2.0), (IH, 0.5), (IQ, -0.25), (IR, MAGIC), (I2, 2.0), (IB, BIG / 2), (IC, -BIG / 2),
+                 (K1, 1.0 * H), (N1, -1.0 * H), (N2, -2.0 * H), (N3, -3.0 * H)):
+        act(x, I1, c)
+    F1 = act(new("S", 128), I1)
+    FB = act(new("S", 128), I1, -BIG)
+    act(("ONE", 0, 512), ("A", V, V + 512), 1 / FAR)
     far = ts("S", ig, g16, A.not_equal, 999.0, A.mult)
-    dz = ts("S", dz0, g16, A.subtract)
-    z = ts("S", col(dz0, 0), g16, A.subtract, float(-H), A.add)
-    ob = ts("S", ob0, g16, A.subtract)
     dc = new("S", 256)
     for k in range(2):
-        tt(half(dc, k), half(dc0, k), far, A.add)
-    bw = new("S", 400)
-    fill(bw, 0.0)
-    fill(("G0", DUMMY, WIN), 256.0)
-    for w in ("G1", "G2") if OPT["late"] else ("G1",):
-        iota((w, DUMMY, WIN), [[0, H]], 256, 0)
-    gxs, nls = [new("S", 320), new("S", 320)], [new("S", 256), new("S", 256)]
-    yss = [new("S", 256), new("S", 256)]
+        tt(part(dc, k), part(dc0, k), far, A.add)
+    n16 = ts("S", n0, ts("S", g16, 16.0, A.mult), A.subtract)
+
+    ys = ("YS", 0, 512)
+    lid = None
     for t in range(2):
-        cp(col(yss[t], 0), z)
-        fill(col(gxs[t], 0), 1.0); fill(col(gxs[t], 4), 0.0); fill(col(nls[t], 0), 0.0)
-    for k in range(2):
-        d = ("D%d" % k, 0, 384)
-        cp(d, ("CHN", 384 * k, 384 * k + 384))
-        move(("HL", 384 * k, 384 * k + 384), d)
-        tt(("HL", 768 + 384 * k, 768 + 384 * k + 384), d, ("HL", 384 * k, 384 * k + 384), A.subtract)
-    fill(("G0", 0, 1), 256.0)
-    rows = []
-    for o in range(3):
-        for k in range(2):
-            c = k * 768 + o * 256
-            rows.append(dma("Y", T.CW[2 * o + k:128:16, :], T.HL[:, c:c + 256], [("HL", c, c + 256)], [], [d0]))
-    recs["CW"] += [(0, V, 1, x) for x in rows]
-    dma("Y", T.O[:, 0:V], T.rec[:], [], [("O", 0, V)], [d1])
-
-    def renew(w):
-        c = OPT["copy"]
-        if c < V:
-            dma("Y", T[w][:, c:V], T.O[:, c:V], [("O", c, V)], [(w, c, V)])
-        for k in range(0, c, 1024):
-            move((w, k, k + 1024), ("O", k, k + 1024))
-
-    dlt = wnm = lid = None
-    for t in range(2):
-        end = V if t == 0 else DUMMY
-        gx, nl = gxs[t], nls[t]
-        zx, wx = new("B", 16 + H), new("B", 16 + H)
-        zt, wt = sub(zx, 16, H), sub(wx, 16, H)
-        fill(sub(zx, 0, 16), 0.0)
-
-        def shift(src):
-            mm(("CA", 64, 66), [("BO", 0, 128), src], [(("BO", 0, 128), src)])
-            i0 = 8 + 8 * t
-            cp(("I", i0, i0 + 1), ("CA", 64, 65))
-            ts(("I", i0 + 2, i0 + 3), ("I", i0, i0 + 1), 4, A.arith_shift_right, 63, A.bitwise_and)
-            ts(("I", i0 + 3, i0 + 4), ("I", i0, i0 + 1), 15, A.bitwise_and)
-            return cp("S", ("I", i0 + 2, i0 + 4))
-        wl, m, um, nh = new("S", 128), roots[0], uroots[0], OPT["ch"][t]
-        for o in (1, 2, 3):
-            ro = gather("G0", end, uroots[o])
-            m2, um2, cm = new("S", 64), new("U", 64), new("B", H)
+        old, win, tgt = ("B", "A", "C") if t == 0 else ("C", "C", "C")
+        roots = [odd(pair(rr, o)) for o in range(4)]
+        top["tag"] = "champion%d" % t
+        m, um, nh = roots[0], col(ur, 0), OPT["nh"][t]
+        if OPT["form"][t] == "P":
+            rd, um = new("W", 4 * H), new("U", 64)
             for h in range(2):
-                sm = (o, h) in OPT["cmode"][t]
-                if sm:
-                    mo = move(new("B", 512), ind("G0", end, half(um, h)))
-                    act(half(cm, h), mix([(I1, mo), (IN, half(ro, h))]), F.Sign, -0.5)
+                for o in range(4):
+                    move("root", sub(rd, o * H + h * 512, 512), ind("A", part(col(ur, o), h)))
+            chain = [pair(rr, 0), new("S", 128), new("S", 128), pair(ys, 0)]
+            for k in range(nh):
+                knockout("duel", rd, True, roots[1:], chain, k, nh)
+                cp(part(um, k, nh), part(odd(chain[3]), k, nh))
+            m = odd(pair(ys, 0))
+        if OPT["form"][t][0] == "T":
+            rd, um, u1, lo = new("W", 3 * H), new("U", 64), new("U", 64), 0
+            chain = [pair(rr, 0), new("S", 128), new("S", 128), pair(ys, 0)]
+            for k in OPT["parts"]:
+                def cut(x):
+                    return sub(x, lo * wid(x) // H, k * wid(x) // H)
+                r = [None] + [move("root", cut(sub(rd, o * H - H, H)), ind("A", cut(col(ur, o)))) for o in (1, 2, 3)]
+                ca, cb, w = sub(duel, 4 * lo, 2 * k), sub(duel, 4 * lo + 2 * k, 2 * k), k // 16
+                tt(part(ca, 0), ind("A", cut(col(ur, 0))), r[1], A.is_gt)
+                if OPT["form"][t][1] == "A":
+                    tt(part(ca, 1), ind("A", cut(col(ur, 2))), r[3], A.is_gt)
+                for c in range(0, k, 512) if OPT["form"][t][1] == "S" else ():
+                    e = min(512, k - c)
+                    above("duel", sub(ca, k + c, e), mix([(I1, sub(r[2], c, e)), (IN, sub(r[3], c, e))]))
+                f = [cut(odd(pair(fq, o))) for o in range(3)]
+
+                def step(o):
+                    tt(cut(even(chain[o])), cut(roots[o + 1]), cut(odd(chain[o])), A.subtract)
+                    return odd(pick(cut(chain[o + 1]), cut(pair(fq, o)), cut(chain[o])))
+                na = count(ca)
+                ts(f[0], part(na, 0), 9.0, A.is_ge)
+                f32 = ts("S", part(na, 1), 9.0 if OPT["form"][t][1] == "A" else 0.5, A.is_ge)
+                cp(cut(u1), step(0))
+                for j in range(2):
+                    tt(part(cb, j), ind("A", cut(u1)), r[2 + j], A.is_gt)
+                nb = count(cb)
+                ts(f[1], part(nb, 0), 9.0, A.is_ge)
+                f3 = ts("S", part(nb, 1), 9.0, A.is_ge)
+                step(1)
+                tt(f[2], tt("S", tt("S", f32, f3, A.subtract), f[1], A.mult), f3, A.add)
+                cp(cut(um), step(2))
+                lo += k
+            m = odd(pair(ys, 0))
+        for o in (1, 2, 3) if OPT["form"][t][0] not in "PT" else ():
+            form = OPT["form"][t][o - 1]
+            ex = gather("root", "A", um if form == "B" else col(ur, o))
+            mo, um2, cm = pair(ys, 0) if o == 3 else new("S", 128), new("U", 64), new("W", H)
+            if form == "S":
+                em = gather("best", "A", um)
+            for h in range(2):
+                if form == "A":
+                    tt(part(cm, h), ind("A", part(um, h)), part(ex, h), A.is_gt)
+                elif form == "B":
+                    tt(part(cm, h), ind("A", part(col(ur, o), h)), part(ex, h), A.is_lt)
                 else:
-                    tt(half(cm, h), ind("G0", end, half(um, h)), half(ro, h), A.is_gt)
+                    above("duel", part(cm, h), mix([(I1, part(em, h)), (IN, part(ex, h))], o // 3))
                 if nh == 1 and h == 0:
                     continue
-                part = (lambda x: half(x, h)) if nh == 2 else (lambda x: x)
-                cnt = ("CB" if h and nh == 2 else "CA", 0, 64 // nh)
-                lists(cnt, part(cm), 0)
-                d = tt("S" if nh == 2 else "VP", part(roots[o]), part(m), A.subtract)
-                w = ts(part(col(gx, 3) if o == 3 else col(wl, o - 1)), cnt, 2.0 if sm else 9.0, A.is_ge)
-                tt(part(m2), part(m), tt("S" if nh == 2 else "VP", w, d, A.mult), A.add)
-                cp(part(um2), part(m2))
-            m, um = m2, um2
-        mid, umid, cg = (m, um, new("B", H)) if t == 0 else (new("S", 64), new("U", 64), new("B", H))
-        for h in range(2):
-            move(half(zt, h), ind("G0", end, half(um, h)))
-            if h == 0 and OPT["early"]:
-                cp(sub(zx, 0, 2), shift(sub(cp(new("B", 16), ind("G0", end, sub(um, 0, 1))), 0, 2)))
-            pa, pb = (sub(wx, 0, 528), sub(zx, 0, 528)) if h == 0 and OPT["early"] else (half(wt, h), half(zt, h))
-            e, k = engines(topo, core, nxt), 2 * t + h
+                k = h if nh == 2 else 0
+                tt(part(odd(pair(dc_, o - 1)), k, nh), part(m, k, nh), part(roots[o], k, nh), A.subtract)
+                ts(part(even(pair(rr, o)), k, nh), count(part(cm, k, nh)), 0.5 if form == "S" else 9.0, A.is_lt)
+                pick(part(mo, k, nh), part(pair(dc_, o - 1), k, nh), part(pair(rr, o), k, nh))
+                cp(part(um2, k, nh), part(odd(mo), k, nh))
+            m, um = odd(mo), um2
+        z, w, near, kg, lo = new("W", H), new("W", H), new("W", 4 * H), ("KG", t * H, t * H + H), 0
+        zn = sub(near, 0, H)
+        for k in OPT["send"][t]:
+            move("z", sub(z, lo, k), ind("A", sub(um, lo // 16, k // 16)))
+            e, s = engines(topo, core, nxt), top["r"]
+            top["r"] += 1
             r_id, pid = topo.addr(nxt)[:2]
 
-            def send(q, a=pa, b=pb, k=k, e=e, r_id=r_id, pid=pid):
-                g.remote_dma(ap(a), ap(b), T.sem["arr%d" % k], T.sem["snt%d" % k], pid, r_id, sum(1 << x for x in e))
-            s = add("r", "G", [], [pb], send, "snt%d" % k, len(e))
-            add("a", "", [pa], [], None, "arr%d" % k, len(engines(topo, prv, core)), [s])
+            def send(q, a=sub(w, lo, k), b=sub(z, lo, k), s=s, e=e, r_id=r_id, pid=pid):
+                g.remote_dma(ap(a), ap(b), T.sem["arr%d" % s], T.sem["snt%d" % s], pid, r_id, sum(1 << x for x in e))
+            x = add("r", "G", [], [sub(z, lo, k)], send, 0.3 + (R["first"] if s == 0 else 0), "snt%d" % s, len(e))
+            add("a", "", [sub(w, lo, k)], [], None, R["net"] * (0.6 + 0.8 * k / H), "arr%d" % s, len(engines(topo, prv, core)), [x])
+            lo += k
+        top["tag"] = "kids%d" % t
+        lo = 0
+        for k in OPT["parts"] if t == 0 else (512, 512):
+            ts(sub(kg, lo, k), ind("CW", sub(um, lo // 16, k // 16)), -V / 2, A.add)
+            lo += k
+        for o in range(4):
+            tt(even(pair(rr, o)), roots[o], m, A.is_equal)
+        keep = [tt("S", roots[0], m, A.not_equal), tt("S", even(pair(rr, 2)), even(pair(rr, 3)), A.add), even(pair(rr, 3))]
+        kd = ("KD", 0, 384)
         if t == 1:
-            cp(umid, tt(mid, m, tt("VP", dlt, tt("VP", m, z, A.is_equal), A.mult), A.add))
-        for h in range(2):
-            move(half(cg, h), ind("CW", V, half(umid, h)))
-        for o in range(3):
-            lists(("CC", 64 * o, 64 * o + 64), cg, 1 + o)
-        tt(col(gx, 2), col(wl, 1), col(gx, 3), A.max)
-        tt(col(gx, 1), col(wl, 0), col(gx, 2), A.max)
-        a = tt("S", rid, tt("VP", col(gx, 0, 4), col(gx, 1, 4), A.is_equal), A.mult)
-        nd = tt("S", dz, ts("VP", col(a, 0, 3), 0.0, A.is_equal), A.mult)
-        a1 = tt("S", col(a, 0, 3), nd, A.add)
-        kid = ("CC", 0, 192)
-        if t == 1:
-            eq = new("VP", 192)
+            won, mc, bw = new("S", 192), cp("S", m), new("S", 384)
             for o in range(3):
-                tt(col(eq, o), col(wnm, o), m, A.is_equal)
-            kid = tt("VP", tt("S", tt("S", lid, kid, A.subtract), eq, A.mult), kid, A.add)
-        dlt = tt("S", mid, z, A.subtract)
+                tt(col(won, o), odd(pair(ys, o + 1)), mc, A.is_equal)
+                tt(odd(pair(nb_, o)), keep[o], col(won, o), A.is_gt)
+            tt(odd(kd), won, tt("S", ts(("KD", 0, 192), lid, float(V), A.is_lt), lid, A.mult), A.mult)
         for o in range(3):
-            move(sub(bw, 128 * o + 64, 64), tt(sub(bw, 128 * o, 64), col(gx, o + 1), col(kid, o), A.mult))
-        Gw = ["G0"] * 3 if t == 0 else ["G1", "G1", "G2" if OPT["late"] else "G1"]
-        zn = (Gw[0], ZONE, DUMMY)
-        sc = sub(wx, 0, 2) if OPT["early"] else shift(sub(wt, 0, 2))
-        uob = ts("U", ob, sub(sc, 0, 1), A.add)
-        pp = ts("S", dc, sub(sc, 1, 1), A.is_equal)
-        g1 = cp(new("S", 240), ("ind", bw, sub(uob, 0, 15)))
-        bs = [("CB", 0, 64), ("CC", 64, 192)]
+            kid = lists(even(pair(kd, o)), kg, ("ZK", 144 * o, 144 * o + 144))
+            if t == 1:
+                pick(pair(bw, o), pair(nb_, o), pair(kd, o))
+            else:
+                tt(odd(pair(bw, o)), keep[o], kid, A.mult)
+        pick(("XB", 1, 385), dp2, pair(rr, 0, 3), A.max)
+        a3 = odd(pick(new("S", 128), pair(dp2, 0), pair(rr, 3), A.max))
+        xb = ("XB", 2, 386)
+        sm = new("#", 2)
+        mm(sm, [("BO", 0, 128), sub(w, 0, 2)], [(("BO", 0, 128), sub(w, 0, 2))])
+        i0 = 8 + 24 * t
+        ts(("I", i0, i0 + 5), n16, sub(sm, 0, 1), A.add)
+        ts(("I", i0 + 8, i0 + 13), ("I", i0, i0 + 5), 3, A.arith_shift_right, 126, A.bitwise_and)
+        us = ts("U", ("I", i0 + 8, i0 + 13), 1.0, A.add)
+        ts(("I", i0 + 16, i0 + 17), ("I", i0, i0 + 1), 15, A.bitwise_and)
+        pp = ts("S", dc, cp("S", ("I", i0 + 16, i0 + 17)), A.is_equal)
+        xs, ux = new("S", 384), new("U", 192)
         for o in range(3):
-            mm(("CC" if o else "CB", 64 * o, 64 * o + 64), [pp, g1], [(half(pp, 0), sub(g1, 80 * o, 64)), (half(pp, 1), sub(g1, 80 * o + 1, 64))])
-        for h in range(2):
-            d = mix([(I1, half(zt, h)), (I1, half(wt, h))])
-            act(d, d, F.Identity, MAGIC, 0.4995)
-            act(half(zn, h), d, F.Identity, -MAGIC)
-        if Gw[2] != Gw[0]:
-            dma("Y", T.G2[:, ZONE:DUMMY], T.G1[:, ZONE:DUMMY], [zn], [("G2", ZONE, DUMMY)])
-        x1, th, ux = new("S", 192), col(nl, 1, 3), new("U", 192)
-        for o, k, b in ((0, 1, bs[0]), (1, 2, bs[1])):
-            nb = ts("VP", b, 0.0, A.is_equal)
-            tt(col(x1, o, k), tt("S", col(a1, o, k), nb, A.mult), b, A.add)
+            g1 = move("shift", new("S", 80), ("ind", pair(bw, o), us))
+            mm(odd(pair(xb, o)), [pp, g1], [(part(pp, 0), sub(g1, 0, 64)), (part(pp, 1), sub(g1, 1, 64))], 4)
+            if o == 1:
+                continue
+            a, k = (0, 1) if o == 0 else (1, 2)
+            ts(odd(pair(nb_, a, k)), odd(pair(xb, a, k)), 0.0, A.is_equal)
+            pick(pair(xs, a, k), pair(nb_, a, k), pair(xb, a, k))
             if o == 0:
-                cp(col(ux, 0), col(x1, 0))
-            tt(col(th, o, k), col(nd, o, k), nb, A.mult)
-        tt(col(th, 1), col(th, 1), col(th, 0), A.max)
-        tt(col(th, 2), col(th, 2), col(th, 1), A.max)
-        cp(col(ux, 1, 2), tt(col(x1, 1, 2), col(x1, 1, 2), col(th, 1, 2), A.max))
-        xt = [col(x1, o) for o in range(3)]
-        st = new("S", 256)
-        ts(col(st, 3), tt("VP", col(th, 2), col(a, 3), A.add), 0.0, A.is_equal)
-        tt(col(st, 0, 3), th, col(nl, 0, 3), A.is_gt)
-        tt(col(a, 0, 3), col(a, 0, 3), tt("VP", x1, col(a, 0, 3), A.not_equal), A.mult)
-        pw = OPT["put"]
+                cp(col(ux, 0), odd(pair(xs, 0)))
+        x = [odd(pair(xs, o)) for o in range(3)]
+        for o in range(3):
+            flag(col(ll, o + 1), x[o])
+            if o < 2:
+                cp(col(ux, o + 1), tt(x[o + 1], x[o + 1], tt("S", col(ll, o + 1), x[o], A.mult), A.max))
+        top["tag"] = "mean%d" % t
+        for lo, k in ((0, 512), (512, 512)):
+            one, zp = ("ONE", 0, k), sub(zn, lo, k)
+            d = mix([(IH, sub(z, lo, k)), (IQ, one), (IH, sub(w, lo, k)), (IR, one)], 2)
+            either("mean", zp, d, lambda o=zp, d=d: g.vector.tensor_scalar(ap(o), ap(d), -MAGIC, None, A.add),
+                   lambda o=zp, d=d: g.scalar.activation(ap(o), ap(d), F.Identity, bias=-MAGIC))
+        form, xd = OPT["meld"][t], []
+        for o in range(3):
+            top["tag"] = "first%d%d" % (t, o)
+            xd.append(gather("first", old, col(ux, o), sub(near, H + o * H, H)) if o or form[0] != "A" else None)
+        top["tag"] = "put%d" % t
+        pw = OPT["putz"]
         for c in range(0, H, pw):
-            cp(ind("O", V, sub(umid, c // 16, pw // 16)), sub(zn, c, pw))
-        ys, yd, lid, rl4 = yss[t], zn, new("S", 192), new("S", 256)
-        y, roots, uroots = col(ys, 0), [], []
+            cp(ind(win, sub(um, c // 16, pw // 16)), sub(zn, c, pw))
+        if t == 0:
+            renew(tgt, win, WIN)
+        top["tag"] = "roots%d" % t
+        flag(col(ll, 4), a3)
+        ns = act("S", mix([(IB, col(ll, 0, 4)), (IC, col(ll, 1, 4))]), 1.0, BIG)
+        tt(("XB", 1, 384, 2), even(xb), odd(xs), A.is_equal)
+        a2 = pick(new("S", 384), dp2, ("XB", 1, 385), A.max)
+        rr, ur, lid = new("S", 512), new("U", 256), new("S", 192)
 
         def root(o, k):
-            ro = tt(col(rl4, o, k), col(a, o, k), tt("VP", col(st, o, k), col(ys, o, k), A.mult), A.add)
-            uo = cp("U", ro)
-            roots.extend([col(ro, j) for j in range(k)]); uroots.extend([col(uo, j) for j in range(k)])
-        for o in range(3):
-            win, cm = Gw[o], new("B", H)
-            if t == 0 and o:
-                root(2, 1) if o == 2 else root(0, 2)
-            dl = tt("VP", y, xt[o], A.subtract)
-            sm = o in OPT["smode"][t]
-            if sm:
-                xd = gather(win, WIN, col(ux, o))
-            for h in range(2):
-                if sm:
-                    act(half(cm, h), mix([(I1, half(xd, h)), (IN, half(yd, h))]), F.Sign, -0.5)
-                else:
-                    tt(half(cm, h), ind(win, WIN, half(col(ux, o), h)), half(yd, h), A.is_gt)
-            lists(("CA", 0, 64), cm, 0)
-            p = tt("VP", ts("S", ("CA", 0, 64), 2.0 if sm else 9.0, A.is_ge), dl, A.mult)
-            y2 = tt(col(ys, o + 1), xt[o], p, A.add)
-            ls = tt("S", y, p, A.subtract)
-            if t == 0 and o == 2:
-                root(3, 1)
-            yo, last = yd, sm and o == 2
-            if not last:
-                yd = gather(win, WIN, cp("U", y2))
-            rl = new("B", H) if sm and not last else gather(win, WIN, cp("U", ls))
-            ut = cp("U", tt(col(lid, o), ls, tt("VP", dlt, tt("VP", ls, z, A.is_equal), A.mult), A.add))
-            sg = new("B", H)
-            for h in range(2):
-                if last:
-                    sign(half(sg, h), mix([(I1, half(xd, h)), (I1, half(yo, h)), (IM, half(rl, h))]))
-                elif sm:
-                    x, y0, y1 = half(xd, h), half(yo, h), half(yd, h)
-                    sign(half(sg, h), mix([(I2, y1), (IN, x), (IN, y0)]))
-                    move(half(rl, h), mix([(I1, x), (I1, y0), (IN, y1)]))
-                else:
-                    sign(half(sg, h), mix([(I1, half(yd, h)), (IN, half(rl, h))]))
-            if t == 0 and o == 2 and OPT["late"]:
-                renew("G1")
-            for c in range(0, H, pw):
-                tt(ind("O", WIN, sub(ut, c // 16, pw // 16)), sub(rl, c, pw), sub(sg, c, pw), A.add)
-            y = y2
-        dm = tt("S", dlt, tt("VP", y, z, A.is_equal), A.mult)
+            a = a3 if o == 3 else odd(pair(a2, o, k))
+            ro = tt(odd(pair(rr, o, k)), a, tt("S", odd(pair(ys, o, k)), col(ns, o, k), A.add), A.min)
+            if t == 0:
+                cp(col(ur, o, k), ro)
+        if form == "P":
+            top["tag"] = "link%d" % t
+            q = knockout("link", near, False, x, [pair(ys, o) for o in range(4)], 0, 1)
+            t1, t2, d = new("W", 64), new("W", 64), new("#", 192)
+            tt(t1, q[0], q[1], A.mult)
+            tt(t2, tt("S", tt("S", q[1], q[1], A.add), q[0], A.max), q[2], A.mult)
+            for o, terms in enumerate(([(N1, q[0])], [(N2, q[1]), (K1, t1)], [(N3, q[2]), (K1, t2)])):
+                mm(col(d, o), [c16, N1, N2, N3, K1] + [b for a, b in terms], [(I1, col(c16, o))] + terms)
+            up = ts("U", d, i16, A.add)
+            ul = cp("U", tt(lid, tt("S", odd(pair(ys, 0, 3)), odd(xs), A.add), odd(pair(ys, 1, 3)), A.subtract))
+            if t == 0:
+                top["tag"] = "roots0"
+                up0 = tt(("KD", 0, 256), odd(ys), ns, A.add)
+                tt(odd(pair(rr, 0, 3)), col(up0, 0, 3), odd(a2), A.min)
+                tt(odd(pair(rr, 3)), col(up0, 3), a3, A.min)
+                cp(ur, odd(rr))
+            terms, pw = [(I1, zn)], OPT["put"]
+            for o in range(3):
+                top["tag"] = "loser%d%d" % (t, o)
+                rl, sg = gather("loser", near, col(up, o)), new("W", H)
+                for h in range(2):
+                    sign("sign", part(sg, h), mix(halves(terms + [(I1, xd[o]), (IM, rl)], h), len(terms) + 1))
+                terms = terms + [(I1, xd[o]), (IN, rl)]
+                for c in range(0, H, pw):
+                    tt(ind(tgt, sub(col(ul, o), c // 16, pw // 16)), sub(rl, c, pw), sub(sg, c, pw), A.add)
+            continue
         if t == 0:
-            renew("G2" if OPT["late"] else "G1")
-            pr = new("VP", 256)
-            for o in range(4):
-                tt(col(pr, o), col(st, o), dm, A.mult)
-            rid = tt("S", rl4, pr, A.add)
-            wnm = tt("S", col(ys, 1, 3), th, A.add)
-        else:
-            yid, pr = tt("S", dm, y, A.add), new("VP", 256)
-            for o in range(4):
-                tt(col(pr, o), col(st, o), yid, A.mult)
-            res = tt("S", a, pr, A.add)
-            dma("Y", T.yrt[:], ap(res), [res], [])
-            dma("Y", T.yrec[:], T.O[:, 0:V], [("O", 0, V)], [])
+            root(0, 1)
+        terms, uy, yd, pw, yp = [(I1, zn)], None, zn, OPT["put"], None
+        for o in range(3):
+            top["tag"] = "link%d%d" % (t, o)
+            y, cm = odd(pair(ys, o)), new("W", H)
+            tt(odd(pair(dm_, o)), y, x[o], A.subtract)
+            both = tt("S", y, x[o], A.add)
+            for h in range(2):
+                if form[o] == "S" and o == 0 and OPT["zcmp"]:
+                    above("link", part(cm, h), mix(halves([(IN, zn), (I1, xd[o])], h), 1))
+                elif form[o] == "S" and o == 0:
+                    above("link", part(cm, h), mix(halves([(IN, z), (IN, w), (I2, xd[o])], h), 2))
+                elif form[o] == "S":
+                    above("link", part(cm, h), mix(halves([(I1, xd[o]), (IN, yd)], h), 1))
+                elif o == 0:
+                    tt(part(cm, h), ind(old, part(col(ux, 0), h)), part(zn, h), A.is_gt)
+                else:
+                    tt(part(cm, h), ind(win, part(uy, h)), part(xd[o], h), A.is_lt)
+            cnt = count(cm)
+            if t == 1:
+                win = sub(near, 0, (o + 2) * H)
+                if o:
+                    tt(odd(pair(dj, o)), yp, odd(pair(jp, o)), A.subtract)
+                ts(even(pair(jp, o)), cnt, 0.5 if form[o] == "S" else 9.0, A.is_ge if o < 2 else A.is_lt)
+                yo, yp = yp, odd(pick(new("S", 128), pair(dj, o), pair(jp, o)))
+                uy = up = cp("U", yp)
+                if o < 2 and (form[o + 1] != "S" or not OPT["lin"][t][o]):
+                    up = cp("U", tt("S", tt("S", yo, odd(pair(jp, o)), A.add) if o else j2, yp, A.subtract))
+            ts(even(pair(xs, o)), cnt, 0.5 if form[o] == "S" else 9.0, A.is_ge)
+            y2 = odd(pick(pair(ys, o + 1), pair(dm_, o), pair(xs, o)))
+            if o < 2 and t == 0:
+                uy = cp("U", y2)
+            if t == 0:
+                root(o + 1, 1)
+            ul = cp("U", tt(col(lid, o), both, y2, A.subtract))
+            sg = new("W", H)
+            yd = gather("carry", win, uy) if xd[o] is None or (o < 2 and form[o + 1] == "S") else None
+            top["tag"] = "loser%d%d" % (t, o)
+            if yd and xd[o] and len(terms) == 1 and OPT["lin"][t][o]:
+                rl = new("W", H)
+                for h in range(2):
+                    move("loser", part(rl, h), mix(halves(terms + [(I1, xd[o]), (IN, yd)], h)))
+                now = [(I1, yd), (IN, rl)] if OPT["after"] else [(IN, terms[0][1]), (IN, xd[o]), (I2, yd)]
+            else:
+                rl = gather("loser", win, up if t else ul)
+                now = [(I1, yd), (IN, rl)] if yd else terms + [(I1, xd[o]), (IM, rl)]
+            terms = [(I1, yd)] if yd else terms + [(I1, xd[o]), (IN, rl)]
+            for h in range(2):
+                sign("sign", part(sg, h), mix(halves(now, h)))
+            for c in range(0, H, pw):
+                tt(ind(tgt, sub(ul, c // 16, pw // 16)), sub(rl, c, pw), sub(sg, c, pw), A.add)
+    top["tag"] = "out"
+    ro, up = new("S", 256), tt(("KD", 0, 256), odd(ys), ns, A.add)
+    tt(col(ro, 0, 3), col(up, 0, 3), odd(a2), A.min)
+    tt(col(ro, 3), col(up, 3), a3, A.min)
+    d = new("#", 256)
+    over = act("S", ro, 1.0, 1.0 - V, F.Relu)
+    mm(d, [F1, FB, ro, over], [(F1, ro), (FB, over)], 4)
+    res = act("S", d, 1.0, 0.0, F.Relu)
+    dma("S", T.yrt[:], ap(res), [res], [], R["mb"])
+    dma("Y", T.yrec[:], T.C[:, 0:V], [("C", 0, V)], [], R["mb"])
     return ops, Q
+
+
+def schedule(ops, deps, fixed):
+    lat, rest, left, users = OPT["lat"], [0.0] * len(ops), [len(d) for d in deps], [[] for d in deps]
+    for i, dd in enumerate(deps):
+        for d in dd:
+            users[d].append(i)
+    order = [i for i in range(len(ops)) if not left[i]]
+    for i in order:
+        for u in users[i]:
+            left[u] -= 1
+            if not left[u]:
+                order.append(u)
+    for i in reversed(order):
+        rest[i] = ops[i]["cost"] + max([rest[u] + lat for u in users[i]] + [0.0])
+    queue = [fixed.get(i, op["qs"]) for i, op in enumerate(ops)]
+
+    def place(weight, before):
+        busy, done, start = {q: [] for q in queue}, [0.0] * len(ops), [0.0] * len(ops)
+        for i in sorted(order, key=lambda i: -weight[i]):
+            at = max([done[d] + lat for d in before[i]] + [0.0])
+            hold, k, line = ops[i]["cost"] if ops[i]["kind"] in "cr" else 0.05, 0, busy[queue[i]]
+            for a, b in line if queue[i] else ():
+                if b > at:
+                    if at + hold <= a:
+                        break
+                    at = b
+                k += 1
+            line.insert(k, (at, at + hold))
+            start[i], done[i] = at, at + ops[i]["cost"]
+        return start, done
+    for i in reversed(order):
+        rest[i] = max([rest[i] - OPT["late"].get(ops[i]["tag"], 0)] + [rest[u] + 1e-6 for u in users[i]])
+    start, done = place(rest, deps)
+    best = (max(done), start, queue, done)
+    for k in range(OPT["turns"]):
+        start, done = place(place(done, users)[1], deps)
+        best = min(best, (max(done), start, queue, done), key=lambda x: x[0])
+    return best
+
+
+def lend(ops, start, done):
+    users, bank, last, deps = {}, {}, {b: (0.0, []) for b in POOL}, [set(op["deps"]) for op in ops]
+    for i, op in enumerate(ops):
+        for x in op["lent"]:
+            users.setdefault(x, []).append(i)
+
+    def follows(i, j, seen):
+        if i == j:
+            return True
+        seen.add(i)
+        return any(d not in seen and follows(d, j, seen) for d in deps[i] if start[d] >= start[j] or d in late)
+    late = set()
+    for x in sorted(users, key=lambda x: start[users[x][0]]):
+        b = bank[x] = [b for b in sorted(POOL, key=lambda b: last[b][0]) if not any(follows(i, users[x][0], set()) for i in last[b][1])][0]
+        late.update(i for i in last[b][1] if start[i] > start[users[x][0]])
+        deps[users[x][0]].update(last[b][1])
+        last[b] = (max(done[i] for i in users[x]), users[x])
+    return bank, deps
+
+
+def replay(order, queue, ops, deps, cost, rate):
+    done, start, why, free, last = [0.0] * len(ops), [0.0] * len(ops), [-1] * len(ops), {}, {}
+    bank, idle, left, wake, land, slow = {}, {b: (0.0, -1) for b in POOL}, {}, rate["lat"], rate["land"], rate["slow"]
+    for i in order:
+        q, op = queue[i], ops[i]
+        t, w = free.get(q, 0.0), last.get(q, -1)
+        for d in deps[i]:
+            if done[d] > t:
+                t, w = done[d], d
+        x = op["opens"]
+        if x:
+            if not idle:
+                return None
+            b = bank[x] = min(idle, key=idle.get)
+            r = idle.pop(b)
+            if r[0] > t:
+                t, w = r
+            left[x] = [op["users"], 0.0, -1]
+        k = op["kind"]
+        e = t + cost[i] + (slow if q == "S" else 0.0)
+        start[i], why[i], done[i] = t, w, e + (wake if k == "c" else land if k != "r" else 0.0)
+        if q:
+            free[q], last[q] = e if k != "d" else t + 0.05, i
+        for x in op["lent"]:
+            u = left[x]
+            u[0] -= 1
+            if done[i] > u[1]:
+                u[1], u[2] = done[i], i
+            if not u[0]:
+                idle[bank[x]] = (u[1], u[2])
+    return max(done), start, why, bank, done
+
+
+def plan(ops, costs):
+    fixed = {i: "V" if op["name"] in OPT["onv"] else "S" for i, op in enumerate(ops) if "name" in op}
+    bank, deps = lend(ops, *schedule(ops, [op["deps"] for op in ops], fixed)[1::2])
+    end, start, queue, done = schedule(ops, deps, fixed)
+    order, n = sorted(range(len(ops)), key=lambda i: (start[i], i)), len(ops)
+    deps, users, above, lent = [], [[] for op in ops], [], {}
+    for i, op in enumerate(ops):
+        m = 0
+        for d in op["deps"]:
+            m |= above[d]
+        deps.append([d for d in op["deps"] if not m >> d & 1])
+        above.append(m | sum(1 << d for d in op["deps"]))
+        for d in deps[i]:
+            users[d].append(i)
+        op["lent"], op["opens"] = sorted(set(op["lent"])), None
+        for x in op["lent"]:
+            lent.setdefault(x, []).append(i)
+    for x in lent:
+        ops[lent[x][0]].update(opens=x, users=len(lent[x]))
+
+    def judge(order, queue):
+        runs = [replay(order, queue, ops, deps, c, r) for c, r in zip(costs, RATES)]
+        return (None, None) if None in runs else (sum(x[0] for x in runs) / len(runs), runs)
+    now, runs = judge(order, queue)
+    best, seed = (now, order, queue), [OPT["seed"]]
+
+    def draw(k):
+        seed[0] = (seed[0] * 1103515245 + 12345) % 2147483648
+        return (seed[0] >> 8) % k
+    for turn in range(OPT["tries"]):
+        run = runs[draw(len(runs))]
+        i, chain = run[4].index(run[0]), []
+        while i >= 0:
+            chain.append(i)
+            i = run[2][i]
+        held = [(i, j) for i, j in zip(chain, chain[1:]) if j not in deps[i]]
+        if not held:
+            break
+        i, j = held[draw(len(held))]
+        new, side, how = list(order), queue, draw(8)
+        if how < 2 and ("name" in ops[i] or "name" in ops[j]):
+            k = i if "name" in ops[i] and ("name" not in ops[j] or how) else j
+            side = list(queue)
+            side[k] = "S" if queue[k] == "V" else "V"
+        elif how < 5:
+            a, b = new.index(j), new.index(i)
+            ahead = [k for k in new[a:b] if above[i] >> k & 1]
+            if j in ahead or a > b:
+                continue
+            new[a:b + 1] = ahead + [i] + [k for k in new[a:b] if not above[i] >> k & 1]
+        else:
+            a, b = new.index(j), new.index(i)
+            behind = [k for k in new[a + 1:b + 1] if above[k] >> j & 1]
+            if i in behind or a > b:
+                continue
+            new[a:b + 1] = [k for k in new[a + 1:b + 1] if not above[k] >> j & 1] + [j] + behind
+        t, r = judge(new, side)
+        if t is not None and t < now + OPT["heat"] * draw(1000) / 1000 * (1 - turn / OPT["tries"]):
+            st = r[0][1]
+            again = sorted(new, key=lambda i: st[i])
+            order, queue, now, runs = (again if turn % 16 == 0 and judge(again, side)[0] == t else new), side, t, r
+            if t < best[0]:
+                best = (t, order, queue)
+    now, order, queue = best
+    bank, deps, last = judge(order, queue)[1][0][3], [set(op["deps"]) for op in ops], {}
+    for i in order:
+        if ops[i]["opens"]:
+            deps[i].update(last.get(bank[ops[i]["opens"]], ()))
+            last[bank[ops[i]["opens"]]] = lent[ops[i]["opens"]]
+    return bank, deps, [(k, i, queue[i]) for k, i in enumerate(order)], now
 
 
 def rank_program(g, core, T, topo):
     if T.rank_of(core) is None:
         return
-    ops, Q = build(g, core, T, topo)
+    if "it" not in PLAN:
+        builds = [build(g, core, T, topo, {}, r)[0] for r in RATES]
+        PLAN["it"] = plan(builds[0], [[op["cost"] for op in b] for b in builds])
+    bank, deps, order, end = PLAN["it"]
+    ops, Q = build(g, core, T, topo, bank, RATES[0])
     count, seen, tok, final = {"V": 0, "S": 0, "P": 0, "G": 0}, {k: {} for k in Q}, {}, {}
-    order = [64 * ABC.index(ORDER[k]) + ABC.index(ORDER[k + 1]) for k in range(0, len(ORDER), 2)] or list(range(len(ops)))
-    place, known = {c % 1024: k for k, c in enumerate(order)}, {}
+    place, known = {i: k for k, (a, i, q) in enumerate(order)}, {}
 
     def wait(q, s, v):
         if seen[q].get(s, 0) < v:
             seen[q][s] = v
             Q[q].wait_ge(T.sem[s], v)
 
-    for code in order:
-        i = code % 1024
+    for a, i, q in order:
         op = ops[i]
         known[i] = {}
         if op["kind"] != "a":
-            q = "V" if code >= 1024 else op["qs"][0]
-            for d in sorted(op["deps"], key=lambda d: -place[d]):
+            for d in sorted(deps[i], key=lambda d: -place[d]):
                 wait(q, tok[d][0], tok[d][1])
                 for s in known[d]:
                     seen[q][s] = max(seen[q].get(s, 0), known[d][s])

@@ -5,28 +5,28 @@ WIN = V + H
 FAR = 1024.0
 MAGIC = 12582912.0
 BIG = 8192.0
-OPT = {"nh": (2, 1), "form": ("AAA", "BAB"), "meld": ("SSS", "SSS"), "send": ((512, 512), (512, 512)), "put": 512, "putz": 512, "early": 1,
-       "lin": ((0, 0), (0, 0)), "after": 1, "zcmp": 1, "held": 3, "parts": (512, 512),
-       "lat": 0.12, "turns": 1, "tries": 25000, "heat": 0.25, "seed": 1,
-       "onv": ("root.0", "first.2", "first.10", "z.0"), "late": {}}
+OPT = {"nh": (2, 1), "form": ("AAA", "BAB"), "meld": ("SLS", "SLS"), "send": ((32, 480, 512), (512, 512)), "put": 512, "putz": 256, "early": 1,
+       "lin": ((0, 0), (0, 0)), "after": 1, "zcmp": 1, "held": 3, "parts": (32, 480, 512),
+       "lat": 0.12, "turns": 1, "tries": 120000, "again": 50000, "heat": 0.3, "seed": 3, "soft": 0, "long": 9, "pp": (0, 1), "cw": 2560, "near": (1,), "two": 0, "pull": 0.2, "far": 30, "reach": 150, "whole": (),
+       "onv": ("root.0", "first.2", "first.10", "z.0", "none.0", "none.1", "none.2"), "late": {}}
 
 RATES = ({"f": 1.0, "g": 1.12, "g2": 1.45, "s": 3.3, "s2": 3.7, "pe": 0.5, "fixp": 0.02, "lat": 0.12, "land": 0.2, "slow": 0.08, "net": 2.4, "first": 1.9, "mb": 3.4},
-         {"f": 1.07, "g": 1.65, "g2": 1.9, "s": 3.6, "s2": 3.6, "pe": 0.45, "fixp": 0.0, "lat": 0.04, "land": 0.5, "slow": 0.0, "net": 1.6, "first": 2.5, "mb": 5.0},
-         {"f": 1.05, "g": 1.2, "g2": 2.2, "s": 2.6, "s2": 3.1, "pe": 0.7, "fixp": 0.0, "lat": 0.06, "land": 0.4, "slow": 0.12, "net": 3.0, "first": 1.4, "mb": 3.8})
+         {"f": 1.16, "g": 1.2, "g2": 1.2, "s": 3.27, "s2": 3.27, "pe": 0.43, "fixp": 0.002, "lat": 0.1, "land": 0.28, "slow": 0.1, "net": 2.75, "first": 1.0, "mb": 4.9},
+         {"f": 1.07, "g": 1.6, "g2": 1.8, "s": 3.0, "s2": 3.1, "pe": 0.8, "fixp": 0.0, "lat": 0.05, "land": 0.45, "slow": 0.03, "net": 2.0, "first": 2.5, "mb": 4.5})
 
 SCRATCH = {
     "A": ("sbuf", [128, WIN], "bfloat16"), "B": ("sbuf", [128, WIN], "bfloat16"), "C": ("sbuf", [128, WIN], "bfloat16"),
-    "CW": ("sbuf", [128, V], "int32"),
+    "CW": ("sbuf", [128, V], "int32"), "CN": ("sbuf", [128, 768], "int32"),
     "RT": ("sbuf", [128, 256], "int32"), "W": ("sbuf", [128, 56 * H], "bfloat16"), "KG": ("sbuf", [128, 2 * H], "float16"),
     "ZS": ("sbuf", [128, 144], "bfloat16"), "ZK": ("sbuf", [128, 3 * 144], "float16"), "BO": ("sbuf", [128, 128], "bfloat16"),
-    "ID": ("sbuf", [128, 1664], "bfloat16"), "ONE": ("sbuf", [128, 512], "bfloat16"),
+    "ID": ("sbuf", [128, 1792], "bfloat16"), "ONE": ("sbuf", [128, 512], "bfloat16"),
     "U": ("sbuf", [128, 3072], "uint16"), "I": ("sbuf", [128, 64], "int32"), "S": ("sbuf", [128, 15360], "float32"),
     "P0": ("psum", [128, 512], "float32"), "P1": ("psum", [128, 512], "float32"), "P2": ("psum", [128, 512], "float32"),
     "P3": ("psum", [128, 512], "float32"), "P4": ("psum", [128, 512], "float32"), "KD": ("psum", [128, 512], "float32"),
     "XB": ("psum", [128, 512], "float32"), "YS": ("psum", [128, 512], "float32"),
 }
 POOL = ("P0", "P1", "P2", "P3", "P4")
-SEMAPHORES = ["cV", "cS", "cP", "cG"] + ["d%d" % i for i in range(16)] + ["arr%d" % i for i in range(8)] + ["snt%d" % i for i in range(8)]
+SEMAPHORES = ["cV", "cS", "cP", "cG"] + ["d%d" % i for i in range(24)] + ["arr%d" % i for i in range(8)] + ["snt%d" % i for i in range(8)]
 PLAN = {}
 
 
@@ -40,7 +40,7 @@ def build(g, core, T, topo, bank, R):
     nxt, prv = T.cores[(rank + 1) % n], T.cores[(rank - 1) % n]
     Q = {"V": g.vector, "S": g.scalar, "P": g.tensor, "G": g, "Y": g.sync}
     ops, recs, top = [], {}, {"S": 0, "U": 0, "W": 0, "#": 0, "d": 0, "r": 0, "tag": "load"}
-    cyc = 0.83e-3 * R["f"]
+    cyc, twos = 0.83e-3 * R["f"], set()
 
     def ap(x):
         if x[0] == "ind":
@@ -56,7 +56,7 @@ def build(g, core, T, topo, bank, R):
             return 16 * wid(x[2])
         return (x[2] - x[1] + x[3] - 1) // x[3] if len(x) == 4 else x[2] - x[1]
 
-    def add(kind, qs, outs, ins, fn, cost, sem=None, cnt=1, after=()):
+    def add(kind, qs, outs, ins, fn, cost, sem=None, cnt=1, after=(), goes_on=False):
         rd, wr = [], []
         for x in ins:
             if isinstance(x, tuple):
@@ -66,14 +66,19 @@ def build(g, core, T, topo, bank, R):
                 wr.append(o[1]); rd.append(o[2])
             else:
                 wr.append(o)
-        deps, me = set(after), len(ops)
+        deps, me, hard = set(after), len(ops), set(after)
         for x, w in [(x, 0) for x in rd] + [(x, 1) for x in wr]:
             for lo, hi, w2, who in recs.get(x[0], []):
-                if (psum(x) and (ops[who]["qs"] != qs or len(qs) > 1)) or ((w or w2) and lo < x[2] and x[1] < hi):
+                meet = (w or w2) and lo < x[2] and x[1] < hi and not (OPT["soft"] and len(x) == 4 and x[3] == 2 and (who, x[0], lo, hi) in twos and (lo - x[1]) % 2)
+                if meet or x[0][0] == "#" or (psum(x) and (ops[who]["qs"] != qs or len(qs) > 1)):
                     deps.add(who)
+                if meet and not (qs == "P" and ops[who]["qs"] == "P" and goes_on):
+                    hard.add(who)
+            if len(x) == 4 and x[3] == 2:
+                twos.add((me, x[0], x[1], x[2]))
         for x, w in [(x, 0) for x in rd] + [(x, 1) for x in wr]:
             recs.setdefault(x[0], []).append((x[1], x[2], w, me))
-        ops.append({"kind": kind, "qs": qs, "deps": deps, "fn": fn, "sem": sem, "cnt": cnt, "cost": cost, "tag": top["tag"],
+        ops.append({"kind": kind, "qs": qs, "deps": deps, "soft": deps - hard, "fn": fn, "sem": sem, "cnt": cnt, "cost": cost, "tag": top["tag"],
                     "lent": [x[0] for x in rd + wr if x[0][0] == "#"]})
         return me
 
@@ -150,6 +155,15 @@ def build(g, core, T, topo, bank, R):
         either(name, o, d, lambda: g.vector.tensor_scalar(ap(o), ap(d), 0.0, 0.5, A.is_gt, A.subtract),
                lambda: g.scalar.activation(ap(o), ap(d), F.Sign, bias=-0.5))
 
+    def below(name, o, d):
+        either(name, o, d, lambda: g.vector.tensor_scalar(ap(o), ap(d), 0.0, 0.5, A.is_lt, A.subtract),
+               lambda: g.scalar.activation(ap(o), ap(d), F.Sign, bias=-0.5, scale=-1.0))
+
+    def absent(o, a):
+        o = out(o, a)
+        return either("none", o, a, lambda: g.vector.tensor_scalar(ap(o), ap(a), 0.0, None, A.is_equal),
+                      lambda: g.scalar.activation(ap(o), ap(a), F.Relu, bias=1.0, scale=-1.0))
+
     def flag(o, a):
         act(o, a, 1.0, 0.5 - V, F.Sign)
 
@@ -158,7 +172,7 @@ def build(g, core, T, topo, bank, R):
             for i, (l, r) in enumerate(terms):
                 last = g.tensor.matmul(ap(o), ap(l), ap(r), opens and i == 0, closes and i == len(terms) - 1)
             return last
-        add("c", "P", [o], whole, fn, len(terms) * (per * max(64, wid(o)) * R["pe"] * 1e-3 + R["fixp"]))
+        add("c", "P", [o], whole, fn, len(terms) * (per * max(64, wid(o)) * R["pe"] * 1e-3 + R["fixp"]), goes_on=not opens)
 
     def iota(o, pat, base, cm, after=()):
         kw = {} if o[0] in ("I", "CW") else {"allow_small_or_imprecise_dtypes": True}
@@ -197,7 +211,7 @@ def build(g, core, T, topo, bank, R):
     def odd(x):
         return (x[0], x[1] + 1, x[2], 2)
 
-    I1, IN, IM, IH, IQ, IR, I2, IB, IC, K1, N1, N2, N3 = [("ID", 128 * k, 128 * k + 128) for k in range(13)]
+    I1, IN, IM, IH, IQ, IR, I2, IB, IC, K1, N1, N2, N3, K2 = [("ID", 128 * k, 128 * k + 128) for k in range(14)]
 
     def mix(terms, early=0):
         d = new("#", wid(terms[0][1]))
@@ -211,10 +225,22 @@ def build(g, core, T, topo, bank, R):
         return [(l, part(v, h)) for l, v in terms]
 
     def gather(name, win, off, o=None):
-        o = o or new("W", H)
-        for h in range(2):
-            move(name, part(o, h), ind(win, part(off, h)))
+        o, k = o or new("W", H), 1 if top["tag"] + name in OPT["whole"] else 2
+        for h in range(k):
+            move(name, part(o, h, k), ind(win, part(off, h, k)))
         return o
+
+    def more(d, terms, opens=False, closes=False):
+        mm(d, [x for p in terms for x in p], terms, 1, opens, closes)
+
+    def total(o, terms):
+        mm(o, [x for p in terms for x in p], terms)
+        return o
+
+    def nodes(o, x):
+        d, over = new("#", wid(x)), act("S", x, 1.0, 1.0 - V, F.Relu)
+        mm(d, [F1, FB, x, over], [(F1, x), (FB, over)], 4)
+        return act(o, d, 1.0, 0.0, F.Relu)
 
     def knockout(name, rec, later, ids, chain, k, nh):
         wh, w, win = H // nh, 64 // nh, A.is_ge if later else A.is_lt
@@ -252,10 +278,12 @@ def build(g, core, T, topo, bank, R):
     dc0 = iota(new("S", 256), [[16, 2], [-1, 128]], 0, 1)
     ig = iota(new("S", 128), [[16, 8], [0, 16]], 0, 0)
     n0 = iota(new("S", 5), [[256, 5]], 0, 16)
-    iota(("CW", 0, V), [[0, V]], V, 0, range(len(ops) - 6, len(ops)))
+    iota(("CW", 0, OPT["cw"]), [[0, OPT["cw"]]], V, 0, range(len(ops) - 6, len(ops)))
+    for c in range(OPT["cw"], V, 512):
+        fill(("CW", c, c + 512), V)
+    filled = [i for lo, hi, w, i in recs["CW"]]
     for o in range(3):
-        dma("Y", T.CW[o:128:16, :], T.ch[:, o * V:(o + 1) * V], [], [("CW", 0, V)] if o == 0 else [], 2.5, [len(ops) - 1 - o])
-    recs["CW"] += [(0, V, 1, len(ops) - 1), (0, V, 1, len(ops) - 2)]
+        recs["CW"].append((0, V, 1, dma("Y", T.CW[o:128:16, :], T.ch[:, o * V:(o + 1) * V], [], [], R["mb"] - 1.5, filled)))
     ts(("I", 1, 2), ("I", 0, 1), 112, A.bitwise_and)
     ts(("I", 2, 3), ("I", 0, 1), 15, A.bitwise_and)
     c2 = cp("S", ("I", 1, 3))
@@ -267,26 +295,22 @@ def build(g, core, T, topo, bank, R):
     fill(("A", V, WIN), FAR, 0.5)
     act(("B", V, WIN), ("A", V, WIN))
     ts(("ZS", 0, 144), tz, g16, A.is_equal)
-    dc_, dm_, nb_, dp2, bw = [act(new("S", 384), ("A", V, V + 384), 0.0) for k in range(5)]
+    dc_, nb_, dp2, bw = [act(new("S", 384), ("A", V, V + 384), 0.0) for k in range(4)]
     ll = new("W", 320)
     act(col(ll, 0), ("A", V, V + 64), 0.0, -1.0)
     act(odd(dp2), col(dp, 0, 3))
     duel, fq = new("W", 6 * H), act(new("W", 384), ("A", V, V + 384), 0.0)
-    c16 = new("W", 192)
-    for o in range(3):
-        ts(col(c16, o), col(dp, 0), i16, A.subtract, float((o + 1) * H - V), A.add)
-    jp, dj = new("S", 384), act(new("S", 384), ("A", V, V + 384), 0.0)
-    for o in range(3):
-        act(odd(pair(jp, o)), col(dp, 0), 1.0, float((o + 1) * H - V))
-    act(odd(pair(dj, 0)), ("A", V, V + 64), -1.0)
-    j2 = act("S", col(dp, 0), 2.0, float(H - 2 * V))
+    c16 = new("W", 256)
+    ts(col(c16, 0), col(dp, 0), i16, A.subtract, -float(V), A.add)
+    for o in (1, 2, 3):
+        act(col(c16, o), col(c16, 0), 1.0, float(o * H))
     rows = ts("S", sub(tz, 15, 3), i16, A.is_equal, ts("S", i16, 3.0, A.is_equal), A.add)
     for o in range(3):
         ts(("ZK", 144 * o, 144 * o + 144), tz, g16, A.is_equal, sub(rows, o, 1), A.mult)
     ts(("BO", 0, 128), ig, g16, A.is_equal)
     ts(I1, sub(dc0, 0, 128), 0.0, A.is_equal)
     for x, c in ((IN, -1.0), (IM, -2.0), (IH, 0.5), (IQ, -0.25), (IR, MAGIC), (I2, 2.0), (IB, BIG / 2), (IC, -BIG / 2),
-                 (K1, 1.0 * H), (N1, -1.0 * H), (N2, -2.0 * H), (N3, -3.0 * H)):
+                 (K1, 1.0 * H), (N1, -1.0 * H), (N2, -2.0 * H), (N3, -3.0 * H), (K2, 2.0 * H)):
         act(x, I1, c)
     F1 = act(new("S", 128), I1)
     FB = act(new("S", 128), I1, -BIG)
@@ -298,7 +322,14 @@ def build(g, core, T, topo, bank, R):
     n16 = ts("S", n0, ts("S", g16, 16.0, A.mult), A.subtract)
 
     ys = ("YS", 0, 512)
-    lid = None
+    lid, held = None, [[], [], [], []]
+
+    def turn(i, writes, after):
+        free = [d for lo, hi, w, d in recs["C"] if "turn" in ops[d] and d != i]
+        ops[i]["deps"] = ops[i]["deps"].difference(free).union(after)
+        ops[i]["soft"] = ops[i]["soft"].difference(free)
+        ops[i]["turn"] = writes
+
     for t in range(2):
         old, win, tgt = ("B", "A", "C") if t == 0 else ("C", "C", "C")
         roots = [odd(pair(rr, o)) for o in range(4)]
@@ -349,28 +380,32 @@ def build(g, core, T, topo, bank, R):
             m = odd(pair(ys, 0))
         for o in (1, 2, 3) if OPT["form"][t][0] not in "PT" else ():
             form = OPT["form"][t][o - 1]
-            ex = gather("root", "A", um if form == "B" else col(ur, o))
-            mo, um2, cm = pair(ys, 0) if o == 3 else new("S", 128), new("U", 64), new("W", H)
-            if form == "S":
-                em = gather("best", "A", um)
-            for h in range(2):
+            mo, um2, cm, ex, em, lo = pair(ys, 0) if o == 3 else ("XB", 128 * o + 128, 128 * o + 256), new("U", 64), new("W", H), new("W", H), new("W", H if form == "S" else 0), 0
+            for h, k in enumerate(OPT["parts"] if nh > 1 else (512, 512)):
+                def cut(x):
+                    return sub(x, lo * wid(x) // H, k * wid(x) // H)
+                top["tag"] = "lead" if k < 256 else "champion%d" % t
+                move("root", cut(ex), ind("A", cut(um if form == "B" else col(ur, o))))
                 if form == "A":
-                    tt(part(cm, h), ind("A", part(um, h)), part(ex, h), A.is_gt)
+                    tt(cut(cm), ind("A", cut(um)), cut(ex), A.is_gt)
                 elif form == "B":
-                    tt(part(cm, h), ind("A", part(col(ur, o), h)), part(ex, h), A.is_lt)
+                    tt(cut(cm), ind("A", cut(col(ur, o))), cut(ex), A.is_lt)
                 else:
-                    above("duel", part(cm, h), mix([(I1, part(em, h)), (IN, part(ex, h))], o // 3))
-                if nh == 1 and h == 0:
-                    continue
-                k = h if nh == 2 else 0
-                tt(part(odd(pair(dc_, o - 1)), k, nh), part(m, k, nh), part(roots[o], k, nh), A.subtract)
-                ts(part(even(pair(rr, o)), k, nh), count(part(cm, k, nh)), 0.5 if form == "S" else 9.0, A.is_lt)
-                pick(part(mo, k, nh), part(pair(dc_, o - 1), k, nh), part(pair(rr, o), k, nh))
-                cp(part(um2, k, nh), part(odd(mo), k, nh))
+                    move("best", cut(em), ind("A", cut(um)))
+                    above("duel", cut(cm), mix([(I1, cut(em)), (IN, cut(ex))], o // 3))
+                if nh == 1:
+                    lo, k = (512, 0) if h == 0 else (0, H)
+                if k:
+                    tt(cut(odd(pair(dc_, o - 1))), cut(m), cut(roots[o]), A.subtract)
+                    ts(cut(even(pair(rr, o))), count(cut(cm)), 0.5 if form == "S" else 9.0, A.is_lt)
+                    pick(cut(mo), cut(pair(dc_, o - 1)), cut(pair(rr, o)))
+                    cp(cut(um2), cut(odd(mo)))
+                lo += k
             m, um = odd(mo), um2
         z, w, near, kg, lo = new("W", H), new("W", H), new("W", 4 * H), ("KG", t * H, t * H + H), 0
         zn = sub(near, 0, H)
         for k in OPT["send"][t]:
+            top["tag"] = "lead" if k < 256 else "champion%d" % t
             move("z", sub(z, lo, k), ind("A", sub(um, lo // 16, k // 16)))
             e, s = engines(topo, core, nxt), top["r"]
             top["r"] += 1
@@ -378,26 +413,29 @@ def build(g, core, T, topo, bank, R):
 
             def send(q, a=sub(w, lo, k), b=sub(z, lo, k), s=s, e=e, r_id=r_id, pid=pid):
                 g.remote_dma(ap(a), ap(b), T.sem["arr%d" % s], T.sem["snt%d" % s], pid, r_id, sum(1 << x for x in e))
-            x = add("r", "G", [], [sub(z, lo, k)], send, 0.3 + (R["first"] if s == 0 else 0), "snt%d" % s, len(e))
+            sent = x = add("r", "G", [], [sub(z, lo, k)], send, 0.3 + (R["first"] if s == 0 else 0), "snt%d" % s, len(e))
             add("a", "", [sub(w, lo, k)], [], None, R["net"] * (0.6 + 0.8 * k / H), "arr%d" % s, len(engines(topo, prv, core)), [x])
             lo += k
         top["tag"] = "kids%d" % t
         lo = 0
-        for k in OPT["parts"] if t == 0 else (512, 512):
+        two = t == 1 and OPT["two"]
+        for k in () if two else OPT["parts"] if t == 0 else (512, 512):
             ts(sub(kg, lo, k), ind("CW", sub(um, lo // 16, k // 16)), -V / 2, A.add)
             lo += k
+        if two:
+            kg = gather("kids", "B", um)
         for o in range(4):
             tt(even(pair(rr, o)), roots[o], m, A.is_equal)
-        keep = [tt("S", roots[0], m, A.not_equal), tt("S", even(pair(rr, 2)), even(pair(rr, 3)), A.add), even(pair(rr, 3))]
+        keep = [absent("S", even(pair(rr, 0))), tt("S", even(pair(rr, 2)), even(pair(rr, 3)), A.add), even(pair(rr, 3))]
         kd = ("KD", 0, 384)
         if t == 1:
-            won, mc, bw = new("S", 192), cp("S", m), new("S", 384)
+            won, mc, bw = ("XB", 0, 192), move("copy", new("S", 64), m), new("S", 384)
             for o in range(3):
                 tt(col(won, o), odd(pair(ys, o + 1)), mc, A.is_equal)
                 tt(odd(pair(nb_, o)), keep[o], col(won, o), A.is_gt)
-            tt(odd(kd), won, tt("S", ts(("KD", 0, 192), lid, float(V), A.is_lt), lid, A.mult), A.mult)
+            tt(odd(kd), nodes("S", lid), won, A.mult)
         for o in range(3):
-            kid = lists(even(pair(kd, o)), kg, ("ZK", 144 * o, 144 * o + 144))
+            kid = lists(even(pair(kd, o)), kg, sub(z2, 144 * o, 144) if two else ("ZK", 144 * o, 144 * o + 144))
             if t == 1:
                 pick(pair(bw, o), pair(nb_, o), pair(kd, o))
             else:
@@ -412,7 +450,12 @@ def build(g, core, T, topo, bank, R):
         ts(("I", i0 + 8, i0 + 13), ("I", i0, i0 + 5), 3, A.arith_shift_right, 126, A.bitwise_and)
         us = ts("U", ("I", i0 + 8, i0 + 13), 1.0, A.add)
         ts(("I", i0 + 16, i0 + 17), ("I", i0, i0 + 1), 15, A.bitwise_and)
-        pp = ts("S", dc, cp("S", ("I", i0 + 16, i0 + 17)), A.is_equal)
+        if t in OPT["pp"]:
+            gap, r = new("S", 256), ts("S", ("I", i0 + 16, i0 + 17), -1.0, A.mult)
+            add("c", "S", [gap], [dc, r], lambda q, gap=gap, r=r: g.scalar.activation(ap(gap), ap(dc), F.Abs, bias=ap(r)), span(gap, dc, 1))
+            pp = act("S", gap, -1.0, 1.0, F.Relu)
+        else:
+            pp = ts("S", dc, cp("S", ("I", i0 + 16, i0 + 17)), A.is_equal)
         xs, ux = new("S", 384), new("U", 192)
         for o in range(3):
             g1 = move("shift", new("S", 80), ("ind", pair(bw, o), us))
@@ -420,7 +463,7 @@ def build(g, core, T, topo, bank, R):
             if o == 1:
                 continue
             a, k = (0, 1) if o == 0 else (1, 2)
-            ts(odd(pair(nb_, a, k)), odd(pair(xb, a, k)), 0.0, A.is_equal)
+            absent(odd(pair(nb_, a, k)), odd(pair(xb, a, k)))
             pick(pair(xs, a, k), pair(nb_, a, k), pair(xb, a, k))
             if o == 0:
                 cp(col(ux, 0), odd(pair(xs, 0)))
@@ -428,7 +471,7 @@ def build(g, core, T, topo, bank, R):
         for o in range(3):
             flag(col(ll, o + 1), x[o])
             if o < 2:
-                cp(col(ux, o + 1), tt(x[o + 1], x[o + 1], tt("S", col(ll, o + 1), x[o], A.mult), A.max))
+                cp(col(ux, o + 1), tt(x[o + 1], x[o + 1], tt(("KD", 384, 448), col(ll, o + 1), x[o], A.mult), A.max))
         top["tag"] = "mean%d" % t
         for lo, k in ((0, 512), (512, 512)):
             one, zp = ("ONE", 0, k), sub(zn, lo, k)
@@ -439,17 +482,40 @@ def build(g, core, T, topo, bank, R):
         for o in range(3):
             top["tag"] = "first%d%d" % (t, o)
             xd.append(gather("first", old, col(ux, o), sub(near, H + o * H, H)) if o or form[0] != "A" else None)
+            for i in range(len(ops) - 2, len(ops)) if t == 1 else ():
+                turn(i, 0, held[o])
+        if t == 0 and OPT["two"]:
+            top["tag"] = "pieces"
+            for o in range(3):
+                dma("Y", T.CN[:, o * 256:(o + 1) * 256], T.ch[:, o * V:(o + 1) * V], [], [("CN", o * 256, o * 256 + 256)], 2.2, [sent])
+            z2, hl, whole = new("W", 432), new("W", 1536), cp("S", ("CN", 0, 768))
+            row2 = ts("S", sub(tz, 15, 3), cp("S", ts(("I", 3, 4), ("I", 0, 1), 1, A.arith_shift_right, 7, A.bitwise_and)), A.is_equal)
+            for o in range(3):
+                add("c", "S", [sub(z2, 144 * o, 144)], [("ZS", 0, 144), row2], lambda q, o=o: g.scalar.activation(
+                    ap(sub(z2, 144 * o, 144)), ap(("ZS", 0, 144)), F.Identity, scale=ap(sub(row2, o, 1))), span(("ZS", 0, 144), ("ZS", 0, 144), 1))
+            act(part(hl, 0), whole)
+            for h in range(2):
+                d = new("#", 384)
+                mm(d, [F1, whole], [(F1, part(whole, h))], 4, True, False)
+                mm(d, [IN, hl], [(IN, part(part(hl, 0), h))], 1, False, True)
+                act(part(part(hl, 1), h), d)
+            rows2 = [dma("Y", T.B[k:128:16, 0:V], ap(sub(hl, k % 2 * 768 + k // 2 * 256, 256)), [sub(hl, k % 2 * 768 + k // 2 * 256, 256)], [], 2.2,
+                         [i for lo, hi, w, i in recs["B"]]) for k in range(6)]
+            recs["B"] += [(0, V, 1, i) for i in rows2]
         top["tag"] = "put%d" % t
         pw = OPT["putz"]
         for c in range(0, H, pw):
             cp(ind(win, sub(um, c // 16, pw // 16)), sub(zn, c, pw))
+            if t == 1:
+                turn(len(ops) - 1, 1, [])
+                held[3].append(len(ops) - 1)
         if t == 0:
             renew(tgt, win, WIN)
         top["tag"] = "roots%d" % t
         flag(col(ll, 4), a3)
         ns = act("S", mix([(IB, col(ll, 0, 4)), (IC, col(ll, 1, 4))]), 1.0, BIG)
         tt(("XB", 1, 384, 2), even(xb), odd(xs), A.is_equal)
-        a2 = pick(new("S", 384), dp2, ("XB", 1, 385), A.max)
+        a2 = pick(kd if t == 0 else new("S", 384), dp2, ("XB", 1, 385), A.max)
         rr, ur, lid = new("S", 512), new("U", 256), new("S", 192)
 
         def root(o, k):
@@ -464,7 +530,7 @@ def build(g, core, T, topo, bank, R):
             tt(t1, q[0], q[1], A.mult)
             tt(t2, tt("S", tt("S", q[1], q[1], A.add), q[0], A.max), q[2], A.mult)
             for o, terms in enumerate(([(N1, q[0])], [(N2, q[1]), (K1, t1)], [(N3, q[2]), (K1, t2)])):
-                mm(col(d, o), [c16, N1, N2, N3, K1] + [b for a, b in terms], [(I1, col(c16, o))] + terms)
+                mm(col(d, o), [c16, N1, N2, N3, K1] + [b for a, b in terms], [(I1, col(c16, o + 1))] + terms)
             up = ts("U", d, i16, A.add)
             ul = cp("U", tt(lid, tt("S", odd(pair(ys, 0, 3)), odd(xs), A.add), odd(pair(ys, 1, 3)), A.subtract))
             if t == 0:
@@ -486,35 +552,66 @@ def build(g, core, T, topo, bank, R):
         if t == 0:
             root(0, 1)
         terms, uy, yd, pw, yp = [(I1, zn)], None, zn, OPT["put"], None
+        q, run, rls, sgs, uls = [None] * 3, [None] * 2, [], [], []
+        qq, far3 = new("W", 64), ("KD", 384, 512)
         for o in range(3):
             top["tag"] = "link%d%d" % (t, o)
             y, cm = odd(pair(ys, o)), new("W", H)
-            tt(odd(pair(dm_, o)), y, x[o], A.subtract)
             both = tt("S", y, x[o], A.add)
+            tt(even(pair(ys, o)), x[o], y, A.subtract)
             for h in range(2):
-                if form[o] == "S" and o == 0 and OPT["zcmp"]:
+                if form[o] == "R":
+                    if o == 0:
+                        run[h] = new("#", 512)
+                        more(run[h], halves([(I1, zn)], h), True)
+                        more(run[h], halves([(IN, xd[0])], h))
+                    elif o == 1:
+                        more(run[h], halves([(I2, xd[0]), (IN, xd[1])], h))
+                        more(run[h], halves([(IN, rls[0])], h))
+                    else:
+                        more(run[h], halves([(I1, rls[0]), (I1, xd[1]), (IN, xd[2])], h))
+                        more(run[h], halves([(IN, rls[1])], h))
+                    below("link", part(cm, h), run[h])
+                    if o:
+                        top["tag"] = "loser%d%d" % (t, o - 1)
+                        more(run[h], halves([(I1, xd[o]), (IN, rls[o - 1])], h))
+                        sign("sign", part(sgs[o - 1], h), run[h])
+                        top["tag"] = "link%d%d" % (t, o)
+                elif form[o] == "S" and o == 0 and OPT["zcmp"]:
                     above("link", part(cm, h), mix(halves([(IN, zn), (I1, xd[o])], h), 1))
                 elif form[o] == "S" and o == 0:
                     above("link", part(cm, h), mix(halves([(IN, z), (IN, w), (I2, xd[o])], h), 2))
                 elif form[o] == "S":
                     above("link", part(cm, h), mix(halves([(I1, xd[o]), (IN, yd)], h), 1))
+                elif form[o] == "L":
+                    above("link", part(cm, h), mix(halves([(I1, xd[o])] + [(IN if l == I1 else I1, v) for l, v in terms], h), len(terms)))
                 elif o == 0:
                     tt(part(cm, h), ind(old, part(col(ux, 0), h)), part(zn, h), A.is_gt)
                 else:
                     tt(part(cm, h), ind(win, part(uy, h)), part(xd[o], h), A.is_lt)
-            cnt = count(cm)
-            if t == 1:
-                win = sub(near, 0, (o + 2) * H)
-                if o:
-                    tt(odd(pair(dj, o)), yp, odd(pair(jp, o)), A.subtract)
-                ts(even(pair(jp, o)), cnt, 0.5 if form[o] == "S" else 9.0, A.is_ge if o < 2 else A.is_lt)
-                yo, yp = yp, odd(pick(new("S", 128), pair(dj, o), pair(jp, o)))
-                uy = up = cp("U", yp)
-                if o < 2 and (form[o + 1] != "S" or not OPT["lin"][t][o]):
-                    up = cp("U", tt("S", tt("S", yo, odd(pair(jp, o)), A.add) if o else j2, yp, A.subtract))
-            ts(even(pair(xs, o)), cnt, 0.5 if form[o] == "S" else 9.0, A.is_ge)
-            y2 = odd(pick(pair(ys, o + 1), pair(dm_, o), pair(xs, o)))
-            if o < 2 and t == 0:
+            q[o] = ts(odd(pair(fq, o)), count(cm), 9.0 if form[o] == "A" else 0.5, A.is_lt)
+            if t in OPT["near"]:
+                win, d = sub(near, 0, (o + 2) * H), new("#", 128)
+                if o < 2 and form[o + 1] in "LR":
+                    d = total(col(d, 0), [(I1, col(c16, o + 1))] + ([(N2, q[1]), (K1, tt(qq, q[0], q[1], A.mult))] if o else [(N1, q[0])]))
+                    if o:
+                        total(even(far3), [(N3, ("ONE", 0, 64)), (K1, q[0]), (K2, q[1]), (N1, qq)])
+                        total(odd(far3), [(I1, col(c16, 3))])
+                elif o == 0:
+                    total(col(d, 0), [(I1, col(c16, 0)), (K1, q[0])])
+                    total(col(d, 1), [(I1, col(c16, 1)), (N1, q[0])])
+                elif o == 1:
+                    tt(qq, q[0], q[1], A.mult)
+                    total(col(d, 0), [(I1, col(c16, 0)), (K1, q[0]), (K2, q[1]), (N1, qq)])
+                    total(col(d, 1), [(I1, col(c16, 2)), (N2, q[1]), (K1, qq)])
+                    total(even(far3), [(N3, ("ONE", 0, 64)), (K1, q[0]), (K2, q[1]), (N1, qq)])
+                    total(odd(far3), [(I1, col(c16, 3))])
+                else:
+                    d = odd(pick(new("S", 128), pair(fq, 2), far3))
+                uy = ts("U", d, i16, A.add)
+                uy, up = col(uy, 0), col(uy, wid(uy) > 64)
+            y2 = odd(pick(pair(ys, o + 1), pair(fq, o), pair(ys, o)))
+            if o < 2 and t not in OPT["near"] and form[o + 1] not in "LR":
                 uy = cp("U", y2)
             if t == 0:
                 root(o + 1, 1)
@@ -528,23 +625,31 @@ def build(g, core, T, topo, bank, R):
                     move("loser", part(rl, h), mix(halves(terms + [(I1, xd[o]), (IN, yd)], h)))
                 now = [(I1, yd), (IN, rl)] if OPT["after"] else [(IN, terms[0][1]), (IN, xd[o]), (I2, yd)]
             else:
-                rl = gather("loser", win, up if t else ul)
+                rl = gather("loser", win, up if t in OPT["near"] else ul)
                 now = [(I1, yd), (IN, rl)] if yd else terms + [(I1, xd[o]), (IM, rl)]
             terms = [(I1, yd)] if yd else terms + [(I1, xd[o]), (IN, rl)]
+            rls.append(rl); sgs.append(sg); uls.append(ul)
             for h in range(2):
-                sign("sign", part(sg, h), mix(halves(now, h)))
-            for c in range(0, H, pw):
-                tt(ind(tgt, sub(ul, c // 16, pw // 16)), sub(rl, c, pw), sub(sg, c, pw), A.add)
+                if form[o] != "R":
+                    sign("sign", part(sg, h), mix(halves(now, h), len(now) - 1 if len(now) > OPT["long"] else 0))
+                elif o == 2:
+                    more(run[h], halves([(I1, rls[1]), (I1, xd[2])], h))
+                    more(run[h], halves([(IM, rl)], h), False, True)
+                    sign("sign", part(sg, h), run[h])
+            for k in (o,) if form[o] != "R" else () if o == 0 else (0,) if o == 1 else (1, 2):
+                top["tag"] = "loser%d%d" % (t, k)
+                for c in range(0, H, pw):
+                    tt(ind("C", sub(uls[k], c // 16, pw // 16)), sub(rls[k], c, pw), sub(sgs[k], c, pw), A.add)
+                    turn(len(ops) - 1, 1, held[3])
+                    held[k].append(len(ops) - 1)
     top["tag"] = "out"
     ro, up = new("S", 256), tt(("KD", 0, 256), odd(ys), ns, A.add)
     tt(col(ro, 0, 3), col(up, 0, 3), odd(a2), A.min)
     tt(col(ro, 3), col(up, 3), a3, A.min)
-    d = new("#", 256)
-    over = act("S", ro, 1.0, 1.0 - V, F.Relu)
-    mm(d, [F1, FB, ro, over], [(F1, ro), (FB, over)], 4)
-    res = act("S", d, 1.0, 0.0, F.Relu)
-    dma("S", T.yrt[:], ap(res), [res], [], R["mb"])
+    res = nodes("S", ro)
+    dma("S", T.yrt[:], ap(res), [res], [], R["mb"] - 1.6)
     dma("Y", T.yrec[:], T.C[:, 0:V], [("C", 0, V)], [], R["mb"])
+    PLAN["top"] = top
     return ops, Q
 
 
@@ -607,71 +712,96 @@ def lend(ops, start, done):
     return bank, deps
 
 
-def replay(order, queue, ops, deps, cost, rate):
-    done, start, why, free, last = [0.0] * len(ops), [0.0] * len(ops), [-1] * len(ops), {}, {}
-    bank, idle, left, wake, land, slow = {}, {b: (0.0, -1) for b in POOL}, {}, rate["lat"], rate["land"], rate["slow"]
+def links(order, queue, ops, deps):
+    steps, last, bank, idle, left, wrote, read = [], {}, {}, [(b, ()) for b in POOL], {}, [], []
     for i in order:
-        q, op = queue[i], ops[i]
-        t, w = free.get(q, 0.0), last.get(q, -1)
-        for d in deps[i]:
-            if done[d] > t:
-                t, w = done[d], d
-        x = op["opens"]
-        if x:
+        q, (hard, soft, turn, opens, lent) = queue[i], deps[i]
+        if soft:
+            hard = hard + [d for d in soft if queue[d] != q]
+        if turn:
+            hard = hard + (wrote + read if turn > 1 else wrote)
+            if turn > 1:
+                wrote, read = [i], []
+            else:
+                read.append(i)
+        if opens:
             if not idle:
                 return None
-            b = bank[x] = min(idle, key=idle.get)
-            r = idle.pop(b)
-            if r[0] > t:
-                t, w = r
-            left[x] = [op["users"], 0.0, -1]
-        k = op["kind"]
-        e = t + cost[i] + (slow if q == "S" else 0.0)
-        start[i], why[i], done[i] = t, w, e + (wake if k == "c" else land if k != "r" else 0.0)
+            bank[opens[0]], users = idle.pop(0)
+            hard = hard + list(users)
+            left[opens[0]] = len(opens[1])
+        for x, users in lent:
+            left[x] -= 1
+            if not left[x]:
+                idle.append((bank[x], users))
+        steps.append((i, last.get(q, -1), hard))
         if q:
-            free[q], last[q] = e if k != "d" else t + 0.05, i
-        for x in op["lent"]:
-            u = left[x]
-            u[0] -= 1
-            if done[i] > u[1]:
-                u[1], u[2] = done[i], i
-            if not u[0]:
-                idle[bank[x]] = (u[1], u[2])
-    return max(done), start, why, bank, done
+            last[q] = i
+    return steps, bank
+
+
+def replay(steps, queue, hold, tail, slow):
+    n = len(hold)
+    done, free, start, why = [0.0] * n, [0.0] * (n + 1), [0.0] * n, [-1] * n
+    for i, w, hard in steps:
+        t = free[w]
+        for d in hard:
+            if done[d] > t:
+                t, w = done[d], d
+        start[i], why[i] = t, w
+        free[i] = t = t + hold[i] + (slow if queue[i] == "S" else 0.0)
+        done[i] = t + tail[i]
+    return max(done), start, why, done
 
 
 def plan(ops, costs):
     fixed = {i: "V" if op["name"] in OPT["onv"] else "S" for i, op in enumerate(ops) if "name" in op}
-    bank, deps = lend(ops, *schedule(ops, [op["deps"] for op in ops], fixed)[1::2])
-    end, start, queue, done = schedule(ops, deps, fixed)
+    turns = [i for i, op in enumerate(ops) if "turn" in op]
+    inline = {j: [i for i in turns if i < j and (ops[i]["turn"] or ops[j]["turn"])] for j in turns}
+    bank, deps = lend(ops, *schedule(ops, [op["deps"].union(inline.get(i, ())) for i, op in enumerate(ops)], fixed)[1::2])
+    end, start, queue, done = schedule(ops, [d.union(inline.get(i, ())) for i, d in enumerate(deps)], fixed)
     order, n = sorted(range(len(ops)), key=lambda i: (start[i], i)), len(ops)
-    deps, users, above, lent = [], [[] for op in ops], [], {}
+    deps, users, above, sure, lent = [], [[] for op in ops], [], [], {}
     for i, op in enumerate(ops):
-        m = 0
+        m = k = 0
         for d in op["deps"]:
             m |= above[d]
-        deps.append([d for d in op["deps"] if not m >> d & 1])
+            k |= 0 if d in op["soft"] else sure[d]
+        deps.append([d for d in op["deps"] if not k >> d & 1])
         above.append(m | sum(1 << d for d in op["deps"]))
+        sure.append(k | sum(1 << d for d in op["deps"] - op["soft"]))
         for d in deps[i]:
             users[d].append(i)
         op["lent"], op["opens"] = sorted(set(op["lent"])), None
         for x in op["lent"]:
             lent.setdefault(x, []).append(i)
     for x in lent:
-        ops[lent[x][0]].update(opens=x, users=len(lent[x]))
+        ops[lent[x][0]]["opens"] = x
+    rule = [([d for d in deps[i] if d not in op["soft"]], [d for d in deps[i] if d in op["soft"]], op.get("turn", -1) + 1,
+             op["opens"] and (op["opens"], lent[op["opens"]]), [(x, lent[x]) for x in op["lent"]]) for i, op in enumerate(ops)]
+    holds = [[c if op["kind"] in "cr" else 0.05 if op["kind"] == "d" else 0.0 for op, c in zip(ops, cost)] for cost in costs]
+    tails = [[r["lat"] if op["kind"] == "c" else 0.0 if op["kind"] == "r" else c + r["land"] for op, c in zip(ops, cost)] for cost, r in zip(costs, RATES)]
 
-    def judge(order, queue):
-        runs = [replay(order, queue, ops, deps, c, r) for c, r in zip(costs, RATES)]
-        return (None, None) if None in runs else (sum(x[0] for x in runs) / len(runs), runs)
+    def judge(order, queue, limit=None):
+        steps, runs = links(order, queue, ops, rule), []
+        for k in range(len(RATES)) if steps else ():
+            runs.append(replay(steps[0], queue, holds[k], tails[k], RATES[k]["slow"]))
+            if limit and runs[k][0] > limit[k][0] + 1.0:
+                return None, None
+        return (sum(x[0] + OPT["pull"] * sum(x[3]) / n for x in runs) / len(runs), runs) if steps else (None, None)
     now, runs = judge(order, queue)
-    best, seed = (now, order, queue), [OPT["seed"]]
+    best, seed, named = (now, order, queue), [OPT["seed"]], sorted(fixed)
 
     def draw(k):
         seed[0] = (seed[0] * 1103515245 + 12345) % 2147483648
         return (seed[0] >> 8) % k
-    for turn in range(OPT["tries"]):
+    for turn in range(OPT["tries"] + OPT["again"]):
+        if turn == OPT["tries"]:
+            now, order, queue = best
+            runs = judge(order, queue)[1]
+        heat = OPT["heat"] * (1 - turn / OPT["tries"]) if turn < OPT["tries"] else 0.12 * (1 - (turn - OPT["tries"]) / OPT["again"])
         run = runs[draw(len(runs))]
-        i, chain = run[4].index(run[0]), []
+        i, chain = run[3].index(run[0]), []
         while i >= 0:
             chain.append(i)
             i = run[2][i]
@@ -680,6 +810,14 @@ def plan(ops, costs):
             break
         i, j = held[draw(len(held))]
         new, side, how = list(order), queue, draw(8)
+        if draw(100) < OPT["far"]:
+            b, k = new.index(i), 1 + draw(OPT["reach"])
+            i, j = (i, new[max(0, b - k)]) if how < 5 else (new[min(n - 1, b + k)], j)
+            if draw(2):
+                k = named[draw(len(named))]
+                side = list(queue)
+                side[k] = "S" if queue[k] == "V" else "V"
+            how = max(how, 2)
         if how < 2 and ("name" in ops[i] or "name" in ops[j]):
             k = i if "name" in ops[i] and ("name" not in ops[j] or how) else j
             side = list(queue)
@@ -696,16 +834,25 @@ def plan(ops, costs):
             if i in behind or a > b:
                 continue
             new[a:b + 1] = [k for k in new[a + 1:b + 1] if not above[k] >> j & 1] + [j] + behind
-        t, r = judge(new, side)
-        if t is not None and t < now + OPT["heat"] * draw(1000) / 1000 * (1 - turn / OPT["tries"]):
-            st = r[0][1]
-            again = sorted(new, key=lambda i: st[i])
-            order, queue, now, runs = (again if turn % 16 == 0 and judge(again, side)[0] == t else new), side, t, r
-            if t < best[0]:
-                best = (t, order, queue)
+        t, r = judge(new, side, runs)
+        if t is not None and t < now + (OPT["heat"] * draw(1000) / 1000 * (1 - turn / OPT["tries"]) if turn < OPT["tries"] else heat * draw(1000) / 1000):
+            order, queue, now, runs = new, side, t, r
+            if turn % 8 == 0:
+                again = sorted(new, key=lambda k: r[0][1][k])
+                t, r = judge(again, side)
+                if t is not None and t <= now + 0.02:
+                    order, now, runs = again, t, r
+            if now < best[0]:
+                best = (now, order, queue)
     now, order, queue = best
-    bank, deps, last = judge(order, queue)[1][0][3], [set(op["deps"]) for op in ops], {}
+    now = sum(x[0] for x in judge(order, queue)[1]) / len(RATES)
+    PLAN["dbg"] = (ops, judge(order, queue)[1], queue, deps, costs)
+    bank, deps, last = links(order, queue, ops, rule)[1], [set(op["deps"]) for op in ops], {}
+    turns = []
     for i in order:
+        if "turn" in ops[i]:
+            deps[i].update(d for d in turns if ops[i]["turn"] or ops[d]["turn"])
+            turns.append(i)
         if ops[i]["opens"]:
             deps[i].update(last.get(bank[ops[i]["opens"]], ()))
             last[bank[ops[i]["opens"]]] = lent[ops[i]["opens"]]
@@ -733,6 +880,8 @@ def rank_program(g, core, T, topo):
         known[i] = {}
         if op["kind"] != "a":
             for d in sorted(deps[i], key=lambda d: -place[d]):
+                if order[place[d]][2] == q and d in op["soft"]:
+                    continue
                 wait(q, tok[d][0], tok[d][1])
                 for s in known[d]:
                     seen[q][s] = max(seen[q].get(s, 0), known[d][s])

from concourse.mybir import AluOpType as A, ActivationFunctionType as F

V, H = 4096, 1024
WIN = V + H
FAR = 1024.0
MAGIC = 12582912.0
BIG = 8192.0
OPT = {"nh": (2, 1), "form": ("AAA", "BAB"), "meld": ("SLS", "SLS"), "send": ((32, 480, 512), (512, 512)), "put": 512, "putz": 256, "early": 1,
       "lin": ((0, 0), (0, 0)), "after": 1, "zcmp": 1, "held": 3, "parts": (32, 480, 512),
       "lat": 0.12, "turns": 1, "tries": 120000, "again": 50000, "heat": 0.3, "seed": 3, "soft": 0, "long": 9, "pp": (0, 1), "cw": 2560, "near": (1,), "two": 0, "pull": 0.2, "far": 30, "reach": 150, "whole": (),
       "onv": ("root.0", "first.2", "first.10", "z.0", "none.0", "none.1", "none.2"), "late": {}}

RATES = ({"f": 1.0, "g": 1.12, "g2": 1.45, "s": 3.3, "s2": 3.7, "pe": 0.5, "fixp": 0.02, "lat": 0.12, "land": 0.2, "slow": 0.08, "net": 2.4, "first": 1.9, "mb": 3.4},
         {"f": 1.16, "g": 1.2, "g2": 1.2, "s": 3.27, "s2": 3.27, "pe": 0.43, "fixp": 0.002, "lat": 0.1, "land": 0.28, "slow": 0.1, "net": 2.75, "first": 1.0, "mb": 4.9},
         {"f": 1.07, "g": 1.6, "g2": 1.8, "s": 3.0, "s2": 3.1, "pe": 0.8, "fixp": 0.0, "lat": 0.05, "land": 0.45, "slow": 0.03, "net": 2.0, "first": 2.5, "mb": 4.5})

SCRATCH = {
    "A": ("sbuf", [128, WIN], "bfloat16"), "B": ("sbuf", [128, WIN], "bfloat16"), "C": ("sbuf", [128, WIN], "bfloat16"),
    "CW": ("sbuf", [128, V], "int32"), "CN": ("sbuf", [128, 768], "int32"),
    "RT": ("sbuf", [128, 256], "int32"), "W": ("sbuf", [128, 56 * H], "bfloat16"), "KG": ("sbuf", [128, 2 * H], "float16"),
    "ZS": ("sbuf", [128, 144], "bfloat16"), "ZK": ("sbuf", [128, 3 * 144], "float16"), "BO": ("sbuf", [128, 128], "bfloat16"),
    "ID": ("sbuf", [128, 1792], "bfloat16"), "ONE": ("sbuf", [128, 512], "bfloat16"),
    "U": ("sbuf", [128, 3072], "uint16"), "I": ("sbuf", [128, 64], "int32"), "S": ("sbuf", [128, 15360], "float32"),
    "P0": ("psum", [128, 512], "float32"), "P1": ("psum", [128, 512], "float32"), "P2": ("psum", [128, 512], "float32"),
    "P3": ("psum", [128, 512], "float32"), "P4": ("psum", [128, 512], "float32"), "KD": ("psum", [128, 512], "float32"),
    "XB": ("psum", [128, 512], "float32"), "YS": ("psum", [128, 512], "float32"),
}
POOL = ("P0", "P1", "P2", "P3", "P4")
SEMAPHORES = ["cV", "cS", "cP", "cG"] + ["d%d" % i for i in range(24)] + ["arr%d" % i for i in range(8)] + ["snt%d" % i for i in range(8)]
PLAN = {}


def engines(topo, a, b):
    e = topo.engines(a, b)
    return e[::max(1, len(e) // 8)]


def build(g, core, T, topo, bank, R):
    rank, n = T.rank_of(core), len(T.cores)
    nxt, prv = T.cores[(rank + 1) % n], T.cores[(rank - 1) % n]
    Q = {"V": g.vector, "S": g.scalar, "P": g.tensor, "G": g, "Y": g.sync}
    ops, recs, top = [], {}, {"S": 0, "U": 0, "W": 0, "#": 0, "d": 0, "r": 0, "tag": "load"}
    cyc, twos = 0.83e-3 * R["f"], set()

    def ap(x):
        if x[0] == "ind":
            return ap(x[1]).indirect(ap(x[2]))
        b = T[bank.get(x[0], x[0])]
        return b[:, x[1]:x[2]:x[3]] if len(x) == 4 else b[:, x[1]:x[2]]

    def psum(x):
        return x[0][0] == "#" or x[0] in ("KD", "XB", "YS")

    def wid(x):
        if x[0] == "ind":
            return 16 * wid(x[2])
        return (x[2] - x[1] + x[3] - 1) // x[3] if len(x) == 4 else x[2] - x[1]

    def add(kind, qs, outs, ins, fn, cost, sem=None, cnt=1, after=(), goes_on=False):
        rd, wr = [], []
        for x in ins:
            if isinstance(x, tuple):
                rd += [x[1], x[2]] if x[0] == "ind" else [x]
        for o in outs:
            if o[0] == "ind":
                wr.append(o[1]); rd.append(o[2])
            else:
                wr.append(o)
        deps, me, hard = set(after), len(ops), set(after)
        for x, w in [(x, 0) for x in rd] + [(x, 1) for x in wr]:
            for lo, hi, w2, who in recs.get(x[0], []):
                meet = (w or w2) and lo < x[2] and x[1] < hi and not (OPT["soft"] and len(x) == 4 and x[3] == 2 and (who, x[0], lo, hi) in twos and (lo - x[1]) % 2)
                if meet or x[0][0] == "#" or (psum(x) and (ops[who]["qs"] != qs or len(qs) > 1)):
                    deps.add(who)
                if meet and not (qs == "P" and ops[who]["qs"] == "P" and goes_on):
                    hard.add(who)
            if len(x) == 4 and x[3] == 2:
                twos.add((me, x[0], x[1], x[2]))
        for x, w in [(x, 0) for x in rd] + [(x, 1) for x in wr]:
            recs.setdefault(x[0], []).append((x[1], x[2], w, me))
        ops.append({"kind": kind, "qs": qs, "deps": deps, "soft": deps - hard, "fn": fn, "sem": sem, "cnt": cnt, "cost": cost, "tag": top["tag"],
                    "lent": [x[0] for x in rd + wr if x[0][0] == "#"]})
        return me

    def span(o, a, per, two=False):
        if o[0] == "ind":
            return 0.05 + wid(o) * R["s2" if two else "s"] * cyc
        if a[0] == "ind":
            return 0.055 + wid(o) * R["g2" if two else "g"] * cyc
        return 0.005 + max(64, wid(o) * per) * cyc

    def new(buf, w):
        lo = top[buf]
        if buf == "#":
            top[buf] += 1
            return ("#%d" % lo, 0, w)
        top[buf] = lo + (w + 15) // 16 * 16
        return (buf, lo, lo + w)

    def sub(x, lo, w):
        if len(x) == 4:
            return (x[0], x[1] + lo * x[3], x[1] + (lo + w - 1) * x[3] + 1, x[3])
        return (x[0], x[1] + lo, x[1] + lo + w)

    def val(x):
        return ap(x) if isinstance(x, tuple) else x

    def out(o, like):
        return new(o, wid(like)) if isinstance(o, str) else o

    def tt(o, a, b, op):
        o = out(o, b)
        add("c", "V", [o], [a, b], lambda q: g.vector.tensor_tensor(ap(o), ap(a), ap(b), op), span(o, a, 1 if psum(a) or psum(b) else 2, True))
        return o

    def ts(o, a, s1, op0, s2=None, op1=None):
        o = out(o, a)
        if op1 is None:
            add("c", "V", [o], [a, s1], lambda q: g.vector.tensor_scalar(ap(o), ap(a), val(s1), None, op0), span(o, a, 1))
        else:
            add("c", "V", [o], [a, s1, s2], lambda q: g.vector.tensor_scalar(ap(o), ap(a), val(s1), val(s2), op0, op1), span(o, a, 1))
        return o

    def cp(o, a):
        o = out(o, a)
        add("c", "V", [o], [a], lambda q: g.vector.tensor_copy(ap(o), ap(a)), span(o, a, 1))
        return o

    def pick(o, d0, d1, op=A.add):
        add("c", "V", [o], [d0, d1], lambda q: g.vector.tensor_tensor_scan(ap(o), ap(d0), ap(d1), 0.0, A.mult, op), span(o, d0, 1))
        return o

    def fill(o, c, per=1):
        return add("c", "V", [o], [], lambda q: g.vector.memset(ap(o), c), span(o, o, per))

    def act(o, a, scale=1.0, bias=0.0, f=F.Identity):
        o = out(o, a)
        add("c", "S", [o], [a], lambda q: g.scalar.activation(ap(o), ap(a), f, bias=bias, scale=scale), span(o, a, 1))
        return o

    def either(name, o, a, fv, fs):
        name = "%s.%d" % (name, len([x for x in ops if x.get("name", "").startswith(name + ".")]))
        i = add("c", "SV", [o], [a], lambda q: fv() if q == "V" else fs(), span(o, a, 1))
        ops[i]["name"] = name
        return o

    def move(name, o, a):
        return either(name, o, a, lambda: g.vector.tensor_copy(ap(o), ap(a)), lambda: g.scalar.activation(ap(o), ap(a), F.Copy))

    def sign(name, o, a):
        return either(name, o, a, lambda: g.vector.tensor_scalar(ap(o), ap(a), -1.0, 1.0, A.max, A.min),
                      lambda: g.scalar.activation(ap(o), ap(a), F.Sign))

    def above(name, o, d):
        either(name, o, d, lambda: g.vector.tensor_scalar(ap(o), ap(d), 0.0, 0.5, A.is_gt, A.subtract),
               lambda: g.scalar.activation(ap(o), ap(d), F.Sign, bias=-0.5))

    def below(name, o, d):
        either(name, o, d, lambda: g.vector.tensor_scalar(ap(o), ap(d), 0.0, 0.5, A.is_lt, A.subtract),
               lambda: g.scalar.activation(ap(o), ap(d), F.Sign, bias=-0.5, scale=-1.0))

    def absent(o, a):
        o = out(o, a)
        return either("none", o, a, lambda: g.vector.tensor_scalar(ap(o), ap(a), 0.0, None, A.is_equal),
                      lambda: g.scalar.activation(ap(o), ap(a), F.Relu, bias=1.0, scale=-1.0))

    def flag(o, a):
        act(o, a, 1.0, 0.5 - V, F.Sign)

    def mm(o, whole, terms, per=1, opens=True, closes=True):
        def fn(q):
            for i, (l, r) in enumerate(terms):
                last = g.tensor.matmul(ap(o), ap(l), ap(r), opens and i == 0, closes and i == len(terms) - 1)
            return last
        add("c", "P", [o], whole, fn, len(terms) * (per * max(64, wid(o)) * R["pe"] * 1e-3 + R["fixp"]), goes_on=not opens)

    def iota(o, pat, base, cm, after=()):
        kw = {} if o[0] in ("I", "CW") else {"allow_small_or_imprecise_dtypes": True}
        add("c", "G", [o], [], lambda q: g.iota(ap(o), pat, base, cm, **kw), 0.13 + 2 * wid(o) * cyc, after=after)
        return o

    def dma(q, o, i, rd, wr, cost, after=()):
        top["d"] += 1
        return add("d", q, wr, rd, lambda q: Q[q].dma_start(o, i), cost, "d%d" % (top["d"] - 1), 16, after)

    def renew(o, i, end, after=()):
        dma("Y", T[o][:, 0:end], T[i][:, 0:end], [(i, 0, end)], [(o, 0, end)], R["mb"], after)

    def ind(win, off):
        return ("ind", win if isinstance(win, tuple) else (win, 0, SCRATCH[win][1][1]), off)

    def lists(o, src, sel):
        mm(o, [sel, src], [(sub(sel, 15 - i, 128), (src[0], src[1] + i, src[2], 16)) for i in range(16)])
        return o

    def count(cm):
        return lists(new("#", wid(cm) // 16), cm, ("ZS", 0, 144))

    def part(x, h, k=2):
        return sub(x, wid(x) // k * h, wid(x) // k)

    def col(x, o, k=1):
        return sub(x, 64 * o, 64 * k)

    def pair(x, o, k=1):
        return sub(x, 128 * o, 128 * k)

    def even(x):
        return (x[0], x[1], x[2] - 1, 2)

    def odd(x):
        return (x[0], x[1] + 1, x[2], 2)

    I1, IN, IM, IH, IQ, IR, I2, IB, IC, K1, N1, N2, N3, K2 = [("ID", 128 * k, 128 * k + 128) for k in range(14)]

    def mix(terms, early=0):
        d = new("#", wid(terms[0][1]))
        early = early if OPT["early"] else 0
        if early:
            mm(d, [x for p in terms[:early] for x in p], terms[:early], 1, True, False)
        mm(d, [x for p in terms[early:] for x in p], terms[early:], 1, not early, True)
        return d

    def halves(terms, h):
        return [(l, part(v, h)) for l, v in terms]

    def gather(name, win, off, o=None):
        o, k = o or new("W", H), 1 if top["tag"] + name in OPT["whole"] else 2
        for h in range(k):
            move(name, part(o, h, k), ind(win, part(off, h, k)))
        return o

    def more(d, terms, opens=False, closes=False):
        mm(d, [x for p in terms for x in p], terms, 1, opens, closes)

    def total(o, terms):
        mm(o, [x for p in terms for x in p], terms)
        return o

    def nodes(o, x):
        d, over = new("#", wid(x)), act("S", x, 1.0, 1.0 - V, F.Relu)
        mm(d, [F1, FB, x, over], [(F1, x), (FB, over)], 4)
        return act(o, d, 1.0, 0.0, F.Relu)

    def knockout(name, rec, later, ids, chain, k, nh):
        wh, w, win = H // nh, 64 // nh, A.is_ge if later else A.is_lt
        cms = sub(duel, 6 * k * wh, 6 * wh)
        for h in range(k * 2 // nh, (k + 1) * 2 // nh):
            r = [sub(rec, o * H + h * 512, 512) for o in range(4)]
            at = [sub(cms, j * wh + h * 512 % wh, 512) for j in range(6)]
            if OPT["held"]:
                d = mix([(I1, r[0])])
            for j, (a, b) in enumerate(((0, 1), (0, 2), (0, 3), (1, 2), (1, 3), (2, 3))):
                if j < OPT["held"]:
                    tt(at[j], d, r[b], A.is_gt if later else A.is_lt)
                else:
                    above(name, at[j], mix([(I1, r[a]), (IN, r[b])] if later else [(IN, r[a]), (I1, r[b])]))
        f = [part(odd(pair(fq, o)), k, nh) for o in range(3)]
        ca, cb = count(sub(cms, 0, 3 * wh)), count(sub(cms, 3 * wh, 3 * wh))
        ts(f[0], sub(ca, 0, w), 9.0 if OPT["held"] else 0.5, win)
        fa, fb = ts("S", sub(ca, w, 2 * w), 9.0 if OPT["held"] else 0.5, win), ts(("KD", 384, 384 + 2 * w), sub(cb, 0, 2 * w), 0.5, win)
        fc = ts("S", sub(cb, 2 * w, w), 0.5, win)
        d = tt(fb, fb, fa, A.subtract)
        tt(f[1], tt(sub(d, 0, w), sub(d, 0, w), f[0], A.mult), sub(fa, 0, w), A.add)
        u = tt(sub(d, w, w), tt(sub(d, w, w), sub(d, w, w), f[0], A.mult), sub(fa, w, w), A.add)
        tt(f[2], tt("S", tt(sub(d, 0, w), fc, u, A.subtract), f[1], A.mult), u, A.add)
        for o in range(3):
            tt(part(even(chain[o]), k, nh), part(ids[o], k, nh), part(odd(chain[o]), k, nh), A.subtract)
            pick(part(chain[o + 1], k, nh), part(pair(fq, o), k, nh), part(chain[o], k, nh))
        return f

    dma("S", T.RT[:], T.rt[:], [], [("RT", 0, 256)], 2.0)
    first = dma("Y", T.A[:, 0:V], T.rec[:], [], [("A", 0, V)], R["mb"] + 0.3)
    dma("Y", T.B[:, 0:V], T.rec[:], [], [("B", 0, V)], R["mb"], [first])
    iota(("I", 0, 1), [[0, 1]], 0, 1)
    dz0 = iota(new("S", 256), [[0, 4], [16, 64]], V, 1)
    tz = iota(new("S", 144), [[1, 144]], -15, 0)
    dc0 = iota(new("S", 256), [[16, 2], [-1, 128]], 0, 1)
    ig = iota(new("S", 128), [[16, 8], [0, 16]], 0, 0)
    n0 = iota(new("S", 5), [[256, 5]], 0, 16)
    iota(("CW", 0, OPT["cw"]), [[0, OPT["cw"]]], V, 0, range(len(ops) - 6, len(ops)))
    for c in range(OPT["cw"], V, 512):
        fill(("CW", c, c + 512), V)
    filled = [i for lo, hi, w, i in recs["CW"]]
    for o in range(3):
        recs["CW"].append((0, V, 1, dma("Y", T.CW[o:128:16, :], T.ch[:, o * V:(o + 1) * V], [], [], R["mb"] - 1.5, filled)))
    ts(("I", 1, 2), ("I", 0, 1), 112, A.bitwise_and)
    ts(("I", 2, 3), ("I", 0, 1), 15, A.bitwise_and)
    c2 = cp("S", ("I", 1, 3))
    g16, i16 = sub(c2, 0, 1), sub(c2, 1, 1)
    dp = ts("S", dz0, g16, A.subtract)
    rr, ur = new("S", 512), new("U", 256)
    r = cp(("KD", 0, 256), ("RT", 0, 256))
    cp(ur, tt(odd(rr), r, tt("S", ts(("KD", 256, 512), r, 0.0, A.is_equal), dp, A.mult), A.max))
    fill(("A", V, WIN), FAR, 0.5)
    act(("B", V, WIN), ("A", V, WIN))
    ts(("ZS", 0, 144), tz, g16, A.is_equal)
    dc_, nb_, dp2, bw = [act(new("S", 384), ("A", V, V + 384), 0.0) for k in range(4)]
    ll = new("W", 320)
    act(col(ll, 0), ("A", V, V + 64), 0.0, -1.0)
    act(odd(dp2), col(dp, 0, 3))
    duel, fq = new("W", 6 * H), act(new("W", 384), ("A", V, V + 384), 0.0)
    c16 = new("W", 256)
    ts(col(c16, 0), col(dp, 0), i16, A.subtract, -float(V), A.add)
    for o in (1, 2, 3):
        act(col(c16, o), col(c16, 0), 1.0, float(o * H))
    rows = ts("S", sub(tz, 15, 3), i16, A.is_equal, ts("S", i16, 3.0, A.is_equal), A.add)
    for o in range(3):
        ts(("ZK", 144 * o, 144 * o + 144), tz, g16, A.is_equal, sub(rows, o, 1), A.mult)
    ts(("BO", 0, 128), ig, g16, A.is_equal)
    ts(I1, sub(dc0, 0, 128), 0.0, A.is_equal)
    for x, c in ((IN, -1.0), (IM, -2.0), (IH, 0.5), (IQ, -0.25), (IR, MAGIC), (I2, 2.0), (IB, BIG / 2), (IC, -BIG / 2),
                 (K1, 1.0 * H), (N1, -1.0 * H), (N2, -2.0 * H), (N3, -3.0 * H), (K2, 2.0 * H)):
        act(x, I1, c)
    F1 = act(new("S", 128), I1)
    FB = act(new("S", 128), I1, -BIG)
    act(("ONE", 0, 512), ("A", V, V + 512), 1 / FAR)
    far = ts("S", ig, g16, A.not_equal, 999.0, A.mult)
    dc = new("S", 256)
    for k in range(2):
        tt(part(dc, k), part(dc0, k), far, A.add)
    n16 = ts("S", n0, ts("S", g16, 16.0, A.mult), A.subtract)

    ys = ("YS", 0, 512)
    lid, held = None, [[], [], [], []]

    def turn(i, writes, after):
        free = [d for lo, hi, w, d in recs["C"] if "turn" in ops[d] and d != i]
        ops[i]["deps"] = ops[i]["deps"].difference(free).union(after)
        ops[i]["soft"] = ops[i]["soft"].difference(free)
        ops[i]["turn"] = writes

    for t in range(2):
        old, win, tgt = ("B", "A", "C") if t == 0 else ("C", "C", "C")
        roots = [odd(pair(rr, o)) for o in range(4)]
        top["tag"] = "champion%d" % t
        m, um, nh = roots[0], col(ur, 0), OPT["nh"][t]
        if OPT["form"][t] == "P":
            rd, um = new("W", 4 * H), new("U", 64)
            for h in range(2):
                for o in range(4):
                    move("root", sub(rd, o * H + h * 512, 512), ind("A", part(col(ur, o), h)))
            chain = [pair(rr, 0), new("S", 128), new("S", 128), pair(ys, 0)]
            for k in range(nh):
                knockout("duel", rd, True, roots[1:], chain, k, nh)
                cp(part(um, k, nh), part(odd(chain[3]), k, nh))
            m = odd(pair(ys, 0))
        if OPT["form"][t][0] == "T":
            rd, um, u1, lo = new("W", 3 * H), new("U", 64), new("U", 64), 0
            chain = [pair(rr, 0), new("S", 128), new("S", 128), pair(ys, 0)]
            for k in OPT["parts"]:
                def cut(x):
                    return sub(x, lo * wid(x) // H, k * wid(x) // H)
                r = [None] + [move("root", cut(sub(rd, o * H - H, H)), ind("A", cut(col(ur, o)))) for o in (1, 2, 3)]
                ca, cb, w = sub(duel, 4 * lo, 2 * k), sub(duel, 4 * lo + 2 * k, 2 * k), k // 16
                tt(part(ca, 0), ind("A", cut(col(ur, 0))), r[1], A.is_gt)
                if OPT["form"][t][1] == "A":
                    tt(part(ca, 1), ind("A", cut(col(ur, 2))), r[3], A.is_gt)
                for c in range(0, k, 512) if OPT["form"][t][1] == "S" else ():
                    e = min(512, k - c)
                    above("duel", sub(ca, k + c, e), mix([(I1, sub(r[2], c, e)), (IN, sub(r[3], c, e))]))
                f = [cut(odd(pair(fq, o))) for o in range(3)]

                def step(o):
                    tt(cut(even(chain[o])), cut(roots[o + 1]), cut(odd(chain[o])), A.subtract)
                    return odd(pick(cut(chain[o + 1]), cut(pair(fq, o)), cut(chain[o])))
                na = count(ca)
                ts(f[0], part(na, 0), 9.0, A.is_ge)
                f32 = ts("S", part(na, 1), 9.0 if OPT["form"][t][1] == "A" else 0.5, A.is_ge)
                cp(cut(u1), step(0))
                for j in range(2):
                    tt(part(cb, j), ind("A", cut(u1)), r[2 + j], A.is_gt)
                nb = count(cb)
                ts(f[1], part(nb, 0), 9.0, A.is_ge)
                f3 = ts("S", part(nb, 1), 9.0, A.is_ge)
                step(1)
                tt(f[2], tt("S", tt("S", f32, f3, A.subtract), f[1], A.mult), f3, A.add)
                cp(cut(um), step(2))
                lo += k
            m = odd(pair(ys, 0))
        for o in (1, 2, 3) if OPT["form"][t][0] not in "PT" else ():
            form = OPT["form"][t][o - 1]
            mo, um2, cm, ex, em, lo = pair(ys, 0) if o == 3 else ("XB", 128 * o + 128, 128 * o + 256), new("U", 64), new("W", H), new("W", H), new("W", H if form == "S" else 0), 0
            for h, k in enumerate(OPT["parts"] if nh > 1 else (512, 512)):
                def cut(x):
                    return sub(x, lo * wid(x) // H, k * wid(x) // H)
                top["tag"] = "lead" if k < 256 else "champion%d" % t
                move("root", cut(ex), ind("A", cut(um if form == "B" else col(ur, o))))
                if form == "A":
                    tt(cut(cm), ind("A", cut(um)), cut(ex), A.is_gt)
                elif form == "B":
                    tt(cut(cm), ind("A", cut(col(ur, o))), cut(ex), A.is_lt)
                else:
                    move("best", cut(em), ind("A", cut(um)))
                    above("duel", cut(cm), mix([(I1, cut(em)), (IN, cut(ex))], o // 3))
                if nh == 1:
                    lo, k = (512, 0) if h == 0 else (0, H)
                if k:
                    tt(cut(odd(pair(dc_, o - 1))), cut(m), cut(roots[o]), A.subtract)
                    ts(cut(even(pair(rr, o))), count(cut(cm)), 0.5 if form == "S" else 9.0, A.is_lt)
                    pick(cut(mo), cut(pair(dc_, o - 1)), cut(pair(rr, o)))
                    cp(cut(um2), cut(odd(mo)))
                lo += k
            m, um = odd(mo), um2
        z, w, near, kg, lo = new("W", H), new("W", H), new("W", 4 * H), ("KG", t * H, t * H + H), 0
        zn = sub(near, 0, H)
        for k in OPT["send"][t]:
            top["tag"] = "lead" if k < 256 else "champion%d" % t
            move("z", sub(z, lo, k), ind("A", sub(um, lo // 16, k // 16)))
            e, s = engines(topo, core, nxt), top["r"]
            top["r"] += 1
            r_id, pid = topo.addr(nxt)[:2]

            def send(q, a=sub(w, lo, k), b=sub(z, lo, k), s=s, e=e, r_id=r_id, pid=pid):
                g.remote_dma(ap(a), ap(b), T.sem["arr%d" % s], T.sem["snt%d" % s], pid, r_id, sum(1 << x for x in e))
            sent = x = add("r", "G", [], [sub(z, lo, k)], send, 0.3 + (R["first"] if s == 0 else 0), "snt%d" % s, len(e))
            add("a", "", [sub(w, lo, k)], [], None, R["net"] * (0.6 + 0.8 * k / H), "arr%d" % s, len(engines(topo, prv, core)), [x])
            lo += k
        top["tag"] = "kids%d" % t
        lo = 0
        two = t == 1 and OPT["two"]
        for k in () if two else OPT["parts"] if t == 0 else (512, 512):
            ts(sub(kg, lo, k), ind("CW", sub(um, lo // 16, k // 16)), -V / 2, A.add)
            lo += k
        if two:
            kg = gather("kids", "B", um)
        for o in range(4):
            tt(even(pair(rr, o)), roots[o], m, A.is_equal)
        keep = [absent("S", even(pair(rr, 0))), tt("S", even(pair(rr, 2)), even(pair(rr, 3)), A.add), even(pair(rr, 3))]
        kd = ("KD", 0, 384)
        if t == 1:
            won, mc, bw = ("XB", 0, 192), move("copy", new("S", 64), m), new("S", 384)
            for o in range(3):
                tt(col(won, o), odd(pair(ys, o + 1)), mc, A.is_equal)
                tt(odd(pair(nb_, o)), keep[o], col(won, o), A.is_gt)
            tt(odd(kd), nodes("S", lid), won, A.mult)
        for o in range(3):
            kid = lists(even(pair(kd, o)), kg, sub(z2, 144 * o, 144) if two else ("ZK", 144 * o, 144 * o + 144))
            if t == 1:
                pick(pair(bw, o), pair(nb_, o), pair(kd, o))
            else:
                tt(odd(pair(bw, o)), keep[o], kid, A.mult)
        pick(("XB", 1, 385), dp2, pair(rr, 0, 3), A.max)
        a3 = odd(pick(new("S", 128), pair(dp2, 0), pair(rr, 3), A.max))
        xb = ("XB", 2, 386)
        sm = new("#", 2)
        mm(sm, [("BO", 0, 128), sub(w, 0, 2)], [(("BO", 0, 128), sub(w, 0, 2))])
        i0 = 8 + 24 * t
        ts(("I", i0, i0 + 5), n16, sub(sm, 0, 1), A.add)
        ts(("I", i0 + 8, i0 + 13), ("I", i0, i0 + 5), 3, A.arith_shift_right, 126, A.bitwise_and)
        us = ts("U", ("I", i0 + 8, i0 + 13), 1.0, A.add)
        ts(("I", i0 + 16, i0 + 17), ("I", i0, i0 + 1), 15, A.bitwise_and)
        if t in OPT["pp"]:
            gap, r = new("S", 256), ts("S", ("I", i0 + 16, i0 + 17), -1.0, A.mult)
            add("c", "S", [gap], [dc, r], lambda q, gap=gap, r=r: g.scalar.activation(ap(gap), ap(dc), F.Abs, bias=ap(r)), span(gap, dc, 1))
            pp = act("S", gap, -1.0, 1.0, F.Relu)
        else:
            pp = ts("S", dc, cp("S", ("I", i0 + 16, i0 + 17)), A.is_equal)
        xs, ux = new("S", 384), new("U", 192)
        for o in range(3):
            g1 = move("shift", new("S", 80), ("ind", pair(bw, o), us))
            mm(odd(pair(xb, o)), [pp, g1], [(part(pp, 0), sub(g1, 0, 64)), (part(pp, 1), sub(g1, 1, 64))], 4)
            if o == 1:
                continue
            a, k = (0, 1) if o == 0 else (1, 2)
            absent(odd(pair(nb_, a, k)), odd(pair(xb, a, k)))
            pick(pair(xs, a, k), pair(nb_, a, k), pair(xb, a, k))
            if o == 0:
                cp(col(ux, 0), odd(pair(xs, 0)))
        x = [odd(pair(xs, o)) for o in range(3)]
        for o in range(3):
            flag(col(ll, o + 1), x[o])
            if o < 2:
                cp(col(ux, o + 1), tt(x[o + 1], x[o + 1], tt(("KD", 384, 448), col(ll, o + 1), x[o], A.mult), A.max))
        top["tag"] = "mean%d" % t
        for lo, k in ((0, 512), (512, 512)):
            one, zp = ("ONE", 0, k), sub(zn, lo, k)
            d = mix([(IH, sub(z, lo, k)), (IQ, one), (IH, sub(w, lo, k)), (IR, one)], 2)
            either("mean", zp, d, lambda o=zp, d=d: g.vector.tensor_scalar(ap(o), ap(d), -MAGIC, None, A.add),
                   lambda o=zp, d=d: g.scalar.activation(ap(o), ap(d), F.Identity, bias=-MAGIC))
        form, xd = OPT["meld"][t], []
        for o in range(3):
            top["tag"] = "first%d%d" % (t, o)
            xd.append(gather("first", old, col(ux, o), sub(near, H + o * H, H)) if o or form[0] != "A" else None)
            for i in range(len(ops) - 2, len(ops)) if t == 1 else ():
                turn(i, 0, held[o])
        if t == 0 and OPT["two"]:
            top["tag"] = "pieces"
            for o in range(3):
                dma("Y", T.CN[:, o * 256:(o + 1) * 256], T.ch[:, o * V:(o + 1) * V], [], [("CN", o * 256, o * 256 + 256)], 2.2, [sent])
            z2, hl, whole = new("W", 432), new("W", 1536), cp("S", ("CN", 0, 768))
            row2 = ts("S", sub(tz, 15, 3), cp("S", ts(("I", 3, 4), ("I", 0, 1), 1, A.arith_shift_right, 7, A.bitwise_and)), A.is_equal)
            for o in range(3):
                add("c", "S", [sub(z2, 144 * o, 144)], [("ZS", 0, 144), row2], lambda q, o=o: g.scalar.activation(
                    ap(sub(z2, 144 * o, 144)), ap(("ZS", 0, 144)), F.Identity, scale=ap(sub(row2, o, 1))), span(("ZS", 0, 144), ("ZS", 0, 144), 1))
            act(part(hl, 0), whole)
            for h in range(2):
                d = new("#", 384)
                mm(d, [F1, whole], [(F1, part(whole, h))], 4, True, False)
                mm(d, [IN, hl], [(IN, part(part(hl, 0), h))], 1, False, True)
                act(part(part(hl, 1), h), d)
            rows2 = [dma("Y", T.B[k:128:16, 0:V], ap(sub(hl, k % 2 * 768 + k // 2 * 256, 256)), [sub(hl, k % 2 * 768 + k // 2 * 256, 256)], [], 2.2,
                         [i for lo, hi, w, i in recs["B"]]) for k in range(6)]
            recs["B"] += [(0, V, 1, i) for i in rows2]
        top["tag"] = "put%d" % t
        pw = OPT["putz"]
        for c in range(0, H, pw):
            cp(ind(win, sub(um, c // 16, pw // 16)), sub(zn, c, pw))
            if t == 1:
                turn(len(ops) - 1, 1, [])
                held[3].append(len(ops) - 1)
        if t == 0:
            renew(tgt, win, WIN)
        top["tag"] = "roots%d" % t
        flag(col(ll, 4), a3)
        ns = act("S", mix([(IB, col(ll, 0, 4)), (IC, col(ll, 1, 4))]), 1.0, BIG)
        tt(("XB", 1, 384, 2), even(xb), odd(xs), A.is_equal)
        a2 = pick(kd if t == 0 else new("S", 384), dp2, ("XB", 1, 385), A.max)
        rr, ur, lid = new("S", 512), new("U", 256), new("S", 192)

        def root(o, k):
            a = a3 if o == 3 else odd(pair(a2, o, k))
            ro = tt(odd(pair(rr, o, k)), a, tt("S", odd(pair(ys, o, k)), col(ns, o, k), A.add), A.min)
            if t == 0:
                cp(col(ur, o, k), ro)
        if form == "P":
            top["tag"] = "link%d" % t
            q = knockout("link", near, False, x, [pair(ys, o) for o in range(4)], 0, 1)
            t1, t2, d = new("W", 64), new("W", 64), new("#", 192)
            tt(t1, q[0], q[1], A.mult)
            tt(t2, tt("S", tt("S", q[1], q[1], A.add), q[0], A.max), q[2], A.mult)
            for o, terms in enumerate(([(N1, q[0])], [(N2, q[1]), (K1, t1)], [(N3, q[2]), (K1, t2)])):
                mm(col(d, o), [c16, N1, N2, N3, K1] + [b for a, b in terms], [(I1, col(c16, o + 1))] + terms)
            up = ts("U", d, i16, A.add)
            ul = cp("U", tt(lid, tt("S", odd(pair(ys, 0, 3)), odd(xs), A.add), odd(pair(ys, 1, 3)), A.subtract))
            if t == 0:
                top["tag"] = "roots0"
                up0 = tt(("KD", 0, 256), odd(ys), ns, A.add)
                tt(odd(pair(rr, 0, 3)), col(up0, 0, 3), odd(a2), A.min)
                tt(odd(pair(rr, 3)), col(up0, 3), a3, A.min)
                cp(ur, odd(rr))
            terms, pw = [(I1, zn)], OPT["put"]
            for o in range(3):
                top["tag"] = "loser%d%d" % (t, o)
                rl, sg = gather("loser", near, col(up, o)), new("W", H)
                for h in range(2):
                    sign("sign", part(sg, h), mix(halves(terms + [(I1, xd[o]), (IM, rl)], h), len(terms) + 1))
                terms = terms + [(I1, xd[o]), (IN, rl)]
                for c in range(0, H, pw):
                    tt(ind(tgt, sub(col(ul, o), c // 16, pw // 16)), sub(rl, c, pw), sub(sg, c, pw), A.add)
            continue
        if t == 0:
            root(0, 1)
        terms, uy, yd, pw, yp = [(I1, zn)], None, zn, OPT["put"], None
        q, run, rls, sgs, uls = [None] * 3, [None] * 2, [], [], []
        qq, far3 = new("W", 64), ("KD", 384, 512)
        for o in range(3):
            top["tag"] = "link%d%d" % (t, o)
            y, cm = odd(pair(ys, o)), new("W", H)
            both = tt("S", y, x[o], A.add)
            tt(even(pair(ys, o)), x[o], y, A.subtract)
            for h in range(2):
                if form[o] == "R":
                    if o == 0:
                        run[h] = new("#", 512)
                        more(run[h], halves([(I1, zn)], h), True)
                        more(run[h], halves([(IN, xd[0])], h))
                    elif o == 1:
                        more(run[h], halves([(I2, xd[0]), (IN, xd[1])], h))
                        more(run[h], halves([(IN, rls[0])], h))
                    else:
                        more(run[h], halves([(I1, rls[0]), (I1, xd[1]), (IN, xd[2])], h))
                        more(run[h], halves([(IN, rls[1])], h))
                    below("link", part(cm, h), run[h])
                    if o:
                        top["tag"] = "loser%d%d" % (t, o - 1)
                        more(run[h], halves([(I1, xd[o]), (IN, rls[o - 1])], h))
                        sign("sign", part(sgs[o - 1], h), run[h])
                        top["tag"] = "link%d%d" % (t, o)
                elif form[o] == "S" and o == 0 and OPT["zcmp"]:
                    above("link", part(cm, h), mix(halves([(IN, zn), (I1, xd[o])], h), 1))
                elif form[o] == "S" and o == 0:
                    above("link", part(cm, h), mix(halves([(IN, z), (IN, w), (I2, xd[o])], h), 2))
                elif form[o] == "S":
                    above("link", part(cm, h), mix(halves([(I1, xd[o]), (IN, yd)], h), 1))
                elif form[o] == "L":
                    above("link", part(cm, h), mix(halves([(I1, xd[o])] + [(IN if l == I1 else I1, v) for l, v in terms], h), len(terms)))
                elif o == 0:
                    tt(part(cm, h), ind(old, part(col(ux, 0), h)), part(zn, h), A.is_gt)
                else:
                    tt(part(cm, h), ind(win, part(uy, h)), part(xd[o], h), A.is_lt)
            q[o] = ts(odd(pair(fq, o)), count(cm), 9.0 if form[o] == "A" else 0.5, A.is_lt)
            if t in OPT["near"]:
                win, d = sub(near, 0, (o + 2) * H), new("#", 128)
                if o < 2 and form[o + 1] in "LR":
                    d = total(col(d, 0), [(I1, col(c16, o + 1))] + ([(N2, q[1]), (K1, tt(qq, q[0], q[1], A.mult))] if o else [(N1, q[0])]))
                    if o:
                        total(even(far3), [(N3, ("ONE", 0, 64)), (K1, q[0]), (K2, q[1]), (N1, qq)])
                        total(odd(far3), [(I1, col(c16, 3))])
                elif o == 0:
                    total(col(d, 0), [(I1, col(c16, 0)), (K1, q[0])])
                    total(col(d, 1), [(I1, col(c16, 1)), (N1, q[0])])
                elif o == 1:
                    tt(qq, q[0], q[1], A.mult)
                    total(col(d, 0), [(I1, col(c16, 0)), (K1, q[0]), (K2, q[1]), (N1, qq)])
                    total(col(d, 1), [(I1, col(c16, 2)), (N2, q[1]), (K1, qq)])
                    total(even(far3), [(N3, ("ONE", 0, 64)), (K1, q[0]), (K2, q[1]), (N1, qq)])
                    total(odd(far3), [(I1, col(c16, 3))])
                else:
                    d = odd(pick(new("S", 128), pair(fq, 2), far3))
                uy = ts("U", d, i16, A.add)
                uy, up = col(uy, 0), col(uy, wid(uy) > 64)
            y2 = odd(pick(pair(ys, o + 1), pair(fq, o), pair(ys, o)))
            if o < 2 and t not in OPT["near"] and form[o + 1] not in "LR":
                uy = cp("U", y2)
            if t == 0:
                root(o + 1, 1)
            ul = cp("U", tt(col(lid, o), both, y2, A.subtract))
            sg = new("W", H)
            yd = gather("carry", win, uy) if xd[o] is None or (o < 2 and form[o + 1] == "S") else None
            top["tag"] = "loser%d%d" % (t, o)
            if yd and xd[o] and len(terms) == 1 and OPT["lin"][t][o]:
                rl = new("W", H)
                for h in range(2):
                    move("loser", part(rl, h), mix(halves(terms + [(I1, xd[o]), (IN, yd)], h)))
                now = [(I1, yd), (IN, rl)] if OPT["after"] else [(IN, terms[0][1]), (IN, xd[o]), (I2, yd)]
            else:
                rl = gather("loser", win, up if t in OPT["near"] else ul)
                now = [(I1, yd), (IN, rl)] if yd else terms + [(I1, xd[o]), (IM, rl)]
            terms = [(I1, yd)] if yd else terms + [(I1, xd[o]), (IN, rl)]
            rls.append(rl); sgs.append(sg); uls.append(ul)
            for h in range(2):
                if form[o] != "R":
                    sign("sign", part(sg, h), mix(halves(now, h), len(now) - 1 if len(now) > OPT["long"] else 0))
                elif o == 2:
                    more(run[h], halves([(I1, rls[1]), (I1, xd[2])], h))
                    more(run[h], halves([(IM, rl)], h), False, True)
                    sign("sign", part(sg, h), run[h])
            for k in (o,) if form[o] != "R" else () if o == 0 else (0,) if o == 1 else (1, 2):
                top["tag"] = "loser%d%d" % (t, k)
                for c in range(0, H, pw):
                    tt(ind("C", sub(uls[k], c // 16, pw // 16)), sub(rls[k], c, pw), sub(sgs[k], c, pw), A.add)
                    turn(len(ops) - 1, 1, held[3])
                    held[k].append(len(ops) - 1)
    top["tag"] = "out"
    ro, up = new("S", 256), tt(("KD", 0, 256), odd(ys), ns, A.add)
    tt(col(ro, 0, 3), col(up, 0, 3), odd(a2), A.min)
    tt(col(ro, 3), col(up, 3), a3, A.min)
    res = nodes("S", ro)
    dma("S", T.yrt[:], ap(res), [res], [], R["mb"] - 1.6)
    dma("Y", T.yrec[:], T.C[:, 0:V], [("C", 0, V)], [], R["mb"])
    PLAN["top"] = top
    return ops, Q


def schedule(ops, deps, fixed):
    lat, rest, left, users = OPT["lat"], [0.0] * len(ops), [len(d) for d in deps], [[] for d in deps]
    for i, dd in enumerate(deps):
        for d in dd:
            users[d].append(i)
    order = [i for i in range(len(ops)) if not left[i]]
    for i in order:
        for u in users[i]:
            left[u] -= 1
            if not left[u]:
                order.append(u)
    for i in reversed(order):
        rest[i] = ops[i]["cost"] + max([rest[u] + lat for u in users[i]] + [0.0])
    queue = [fixed.get(i, op["qs"]) for i, op in enumerate(ops)]

    def place(weight, before):
        busy, done, start = {q: [] for q in queue}, [0.0] * len(ops), [0.0] * len(ops)
        for i in sorted(order, key=lambda i: -weight[i]):
            at = max([done[d] + lat for d in before[i]] + [0.0])
            hold, k, line = ops[i]["cost"] if ops[i]["kind"] in "cr" else 0.05, 0, busy[queue[i]]
            for a, b in line if queue[i] else ():
                if b > at:
                    if at + hold <= a:
                        break
                    at = b
                k += 1
            line.insert(k, (at, at + hold))
            start[i], done[i] = at, at + ops[i]["cost"]
        return start, done
    for i in reversed(order):
        rest[i] = max([rest[i] - OPT["late"].get(ops[i]["tag"], 0)] + [rest[u] + 1e-6 for u in users[i]])
    start, done = place(rest, deps)
    best = (max(done), start, queue, done)
    for k in range(OPT["turns"]):
        start, done = place(place(done, users)[1], deps)
        best = min(best, (max(done), start, queue, done), key=lambda x: x[0])
    return best


def lend(ops, start, done):
    users, bank, last, deps = {}, {}, {b: (0.0, []) for b in POOL}, [set(op["deps"]) for op in ops]
    for i, op in enumerate(ops):
        for x in op["lent"]:
            users.setdefault(x, []).append(i)

    def follows(i, j, seen):
        if i == j:
            return True
        seen.add(i)
        return any(d not in seen and follows(d, j, seen) for d in deps[i] if start[d] >= start[j] or d in late)
    late = set()
    for x in sorted(users, key=lambda x: start[users[x][0]]):
        b = bank[x] = [b for b in sorted(POOL, key=lambda b: last[b][0]) if not any(follows(i, users[x][0], set()) for i in last[b][1])][0]
        late.update(i for i in last[b][1] if start[i] > start[users[x][0]])
        deps[users[x][0]].update(last[b][1])
        last[b] = (max(done[i] for i in users[x]), users[x])
    return bank, deps


def links(order, queue, ops, deps):
    steps, last, bank, idle, left, wrote, read = [], {}, {}, [(b, ()) for b in POOL], {}, [], []
    for i in order:
        q, (hard, soft, turn, opens, lent) = queue[i], deps[i]
        if soft:
            hard = hard + [d for d in soft if queue[d] != q]
        if turn:
            hard = hard + (wrote + read if turn > 1 else wrote)
            if turn > 1:
                wrote, read = [i], []
            else:
                read.append(i)
        if opens:
            if not idle:
                return None
            bank[opens[0]], users = idle.pop(0)
            hard = hard + list(users)
            left[opens[0]] = len(opens[1])
        for x, users in lent:
            left[x] -= 1
            if not left[x]:
                idle.append((bank[x], users))
        steps.append((i, last.get(q, -1), hard))
        if q:
            last[q] = i
    return steps, bank


def replay(steps, queue, hold, tail, slow):
    n = len(hold)
    done, free, start, why = [0.0] * n, [0.0] * (n + 1), [0.0] * n, [-1] * n
    for i, w, hard in steps:
        t = free[w]
        for d in hard:
            if done[d] > t:
                t, w = done[d], d
        start[i], why[i] = t, w
        free[i] = t = t + hold[i] + (slow if queue[i] == "S" else 0.0)
        done[i] = t + tail[i]
    return max(done), start, why, done


def plan(ops, costs):
    fixed = {i: "V" if op["name"] in OPT["onv"] else "S" for i, op in enumerate(ops) if "name" in op}
    turns = [i for i, op in enumerate(ops) if "turn" in op]
    inline = {j: [i for i in turns if i < j and (ops[i]["turn"] or ops[j]["turn"])] for j in turns}
    bank, deps = lend(ops, *schedule(ops, [op["deps"].union(inline.get(i, ())) for i, op in enumerate(ops)], fixed)[1::2])
    end, start, queue, done = schedule(ops, [d.union(inline.get(i, ())) for i, d in enumerate(deps)], fixed)
    order, n = sorted(range(len(ops)), key=lambda i: (start[i], i)), len(ops)
    deps, users, above, sure, lent = [], [[] for op in ops], [], [], {}
    for i, op in enumerate(ops):
        m = k = 0
        for d in op["deps"]:
            m |= above[d]
            k |= 0 if d in op["soft"] else sure[d]
        deps.append([d for d in op["deps"] if not k >> d & 1])
        above.append(m | sum(1 << d for d in op["deps"]))
        sure.append(k | sum(1 << d for d in op["deps"] - op["soft"]))
        for d in deps[i]:
            users[d].append(i)
        op["lent"], op["opens"] = sorted(set(op["lent"])), None
        for x in op["lent"]:
            lent.setdefault(x, []).append(i)
    for x in lent:
        ops[lent[x][0]]["opens"] = x
    rule = [([d for d in deps[i] if d not in op["soft"]], [d for d in deps[i] if d in op["soft"]], op.get("turn", -1) + 1,
             op["opens"] and (op["opens"], lent[op["opens"]]), [(x, lent[x]) for x in op["lent"]]) for i, op in enumerate(ops)]
    holds = [[c if op["kind"] in "cr" else 0.05 if op["kind"] == "d" else 0.0 for op, c in zip(ops, cost)] for cost in costs]
    tails = [[r["lat"] if op["kind"] == "c" else 0.0 if op["kind"] == "r" else c + r["land"] for op, c in zip(ops, cost)] for cost, r in zip(costs, RATES)]

    def judge(order, queue, limit=None):
        steps, runs = links(order, queue, ops, rule), []
        for k in range(len(RATES)) if steps else ():
            runs.append(replay(steps[0], queue, holds[k], tails[k], RATES[k]["slow"]))
            if limit and runs[k][0] > limit[k][0] + 1.0:
                return None, None
        return (sum(x[0] + OPT["pull"] * sum(x[3]) / n for x in runs) / len(runs), runs) if steps else (None, None)
    now, runs = judge(order, queue)
    best, seed, named = (now, order, queue), [OPT["seed"]], sorted(fixed)

    def draw(k):
        seed[0] = (seed[0] * 1103515245 + 12345) % 2147483648
        return (seed[0] >> 8) % k
    for turn in range(OPT["tries"] + OPT["again"]):
        if turn == OPT["tries"]:
            now, order, queue = best
            runs = judge(order, queue)[1]
        heat = OPT["heat"] * (1 - turn / OPT["tries"]) if turn < OPT["tries"] else 0.12 * (1 - (turn - OPT["tries"]) / OPT["again"])
        run = runs[draw(len(runs))]
        i, chain = run[3].index(run[0]), []
        while i >= 0:
            chain.append(i)
            i = run[2][i]
        held = [(i, j) for i, j in zip(chain, chain[1:]) if j not in deps[i]]
        if not held:
            break
        i, j = held[draw(len(held))]
        new, side, how = list(order), queue, draw(8)
        if draw(100) < OPT["far"]:
            b, k = new.index(i), 1 + draw(OPT["reach"])
            i, j = (i, new[max(0, b - k)]) if how < 5 else (new[min(n - 1, b + k)], j)
            if draw(2):
                k = named[draw(len(named))]
                side = list(queue)
                side[k] = "S" if queue[k] == "V" else "V"
            how = max(how, 2)
        if how < 2 and ("name" in ops[i] or "name" in ops[j]):
            k = i if "name" in ops[i] and ("name" not in ops[j] or how) else j
            side = list(queue)
            side[k] = "S" if queue[k] == "V" else "V"
        elif how < 5:
            a, b = new.index(j), new.index(i)
            ahead = [k for k in new[a:b] if above[i] >> k & 1]
            if j in ahead or a > b:
                continue
            new[a:b + 1] = ahead + [i] + [k for k in new[a:b] if not above[i] >> k & 1]
        else:
            a, b = new.index(j), new.index(i)
            behind = [k for k in new[a + 1:b + 1] if above[k] >> j & 1]
            if i in behind or a > b:
                continue
            new[a:b + 1] = [k for k in new[a + 1:b + 1] if not above[k] >> j & 1] + [j] + behind
        t, r = judge(new, side, runs)
        if t is not None and t < now + (OPT["heat"] * draw(1000) / 1000 * (1 - turn / OPT["tries"]) if turn < OPT["tries"] else heat * draw(1000) / 1000):
            order, queue, now, runs = new, side, t, r
            if turn % 8 == 0:
                again = sorted(new, key=lambda k: r[0][1][k])
                t, r = judge(again, side)
                if t is not None and t <= now + 0.02:
                    order, now, runs = again, t, r
            if now < best[0]:
                best = (now, order, queue)
    now, order, queue = best
    now = sum(x[0] for x in judge(order, queue)[1]) / len(RATES)
    PLAN["dbg"] = (ops, judge(order, queue)[1], queue, deps, costs)
    bank, deps, last = links(order, queue, ops, rule)[1], [set(op["deps"]) for op in ops], {}
    turns = []
    for i in order:
        if "turn" in ops[i]:
            deps[i].update(d for d in turns if ops[i]["turn"] or ops[d]["turn"])
            turns.append(i)
        if ops[i]["opens"]:
            deps[i].update(last.get(bank[ops[i]["opens"]], ()))
            last[bank[ops[i]["opens"]]] = lent[ops[i]["opens"]]
    return bank, deps, [(k, i, queue[i]) for k, i in enumerate(order)], now


def rank_program(g, core, T, topo):
    if T.rank_of(core) is None:
        return
    if "it" not in PLAN:
        builds = [build(g, core, T, topo, {}, r)[0] for r in RATES]
        PLAN["it"] = plan(builds[0], [[op["cost"] for op in b] for b in builds])
    bank, deps, order, end = PLAN["it"]
    ops, Q = build(g, core, T, topo, bank, RATES[0])
    count, seen, tok, final = {"V": 0, "S": 0, "P": 0, "G": 0}, {k: {} for k in Q}, {}, {}
    place, known = {i: k for k, (a, i, q) in enumerate(order)}, {}

    def wait(q, s, v):
        if seen[q].get(s, 0) < v:
            seen[q][s] = v
            Q[q].wait_ge(T.sem[s], v)

    for a, i, q in order:
        op = ops[i]
        known[i] = {}
        if op["kind"] != "a":
            for d in sorted(deps[i], key=lambda d: -place[d]):
                if order[place[d]][2] == q and d in op["soft"]:
                    continue
                wait(q, tok[d][0], tok[d][1])
                for s in known[d]:
                    seen[q][s] = max(seen[q].get(s, 0), known[d][s])
            known[i] = dict(seen[q])
            ins = op["fn"](q)
        if op["kind"] == "c":
            count[q] += 1
            tok[i] = ("c" + q, count[q])
            ins.then_inc(T.sem["c" + q], 1)
        else:
            tok[i] = (op["sem"], op["cnt"])
            if op["kind"] == "d":
                ins.then_inc(T.sem[op["sem"]], 16)
        final[tok[i][0]] = tok[i][1]
    seen["G"] = {}
    for s in sorted(final):
        wait("G", s, final[s])
